import numpy as np
import ml_dtypes


def mxq(x, axis, fmt="e4m3"):
    dtype, down = {"e4m3": (ml_dtypes.float8_e4m3fn, 7), "e5m2": (ml_dtypes.float8_e5m2, 14)}[fmt]
    v = np.moveaxis(np.asarray(x, np.float32).astype(ml_dtypes.bfloat16).astype(np.float64), axis, -1)
    blocks = v.reshape(v.shape[:-1] + (-1, 32))
    amax = np.abs(blocks).max(-1, keepdims=True)
    byte = np.maximum(np.where(amax > 0, np.frexp(amax)[1] - 1 + 127, 0) - down, 1)
    scale = np.exp2(byte - 127.0)
    codes = (blocks / scale).astype(np.float32).astype(dtype).astype(np.float64)
    return np.moveaxis((codes * scale).reshape(v.shape), -1, axis)


WIDE = False


def mx_kscale(k):
    if not WIDE:
        return np.ones(k)
    levels = np.array([10, -10, 5, -5, 0])
    if k % 512:
        return np.exp2(np.random.permutation(np.resize(levels, k // 32))).repeat(32)
    a = np.empty((k // 512, 16))
    for p in range(k // 512):
        a[p, :8] = np.random.permutation(np.resize(levels, 8))
        for g in range(8):
            far = levels[np.abs(levels - a[p, g]) >= 10]
            a[p, g + 8] = far[np.random.randint(len(far))]
    return np.exp2(a.ravel()).repeat(32)


BF16 = ml_dtypes.bfloat16


def bf(x):
    return np.asarray(x, np.float32).astype(BF16)


def f64(x):
    return np.asarray(x).astype(np.float64)


E2M1 = np.array([0.0, 0.5, 1.0, 1.5, 2.0, 3.0, 4.0, 6.0, -0.0, -0.5, -1.0, -1.5, -2.0, -3.0, -4.0, -6.0])


def pack_weight(w, fmt):
    k, n = w.shape
    w = f64(bf(w)).reshape(k // 32, 32, n)
    amax = np.abs(w).max(1)
    if fmt == "e4m3":
        byte = np.frexp(amax)[1] - 1 + 127 - 7
    else:
        mant, ex = np.frexp(amax / 6.0)
        byte = np.where(mant > 0.5, ex, ex - 1) + 127
    byte = np.clip(np.where(amax > 0, byte, 1), 1, 254)
    scaled = (w * np.exp2(127.0 - byte)[:, None, :]).reshape(k, n).astype(np.float32)
    by_word = np.ascontiguousarray(scaled.reshape(k // 512, 128, 4, n).transpose(0, 1, 3, 2))
    if fmt == "e4m3":
        words = by_word.astype(ml_dtypes.float8_e4m3fn).view(np.uint8)
    else:
        c = by_word.astype(ml_dtypes.float4_e2m1fn).view(np.uint8) & 0xF
        words = c[..., 0::2] | (c[..., 1::2] << 4)
    return np.ascontiguousarray(words), np.ascontiguousarray(byte.astype(np.uint8).reshape(k // 512, 16, n))


def unpack_weight(words, scales, fmt):
    g, p, n, _ = words.shape
    if fmt == "e4m3":
        vals = np.ascontiguousarray(words).view(ml_dtypes.float8_e4m3fn).astype(np.float64)
    else:
        nib = np.empty((g, p, n, 4), np.uint8)
        nib[..., 0::2] = words & 0xF
        nib[..., 1::2] = words >> 4
        vals = E2M1[nib]
    vals = vals * np.repeat(np.exp2(scales.astype(np.float64) - 127.0), 8, axis=1)[..., None]
    return vals.transpose(0, 1, 3, 2).reshape(g * 512, n)
def pack4(w):
    words, scales = pack_weight(w, "e2m1")
    return words.reshape(words.shape[0], 128, -1), scales


def unpack4(words, scales):
    return unpack_weight(words.reshape(words.shape[0], 128, -1, 2), scales, "e2m1")


T, DI, DO, R = 2048, 1024, 1024, 256


def draw0():
    s, t = mx_kscale(T), mx_kscale(DO)
    x = bf((0.3 + np.random.standard_normal((T, DI))) * s[:, None])
    g = bf(np.random.standard_normal((T, DO)) / np.sqrt(T) / s[:, None])
    v = bf((0.5 + np.random.standard_normal((DI, DO))) / np.sqrt(DI))
    m = bf((1.0 + 0.1 * np.random.standard_normal(DO)) * t)
    b = np.random.standard_normal((R, DO)) / np.sqrt(DO) / t[None, :]
    b_words, b_scales = pack4(b.T)
    return {"x": x, "g": g, "v": v, "m": m, "b_words": b_words, "b_scales": b_scales}


def unit_columns(v):
    n = np.sqrt(np.sum(v * v, axis=0))
    u = v / n[None, :]
    return n, u


def core(x, g, v, m, b_words, b_scales):
    n, u = unit_columns(f64(v))
    gw = mxq(f64(x), 0, "e4m3").T @ mxq(f64(g), 0, "e4m3")
    c = np.sum(u * gw, axis=0)
    dv = (f64(m) / n)[None, :] * (gw - u * c[None, :])
    return mxq(dv, 1, "e4m3") @ unpack4(b_words, b_scales)


def e4m3fn_bytes(y):
    return np.clip(np.asarray(y, np.float64), -448.0, 448.0).astype(np.float32).astype(ml_dtypes.float8_e4m3fn).view(np.uint8)


def e4m3fn_values(b):
    return np.asarray(b, np.uint8).view(ml_dtypes.float8_e4m3fn).astype(np.float64)


def setup_inputs():
    d = draw0()
    x0 = np.asarray(d['x']).astype(np.float64)
    s = (np.max(np.abs(x0), axis=(1,), keepdims=True) / 448.0).astype(np.float32)
    out = {}
    for k, v in d.items():
        if k == 'x':
            out['x_bytes'] = e4m3fn_bytes(x0 / s.astype(np.float64))
            out['x_scale'] = s
        else:
            out[k] = v
    return out


def reference(x_bytes, x_scale, g, v, m, b_words, b_scales):
    return core(e4m3fn_values(x_bytes) * x_scale.astype(np.float64), g, v, m, b_words, b_scales)

@@ -1,0 +1,355 @@
+from contextlib import ExitStack
+
+import concourse.mybir as mybir
+from concourse.masks import make_identity
+
+T, DI, DO, R = 2048, 1024, 1024, 256
+FLOPS = 2 * T * DI * DO + 2 * DI * DO * R
+
+P = 128
+F32 = mybir.dt.float32
+BF16 = mybir.dt.bfloat16
+I32 = mybir.dt.int32
+U32 = mybir.dt.uint32
+U8 = mybir.dt.uint8
+FP8 = mybir.dt.float8_e4m3fn
+E4M3X4 = mybir.dt.float8_e4m3fn_x4
+E2M1X4 = mybir.dt.float4_e2m1fn_x4
+ACT = mybir.ActivationFunctionType
+ALU = mybir.AluOpType
+
+NQ = T // 512
+NG = DO // 512
+HALF = 512
+
+SCALAR_WIDENS = {0: (0, 2, 3), 1: (0, 1, 2, 3), 2: (0, 1, 2, 3), 3: (0, 1, 2, 3)}
+
+
+def tile_doradirectiongradienttoloradown_w4_kernel(tc, x_bytes, x_scale, g, v, m, b_words, b_scales, out):
+    nc = tc.nc
+    with ExitStack() as ctx:
+        keep = ctx.enter_context(tc.tile_pool(name="keep", bufs=1))
+        work = ctx.enter_context(tc.tile_pool(name="work", bufs=2))
+        psum = ctx.enter_context(tc.psum_pool(name="psum", bufs=1))
+        ctx.enter_context(tc.manual_schedule())
+
+        def kt(shape, dtype, name):
+            t = keep.tile(shape, dtype, name=name, align_bytes=64)
+            return t
+
+        def wt(shape, dtype, name, bufs):
+            t = work.tile(shape, dtype, name=name, tag=name, bufs=bufs, align_bytes=64)
+            return t
+
+        def bank_gw():
+            t = psum.tile([P, HALF], F32, name="gw_bank", tag="gw_bank", bufs=6)
+            return t
+
+        def bank_aux(shape, dtype):
+            t = psum.tile(shape, dtype, name="aux_bank", tag="aux_bank", bufs=2)
+            return t
+
+        xs = kt([P, NQ, 4], F32, "xs")
+        xb = [kt([P, 4, DI], U8, f"xb{q}") for q in range(NQ)]
+        gr = [kt([P, 4, DO], BF16, f"gr{q}") for q in range(NQ)]
+        vr = [[kt([P, 4, HALF], BF16, f"vr{s}_{h}") for h in range(NG)] for s in range(2)]
+        vt = [[kt([P, DI], F32, f"vt{h}_{u}") for u in range(2)] for h in range(NG)]
+        xc = kt([P, NQ, DI], U32, "xc")
+        xcs = kt([P, NQ, DI], U8, "xcs")
+        gc = kt([P, NQ, DO], U32, "gc")
+        gcs = kt([P, NQ, DO], U8, "gcs")
+        dc = kt([P, NG, DI], U32, "dc")
+        dcs = kt([P, NG, DI], U8, "dcs")
+        ww = kt([P, NG, 2 * R], U8, "ww")
+        ws = kt([P, NG, R], U8, "ws")
+        mt = kt([P, NG, 4], BF16, "mt")
+        n2 = kt([P, NG, 4], F32, "n2")
+        nrm = kt([P, NG, 4], F32, "nrm")
+        rn = kt([P, NG, 4], F32, "rn")
+        beta = kt([P, NG, 4], F32, "beta")
+        r2 = kt([P, NG, 4], F32, "r2")
+        negr = kt([P, NG, 4], F32, "negr")
+        gam = kt([P, NG, 4], F32, "gam")
+        idf = kt([P, P], F32, "idf")
+        warm = kt([P, 1], F32, "warm")
+
+        g4 = g.rearrange("(q p j) o -> q p j o", p=P, j=4)
+        x4 = x_bytes.rearrange("(q p j) i -> q p j i", p=P, j=4)
+        v4 = v.rearrange("(s n p) o -> s p n o", p=P, n=4)
+        nc.scalar.dma_start(out=xs[:], in_=x_scale.rearrange("(q p j) o -> p q (j o)", p=P, j=4))
+
+        def load_x(q):
+            nc.sync.dma_start(out=xb[q][:], in_=x4[q])
+
+        def load_g(q):
+            nc.sync.dma_start(out=gr[q][:], in_=g4[q])
+
+        def load_v(h):
+            for s in range(2):
+                nc.sync.dma_start(out=vr[s][h][:], in_=v4[s][:, :, HALF * h : HALF * (h + 1)])
+
+        for h in range(NG):
+            nc.sync.dma_start(out=xb[0][:, 2 * h : 2 * h + 2, :], in_=x4[0][:, 2 * h : 2 * h + 2, :])
+            nc.sync.dma_start(out=gr[0][:, :, HALF * h : HALF * (h + 1)], in_=g4[0][:, :, HALF * h : HALF * (h + 1)])
+        load_x(1)
+        load_v(0)
+        load_x(2)
+        load_g(1)
+        load_x(3)
+        load_v(1)
+        load_g(2)
+        load_g(3)
+        nc.gpsimd.memset(warm[:], 1.0)
+        make_identity(nc, idf[:])
+        nc.gpsimd.memset(ws[:].rearrange("p g n -> p (g n)").bitcast(I32), 0)
+        nc.sync.dma_start(out=mt[:], in_=m.rearrange("(h p t) -> p h t", p=P, t=4))
+        nc.sync.dma_start(out=ww[:].rearrange("p g n -> p (g n)").bitcast(I32).rearrange("p (g n) -> p g n", g=NG),
+                          in_=b_words.bitcast(I32).rearrange("g p n -> p g n"))
+        ws32 = ws[:].rearrange("p g n -> p (g n)").bitcast(I32).rearrange("p (g n) -> p g n", g=NG)
+        bs32 = b_scales.bitcast(I32)
+        for quad in range(4):
+            nc.sync.dma_start(out=ws32[32 * quad : 32 * quad + 4, :, :],
+                              in_=bs32[:, 4 * quad : 4 * quad + 4, :].rearrange("g q n -> q g n"))
+
+        nc.scalar.activation(warm[:], warm[:], ACT.Sqrt)
+
+        xp = {}
+        xi = {}
+        gi = {}
+
+        def widen_v(q, j):
+            nc.vector.tensor_scalar(out=xp[q][:, j, :], in0=xb[q][:, j, :].bitcast(FP8), scalar1=xs[:, q, j : j + 1], scalar2=None, op0=ALU.mult)
+
+        def widen_s(q, j):
+            nc.scalar.activation(xp[q][:, j, :], xb[q][:, j, :].bitcast(FP8), ACT.Copy, scale=xs[:, q, j : j + 1])
+
+        def new_xp(q):
+            xp[q] = wt([P, 4, DI], BF16, "xp", 2)
+
+        def ileave_x(q):
+            xi[q] = wt([P, 4 * DI], BF16, "xi", 2)
+            nc.vector.tensor_copy(
+                out=xi[q][:].rearrange("p (c i t) -> p c t i", i=4, t=4),
+                in_=xp[q][:].rearrange("p t (c i) -> p c t i", i=4),
+            )
+
+        def quant_x(q):
+            nc.vector.quantize_mx(out=xc[:, q, :].bitcast(E4M3X4), scales=xcs[:, q, :], in_=xi[q][:])
+
+        def ileave_g(q, h, copy=nc.scalar.copy):
+            gi[q, h] = wt([P, 4 * HALF], BF16, "gi", 3)
+            copy(
+                gi[q, h][:].rearrange("p (t m j) -> p t m j", t=4, j=4),
+                gr[q][:, :, HALF * h : HALF * (h + 1)].rearrange("p j (m t) -> p t m j", t=4),
+            )
+
+        def quant_g(q, h):
+            cols = slice(HALF * h, HALF * (h + 1))
+            nc.vector.quantize_mx(out=gc[:, q, cols].bitcast(E4M3X4), scales=gcs[:, q, cols], in_=gi[q, h][:])
+
+        def vt_bf(h, t):
+            u, e = divmod(t, 2)
+            return vt[h][u][:].bitcast(BF16).rearrange("p (i e) -> p i e", e=2)[:, :, e]
+
+        def turn_v(h, u):
+            for s in range(2):
+                bank = bank_aux([P, HALF], F32)
+                for a in range(4):
+                    words = vr[s][h][:, a, :].bitcast(F32)
+                    nc.tensor.transpose(bank[:, P * a : P * (a + 1)], words[:, u : 256 : 2], idf[:])
+                nc.scalar.copy(vt[h][u][:, HALF * s : HALF * (s + 1)], bank[:])
+
+        def gram(h):
+            bank = bank_aux([P, 4, P], F32)
+            for t in range(4):
+                for n in range(8):
+                    cols = vr[n // 4][h][:, n % 4, t : HALF : 4]
+                    nc.tensor.matmul(bank[:, t, :], lhsT=cols, rhs=cols, start=(n == 0), stop=(n == 7))
+            return bank
+
+        def norms(h, bank):
+            for t in range(4):
+                dump = wt([P, P], F32, "norm_dump", 2)
+                nc.vector.scalar_tensor_tensor(out=dump[:], in0=bank[:, t, :], scalar=1.0, in1=idf[:], op0=ALU.mult, op1=ALU.mult, accum_out=n2[:, h, t : t + 1])
+
+        def root(h):
+            nc.scalar.activation(nrm[:, h, :], n2[:, h, :], ACT.Sqrt)
+
+        def factors(h):
+            nc.vector.reciprocal(r2[:, h, :], n2[:, h, :])
+            nc.vector.reciprocal(rn[:, h, :], nrm[:, h, :])
+            nc.gpsimd.tensor_scalar(negr[:, h, :], r2[:, h, :], -1.0, None, op0=ALU.mult)
+            nc.gpsimd.tensor_tensor(beta[:, h, :], rn[:, h, :], mt[:, h, :], op=ALU.mult)
+
+        banks = {}
+
+        def mm1(k, q):
+            for h in range(2):
+                if q == 0:
+                    banks[k, h] = bank_gw()
+                nc.tensor.matmul_mx(
+                    banks[k, h][:],
+                    lhsT=gc[:, q, P * k : P * (k + 1)].bitcast(E4M3X4), lhsT_scale=gcs[:, q, P * k : P * (k + 1)],
+                    rhs=xc[:, q, HALF * h : HALF * (h + 1)].bitcast(E4M3X4), rhs_scale=xcs[:, q, HALF * h : HALF * (h + 1)],
+                    start=(q == 0), stop=(q == NQ - 1),
+                )
+
+        gw = {}
+        dvp = {}
+        dvi = {}
+
+        def evac(k):
+            h, t = divmod(k, 4)
+            gw[k] = wt([P, DI], F32, "gw", 4)
+            for s in range(2):
+                nc.scalar.activation(gw[k][:, HALF * s : HALF * (s + 1)], banks[k, s][:], ACT.Copy, scale=beta[:, h, t : t + 1])
+
+        def fold(k):
+            h, t = divmod(k, 4)
+            dump = wt([P, DI], F32, "fold_dump", 1)
+            nc.vector.scalar_tensor_tensor(out=dump[:], in0=gw[k][:], scalar=negr[:, h, t : t + 1], in1=vt_bf(h, t), op0=ALU.mult, op1=ALU.mult, accum_out=gam[:, h, t : t + 1])
+
+        def direction(k, cols=slice(0, DI)):
+            h, t = divmod(k, 4)
+            if t == 0:
+                dvp[h] = wt([P, 4, DI], BF16, "dvp", 2)
+            nc.vector.scalar_tensor_tensor(out=dvp[h][:, t, cols], in0=vt_bf(h, t)[:, cols], scalar=gam[:, h, t : t + 1], in1=gw[k][:, cols], op0=ALU.mult, op1=ALU.add)
+
+        def ileave_d(h, c, copy):
+            dvi[h, c] = wt([P, 1024], BF16, "dvi", 4)
+            copy(
+                dvi[h, c][:].rearrange("p (c i t) -> p c t i", i=4, t=4),
+                dvp[h][:, :, 256 * c : 256 * (c + 1)].rearrange("p t (c i) -> p c t i", i=4),
+            )
+
+        def quant_d(h, c):
+            cols = slice(256 * c, 256 * (c + 1))
+            nc.vector.quantize_mx(out=dc[:, h, cols].bitcast(E4M3X4), scales=dcs[:, h, cols], in_=dvi[h, c][:])
+
+        def mm2(c, copies):
+            rows_out = out[256 * c : 256 * (c + 1), :].rearrange("(a p) r -> a p r", p=P)
+            for a in range(2):
+                bank = bank_gw()
+                rows = slice(256 * c + P * a, 256 * c + P * (a + 1))
+                for r0 in range(0, R, P):
+                    for h in range(NG):
+                        nc.tensor.matmul_mx(
+                            bank[:, r0 : r0 + P],
+                            lhsT=dc[:, h, rows].bitcast(E4M3X4), lhsT_scale=dcs[:, h, rows],
+                            rhs=ww[:, h, 2 * r0 : 2 * (r0 + P)].bitcast(E2M1X4), rhs_scale=ws[:, h, r0 : r0 + P],
+                            start=(h == 0), stop=(h == NG - 1),
+                        )
+                res = wt([P, R], F32, "res", 4)
+                copies[a](res[:], bank[:, 0:R])
+                nc.sync.dma_start(out=rows_out[a], in_=res[:])
+
+        def widen(q):
+            new_xp(q)
+            for j in range(4):
+                if j in SCALAR_WIDENS[q]:
+                    widen_s(q, j)
+                else:
+                    widen_v(q, j)
+
+        def mm_pass(q):
+            for k in range(3):
+                mm1(k, q)
+
+        widen(0)
+        ileave_g(0, 0, nc.vector.tensor_copy)
+        quant_g(0, 0)
+        ileave_g(0, 1, nc.vector.tensor_copy)
+        widen(1)
+        ileave_x(0)
+        quant_g(0, 1)
+        quant_x(0)
+        gram0 = gram(0)
+        mm_pass(0)
+        ileave_x(1)
+        widen(2)
+        turn_v(0, 0)
+        ileave_g(1, 0, nc.vector.tensor_copy)
+        quant_x(1)
+        norms(0, gram0)
+        quant_g(1, 0)
+        root(0)
+        mm_pass(1)
+        ileave_g(1, 1)
+        ileave_x(2)
+        widen(3)
+        factors(0)
+        gram1 = gram(1)
+        quant_g(1, 1)
+        ileave_g(2, 0, nc.vector.tensor_copy)
+        quant_x(2)
+        quant_g(2, 0)
+        norms(1, gram1)
+        mm_pass(2)
+        ileave_g(3, 0)
+        root(1)
+        turn_v(0, 1)
+        ileave_x(3)
+        factors(1)
+        quant_g(3, 0)
+        quant_x(3)
+        mm_pass(3)
+        ileave_g(2, 1)
+        ileave_g(3, 1, nc.vector.tensor_copy)
+        quant_g(2, 1)
+        quant_g(3, 1)
+        evac(0)
+        evac(1)
+        for q in range(NQ):
+            mm1(3, q)
+        fold(0)
+        evac(2)
+        turn_v(1, 0)
+        fold(1)
+        direction(0)
+        for q in range(NQ):
+            mm1(4, q)
+        fold(2)
+        direction(1)
+        evac(3)
+        turn_v(1, 1)
+        fold(3)
+        direction(2)
+        for k in (5, 6):
+            for q in range(NQ):
+                mm1(k, q)
+        direction(3)
+        evac(4)
+        evac(5)
+        fold(4)
+        for q in range(NQ):
+            mm1(7, q)
+        ileave_d(0, 0, nc.scalar.copy)
+        evac(6)
+        fold(5)
+        direction(4)
+        ileave_d(0, 1, nc.scalar.copy)
+        evac(7)
+        fold(6)
+        direction(5)
+        quant_d(0, 0)
+        ileave_d(0, 2, nc.scalar.copy)
+        fold(7)
+        direction(6)
+        quant_d(0, 1)
+        ileave_d(0, 3, nc.scalar.copy)
+        direction(7, slice(0, HALF))
+        quant_d(0, 2)
+        ileave_d(1, 0, nc.vector.tensor_copy)
+        ileave_d(1, 1, nc.scalar.copy)
+        direction(7, slice(HALF, DI))
+        quant_d(0, 3)
+        quant_d(1, 0)
+        ileave_d(1, 2, nc.vector.tensor_copy)
+        ileave_d(1, 3, nc.scalar.copy)
+        mm2(0, [nc.scalar.copy] * 2)
+        quant_d(1, 1)
+        mm2(1, [nc.scalar.copy] * 2)
+        quant_d(1, 2)
+        mm2(2, [nc.scalar.copy] * 2)
+        quant_d(1, 3)
+        mm2(3, [nc.scalar.copy, nc.vector.tensor_copy])

@@ -21,8 +21,7 @@ ALU = mybir.AluOpType
 NQ = T // 512
 NG = DO // 512
 HALF = 512
-
-SCALAR_WIDENS = {0: (0, 2, 3), 1: (0, 1, 2, 3), 2: (0, 1, 2, 3), 3: (0, 1, 2, 3)}
+QUART = 256
 
 
 def tile_doradirectiongradienttoloradown_w4_kernel(tc, x_bytes, x_scale, g, v, m, b_words, b_scales, out):
@@ -41,19 +40,18 @@ def tile_doradirectiongradienttoloradown_w4_kernel(tc, x_bytes, x_scale, g, v, m
             t = work.tile(shape, dtype, name=name, tag=name, bufs=bufs, align_bytes=64)
             return t
 
-        def bank_gw():
-            t = psum.tile([P, HALF], F32, name="gw_bank", tag="gw_bank", bufs=6)
+        def bank_mx():
+            t = psum.tile([P, HALF], F32, name="mx_bank", tag="mx_bank", bufs=6)
             return t
 
-        def bank_aux(shape, dtype):
-            t = psum.tile(shape, dtype, name="aux_bank", tag="aux_bank", bufs=2)
+        def bank_v(shape, dtype):
+            t = psum.tile(shape, dtype, name="v_bank", tag="v_bank", bufs=2)
             return t
 
         xs = kt([P, NQ, 4], F32, "xs")
         xb = [kt([P, 4, DI], U8, f"xb{q}") for q in range(NQ)]
-        gr = [kt([P, 4, DO], BF16, f"gr{q}") for q in range(NQ)]
+        gr = [[kt([P, 4, HALF], BF16, f"gr{q}_{h}") for h in range(NG)] for q in range(NQ)]
         vr = [[kt([P, 4, HALF], BF16, f"vr{s}_{h}") for h in range(NG)] for s in range(2)]
-        vt = [[kt([P, DI], F32, f"vt{h}_{u}") for u in range(2)] for h in range(NG)]
         xc = kt([P, NQ, DI], U32, "xc")
         xcs = kt([P, NQ, DI], U8, "xcs")
         gc = kt([P, NQ, DO], U32, "gc")
@@ -64,45 +62,46 @@ def tile_doradirectiongradienttoloradown_w4_kernel(tc, x_bytes, x_scale, g, v, m
         ws = kt([P, NG, R], U8, "ws")
         mt = kt([P, NG, 4], BF16, "mt")
         n2 = kt([P, NG, 4], F32, "n2")
-        nrm = kt([P, NG, 4], F32, "nrm")
-        rn = kt([P, NG, 4], F32, "rn")
-        beta = kt([P, NG, 4], F32, "beta")
         r2 = kt([P, NG, 4], F32, "r2")
-        negr = kt([P, NG, 4], F32, "negr")
+        rn = kt([P, NG, 4], F32, "rn")
+        nbeta = kt([P, NG, 4], F32, "nbeta")
         gam = kt([P, NG, 4], F32, "gam")
-        idf = kt([P, P], F32, "idf")
+        ident = kt([P, P], BF16, "ident")
         warm = kt([P, 1], F32, "warm")
 
         g4 = g.rearrange("(q p j) o -> q p j o", p=P, j=4)
         x4 = x_bytes.rearrange("(q p j) i -> q p j i", p=P, j=4)
         v4 = v.rearrange("(s n p) o -> s p n o", p=P, n=4)
+
+        def load_x(q, rows=slice(0, 4)):
+            nc.sync.dma_start(out=xb[q][:, rows, :], in_=x4[q][:, rows, :])
+
+        def load_g(q, h):
+            nc.sync.dma_start(out=gr[q][h][:], in_=g4[q][:, :, HALF * h : HALF * (h + 1)])
+
+        def load_v(s, h):
+            nc.sync.dma_start(out=vr[s][h][:], in_=v4[s][:, :, HALF * h : HALF * (h + 1)])
+
         nc.scalar.dma_start(out=xs[:], in_=x_scale.rearrange("(q p j) o -> p q (j o)", p=P, j=4))
-
-        def load_x(q):
-            nc.sync.dma_start(out=xb[q][:], in_=x4[q])
-
-        def load_g(q):
-            nc.sync.dma_start(out=gr[q][:], in_=g4[q])
-
-        def load_v(h):
-            for s in range(2):
-                nc.sync.dma_start(out=vr[s][h][:], in_=v4[s][:, :, HALF * h : HALF * (h + 1)])
-
-        for h in range(NG):
-            nc.sync.dma_start(out=xb[0][:, 2 * h : 2 * h + 2, :], in_=x4[0][:, 2 * h : 2 * h + 2, :])
-            nc.sync.dma_start(out=gr[0][:, :, HALF * h : HALF * (h + 1)], in_=g4[0][:, :, HALF * h : HALF * (h + 1)])
+        load_x(0, slice(0, 2))
+        load_x(0, slice(2, 4))
         load_x(1)
-        load_v(0)
+        load_g(0, 0)
+        load_v(0, 0)
         load_x(2)
-        load_g(1)
+        load_v(1, 0)
+        load_g(1, 0)
         load_x(3)
-        load_v(1)
-        load_g(2)
-        load_g(3)
+        load_v(0, 1)
+        load_v(1, 1)
+        load_g(2, 0)
+        load_g(3, 0)
         nc.gpsimd.memset(warm[:], 1.0)
-        make_identity(nc, idf[:])
+        make_identity(nc, ident[:])
         nc.gpsimd.memset(ws[:].rearrange("p g n -> p (g n)").bitcast(I32), 0)
         nc.sync.dma_start(out=mt[:], in_=m.rearrange("(h p t) -> p h t", p=P, t=4))
+        for q in range(NQ):
+            load_g(q, 1)
         nc.sync.dma_start(out=ww[:].rearrange("p g n -> p (g n)").bitcast(I32).rearrange("p (g n) -> p g n", g=NG),
                           in_=b_words.bitcast(I32).rearrange("g p n -> p g n"))
         ws32 = ws[:].rearrange("p g n -> p (g n)").bitcast(I32).rearrange("p (g n) -> p g n", g=NG)
@@ -117,14 +116,13 @@ def tile_doradirectiongradienttoloradown_w4_kernel(tc, x_bytes, x_scale, g, v, m
         xi = {}
         gi = {}
 
-        def widen_v(q, j):
-            nc.vector.tensor_scalar(out=xp[q][:, j, :], in0=xb[q][:, j, :].bitcast(FP8), scalar1=xs[:, q, j : j + 1], scalar2=None, op0=ALU.mult)
-
-        def widen_s(q, j):
-            nc.scalar.activation(xp[q][:, j, :], xb[q][:, j, :].bitcast(FP8), ACT.Copy, scale=xs[:, q, j : j + 1])
-
-        def new_xp(q):
+        def widen(q, on_vector=()):
             xp[q] = wt([P, 4, DI], BF16, "xp", 2)
+            for j in range(4):
+                if j in on_vector:
+                    nc.vector.tensor_scalar(out=xp[q][:, j, :], in0=xb[q][:, j, :].bitcast(FP8), scalar1=xs[:, q, j : j + 1], scalar2=None, op0=ALU.mult)
+                else:
+                    nc.scalar.activation(xp[q][:, j, :], xb[q][:, j, :].bitcast(FP8), ACT.Copy, scale=xs[:, q, j : j + 1])
 
         def ileave_x(q):
             xi[q] = wt([P, 4 * DI], BF16, "xi", 2)
@@ -136,220 +134,239 @@ def tile_doradirectiongradienttoloradown_w4_kernel(tc, x_bytes, x_scale, g, v, m
         def quant_x(q):
             nc.vector.quantize_mx(out=xc[:, q, :].bitcast(E4M3X4), scales=xcs[:, q, :], in_=xi[q][:])
 
-        def ileave_g(q, h, copy=nc.scalar.copy):
-            gi[q, h] = wt([P, 4 * HALF], BF16, "gi", 3)
+        def ileave_g(q, h, copy):
+            gi[q, h] = wt([P, 4 * HALF], BF16, "gi", 4)
             copy(
                 gi[q, h][:].rearrange("p (t m j) -> p t m j", t=4, j=4),
-                gr[q][:, :, HALF * h : HALF * (h + 1)].rearrange("p j (m t) -> p t m j", t=4),
+                gr[q][h][:].rearrange("p j (m t) -> p t m j", t=4),
             )
 
         def quant_g(q, h):
             cols = slice(HALF * h, HALF * (h + 1))
             nc.vector.quantize_mx(out=gc[:, q, cols].bitcast(E4M3X4), scales=gcs[:, q, cols], in_=gi[q, h][:])
 
-        def vt_bf(h, t):
-            u, e = divmod(t, 2)
-            return vt[h][u][:].bitcast(BF16).rearrange("p (i e) -> p i e", e=2)[:, :, e]
+        def v_block(h, t, n):
+            return vr[n // 4][h][:, n % 4, t : HALF : 4]
 
-        def turn_v(h, u):
-            for s in range(2):
-                bank = bank_aux([P, HALF], F32)
-                for a in range(4):
-                    words = vr[s][h][:, a, :].bitcast(F32)
-                    nc.tensor.transpose(bank[:, P * a : P * (a + 1)], words[:, u : 256 : 2], idf[:])
-                nc.scalar.copy(vt[h][u][:, HALF * s : HALF * (s + 1)], bank[:])
+        grams = {}
 
         def gram(h):
-            bank = bank_aux([P, 4, P], F32)
-            for t in range(4):
-                for n in range(8):
-                    cols = vr[n // 4][h][:, n % 4, t : HALF : 4]
-                    nc.tensor.matmul(bank[:, t, :], lhsT=cols, rhs=cols, start=(n == 0), stop=(n == 7))
-            return bank
+            grams[h] = bank_v([P, 4, P], F32)
+            for n in range(8):
+                for t in range(4):
+                    nc.tensor.matmul(grams[h][:, t, :], lhsT=v_block(h, t, n), rhs=v_block(h, t, n), start=(n == 0 and t == 0), stop=(n == 7 and t == 3))
 
-        def norms(h, bank):
+        def norms(h):
             for t in range(4):
-                dump = wt([P, P], F32, "norm_dump", 2)
-                nc.vector.scalar_tensor_tensor(out=dump[:], in0=bank[:, t, :], scalar=1.0, in1=idf[:], op0=ALU.mult, op1=ALU.mult, accum_out=n2[:, h, t : t + 1])
+                dump = wt([P, P], F32, "norm_dump", 4)
+                nc.vector.scalar_tensor_tensor(out=dump[:], in0=grams[h][:, t, :], scalar=1.0, in1=ident[:], op0=ALU.mult, op1=ALU.mult, accum_out=n2[:, h, t : t + 1])
+
+        vt = {}
+
+        def turn_v(k):
+            h, t = divmod(k, 4)
+            vt[k] = bank_v([P, DI], BF16)
+            for n in range(8):
+                nc.tensor.transpose(vt[k][:, P * n : P * (n + 1)], v_block(h, t, n), ident[:])
+
+        def park_v(k):
+            parked = kt([P, DI], BF16, f"vt{k}")
+            nc.scalar.copy(parked[:], vt[k][:])
+            vt[k] = parked
+
+        def inverse(h):
+            nc.vector.reciprocal(r2[:, h, :], n2[:, h, :])
 
         def root(h):
-            nc.scalar.activation(nrm[:, h, :], n2[:, h, :], ACT.Sqrt)
+            nc.scalar.activation(rn[:, h, :], r2[:, h, :], ACT.Sqrt)
 
-        def factors(h):
-            nc.vector.reciprocal(r2[:, h, :], n2[:, h, :])
-            nc.vector.reciprocal(rn[:, h, :], nrm[:, h, :])
-            nc.gpsimd.tensor_scalar(negr[:, h, :], r2[:, h, :], -1.0, None, op0=ALU.mult)
-            nc.gpsimd.tensor_tensor(beta[:, h, :], rn[:, h, :], mt[:, h, :], op=ALU.mult)
+        def factor(h):
+            nc.vector.scalar_tensor_tensor(out=nbeta[:, h, :], in0=rn[:, h, :], scalar=-1.0, in1=mt[:, h, :], op0=ALU.mult, op1=ALU.mult)
 
         banks = {}
 
-        def mm1(k, q):
-            for h in range(2):
-                if q == 0:
-                    banks[k, h] = bank_gw()
-                nc.tensor.matmul_mx(
-                    banks[k, h][:],
-                    lhsT=gc[:, q, P * k : P * (k + 1)].bitcast(E4M3X4), lhsT_scale=gcs[:, q, P * k : P * (k + 1)],
-                    rhs=xc[:, q, HALF * h : HALF * (h + 1)].bitcast(E4M3X4), rhs_scale=xcs[:, q, HALF * h : HALF * (h + 1)],
-                    start=(q == 0), stop=(q == NQ - 1),
-                )
-
-        gw = {}
-        dvp = {}
-        dvi = {}
-
-        def evac(k):
-            h, t = divmod(k, 4)
-            gw[k] = wt([P, DI], F32, "gw", 4)
-            for s in range(2):
-                nc.scalar.activation(gw[k][:, HALF * s : HALF * (s + 1)], banks[k, s][:], ACT.Copy, scale=beta[:, h, t : t + 1])
-
-        def fold(k):
-            h, t = divmod(k, 4)
-            dump = wt([P, DI], F32, "fold_dump", 1)
-            nc.vector.scalar_tensor_tensor(out=dump[:], in0=gw[k][:], scalar=negr[:, h, t : t + 1], in1=vt_bf(h, t), op0=ALU.mult, op1=ALU.mult, accum_out=gam[:, h, t : t + 1])
-
-        def direction(k, cols=slice(0, DI)):
-            h, t = divmod(k, 4)
-            if t == 0:
-                dvp[h] = wt([P, 4, DI], BF16, "dvp", 2)
-            nc.vector.scalar_tensor_tensor(out=dvp[h][:, t, cols], in0=vt_bf(h, t)[:, cols], scalar=gam[:, h, t : t + 1], in1=gw[k][:, cols], op0=ALU.mult, op1=ALU.add)
-
-        def ileave_d(h, c, copy):
-            dvi[h, c] = wt([P, 1024], BF16, "dvi", 4)
-            copy(
-                dvi[h, c][:].rearrange("p (c i t) -> p c t i", i=4, t=4),
-                dvp[h][:, :, 256 * c : 256 * (c + 1)].rearrange("p t (c i) -> p c t i", i=4),
-            )
-
-        def quant_d(h, c):
-            cols = slice(256 * c, 256 * (c + 1))
-            nc.vector.quantize_mx(out=dc[:, h, cols].bitcast(E4M3X4), scales=dcs[:, h, cols], in_=dvi[h, c][:])
-
-        def mm2(c, copies):
-            rows_out = out[256 * c : 256 * (c + 1), :].rearrange("(a p) r -> a p r", p=P)
-            for a in range(2):
-                bank = bank_gw()
-                rows = slice(256 * c + P * a, 256 * c + P * (a + 1))
-                for r0 in range(0, R, P):
-                    for h in range(NG):
-                        nc.tensor.matmul_mx(
-                            bank[:, r0 : r0 + P],
-                            lhsT=dc[:, h, rows].bitcast(E4M3X4), lhsT_scale=dcs[:, h, rows],
-                            rhs=ww[:, h, 2 * r0 : 2 * (r0 + P)].bitcast(E2M1X4), rhs_scale=ws[:, h, r0 : r0 + P],
-                            start=(h == 0), stop=(h == NG - 1),
-                        )
-                res = wt([P, R], F32, "res", 4)
-                copies[a](res[:], bank[:, 0:R])
-                nc.sync.dma_start(out=rows_out[a], in_=res[:])
-
-        def widen(q):
-            new_xp(q)
-            for j in range(4):
-                if j in SCALAR_WIDENS[q]:
-                    widen_s(q, j)
-                else:
-                    widen_v(q, j)
+        def mm1(k, passes):
+            for q in passes:
+                for s in range(2):
+                    if q == 0:
+                        banks[k, s] = bank_mx()
+                    nc.tensor.matmul_mx(
+                        banks[k, s][:],
+                        lhsT=gc[:, q, P * k : P * (k + 1)].bitcast(E4M3X4), lhsT_scale=gcs[:, q, P * k : P * (k + 1)],
+                        rhs=xc[:, q, HALF * s : HALF * (s + 1)].bitcast(E4M3X4), rhs_scale=xcs[:, q, HALF * s : HALF * (s + 1)],
+                        start=(q == 0), stop=(q == NQ - 1),
+                    )
 
         def mm_pass(q):
             for k in range(3):
-                mm1(k, q)
+                mm1(k, [q])
 
-        widen(0)
-        ileave_g(0, 0, nc.vector.tensor_copy)
-        quant_g(0, 0)
-        ileave_g(0, 1, nc.vector.tensor_copy)
+        gs = {}
+        dvp = {}
+        dvi = [kt([P, 4 * DI], BF16, f"dvi{h}") for h in range(NG)]
+
+        def evac(k):
+            h, t = divmod(k, 4)
+            gs[k] = wt([P, DI], F32, "gs", 4)
+            for s in range(2):
+                nc.scalar.activation(gs[k][:, HALF * s : HALF * (s + 1)], banks[k, s][:], ACT.Copy, scale=nbeta[:, h, t : t + 1])
+
+        def fold(k):
+            h, t = divmod(k, 4)
+            dump = wt([P, DI], F32, "fold_dump", 2)
+            nc.vector.scalar_tensor_tensor(out=dump[:], in0=gs[k][:], scalar=r2[:, h, t : t + 1], in1=vt[k][:], op0=ALU.mult, op1=ALU.mult, accum_out=gam[:, h, t : t + 1])
+
+        def direction(k, chunks=slice(0, 4)):
+            h, t = divmod(k, 4)
+            if t == 0:
+                dvp[h] = wt([P, 4, 4, QUART], BF16, "dvp", 2)
+            nc.vector.scalar_tensor_tensor(
+                out=dvp[h][:, chunks, t, :], in0=vt[k][:].rearrange("p (c i) -> p c i", i=QUART)[:, chunks, :], scalar=gam[:, h, t : t + 1],
+                in1=gs[k][:].rearrange("p (c i) -> p c i", i=QUART)[:, chunks, :], op0=ALU.mult, op1=ALU.subtract)
+
+        def ileave_d(h, c, copy):
+            copy(
+                dvi[h][:, 4 * QUART * c : 4 * QUART * (c + 1)].rearrange("p (c i t) -> p c t i", i=4, t=4),
+                dvp[h][:, c, :, :].rearrange("p t (c i) -> p c t i", i=4),
+            )
+
+        def quant_d(h, cols):
+            nc.vector.quantize_mx(out=dc[:, h, cols].bitcast(E4M3X4), scales=dcs[:, h, cols], in_=dvi[h][:, 4 * cols.start : 4 * cols.stop])
+
+        outs = {}
+
+        def mm2(cols, h):
+            blocks = (cols.stop - cols.start) // P
+            if h == 0:
+                outs[cols.start] = bank_mx()
+            for a in range(blocks):
+                rows = slice(cols.start + P * a, cols.start + P * (a + 1))
+                for r0 in range(0, R, P):
+                    nc.tensor.matmul_mx(
+                        outs[cols.start][:, R * a + r0 : R * a + r0 + P],
+                        lhsT=dc[:, h, rows].bitcast(E4M3X4), lhsT_scale=dcs[:, h, rows],
+                        rhs=ww[:, h, 2 * r0 : 2 * (r0 + P)].bitcast(E2M1X4), rhs_scale=ws[:, h, r0 : r0 + P],
+                        start=(h == 0 and a == 0 and r0 == 0), stop=(h == NG - 1 and a == blocks - 1 and r0 == R - P),
+                    )
+
+        def store(cols, copy):
+            blocks = (cols.stop - cols.start) // P
+            res = kt([P, blocks * R], F32, f"res{cols.start}")
+            copy(res[:], outs[cols.start][:, 0 : blocks * R])
+            nc.sync.dma_start(out=out[cols, :].rearrange("(a p) r -> p a r", p=P), in_=res[:].rearrange("p (a r) -> p a r", r=R))
+
+        on_v, on_s = nc.vector.tensor_copy, nc.scalar.copy
+
+        quarter = [slice(256 * c, 256 * (c + 1)) for c in range(4)]
+        widen(0, on_vector=(1, 2, 3))
         widen(1)
         ileave_x(0)
-        quant_g(0, 1)
+        ileave_g(0, 0, on_v)
         quant_x(0)
-        gram0 = gram(0)
+        quant_g(0, 0)
+        gram(0)
+        gram(1)
         mm_pass(0)
-        ileave_x(1)
         widen(2)
-        turn_v(0, 0)
-        ileave_g(1, 0, nc.vector.tensor_copy)
+        ileave_x(1)
+        ileave_g(1, 0, on_v)
         quant_x(1)
-        norms(0, gram0)
+        norms(0)
         quant_g(1, 0)
-        root(0)
+        turn_v(4)
         mm_pass(1)
-        ileave_g(1, 1)
-        ileave_x(2)
         widen(3)
-        factors(0)
-        gram1 = gram(1)
-        quant_g(1, 1)
-        ileave_g(2, 0, nc.vector.tensor_copy)
+        inverse(0)
+        ileave_x(2)
+        norms(1)
         quant_x(2)
-        quant_g(2, 0)
-        norms(1, gram1)
-        mm_pass(2)
-        ileave_g(3, 0)
-        root(1)
-        turn_v(0, 1)
+        turn_v(6)
+        ileave_g(2, 0, on_s)
+        ileave_g(3, 0, on_s)
+        root(0)
+        park_v(4)
+        turn_v(0)
+        inverse(1)
         ileave_x(3)
-        factors(1)
-        quant_g(3, 0)
+        quant_g(2, 0)
+        mm_pass(2)
+        factor(0)
         quant_x(3)
+        quant_g(3, 0)
         mm_pass(3)
-        ileave_g(2, 1)
-        ileave_g(3, 1, nc.vector.tensor_copy)
-        quant_g(2, 1)
-        quant_g(3, 1)
+        ileave_g(0, 1, on_s)
+        park_v(6)
+        turn_v(1)
+        root(1)
+        ileave_g(1, 1, on_v)
+        quant_g(0, 1)
         evac(0)
+        factor(1)
         evac(1)
-        for q in range(NQ):
-            mm1(3, q)
+        mm1(3, range(NQ))
+        ileave_g(2, 1, on_s)
         fold(0)
-        evac(2)
-        turn_v(1, 0)
-        fold(1)
+        quant_g(1, 1)
         direction(0)
-        for q in range(NQ):
-            mm1(4, q)
-        fold(2)
+        turn_v(2)
+        mm1(4, [0, 1])
+        evac(2)
+        ileave_g(3, 1, on_s)
+        fold(1)
+        quant_g(2, 1)
         direction(1)
+        mm1(4, [2])
+        turn_v(3)
+        mm1(5, [0, 1, 2])
         evac(3)
-        turn_v(1, 1)
-        fold(3)
+        fold(2)
         direction(2)
-        for k in (5, 6):
-            for q in range(NQ):
-                mm1(k, q)
-        direction(3)
+        quant_g(3, 1)
+        mm1(4, [3])
+        mm1(5, [3])
+        turn_v(5)
+        fold(3)
         evac(4)
+        direction(3)
+        mm1(6, range(NQ))
         evac(5)
+        mm1(7, range(NQ))
+        turn_v(7)
         fold(4)
-        for q in range(NQ):
-            mm1(7, q)
-        ileave_d(0, 0, nc.scalar.copy)
+        ileave_d(0, 0, on_s)
+        ileave_d(0, 1, on_s)
+        direction(4)
         evac(6)
         fold(5)
-        direction(4)
-        ileave_d(0, 1, nc.scalar.copy)
-        evac(7)
-        fold(6)
+        quant_d(0, slice(0, 512))
         direction(5)
-        quant_d(0, 0)
-        ileave_d(0, 2, nc.scalar.copy)
+        evac(7)
+        ileave_d(0, 2, on_s)
+        ileave_d(0, 3, on_s)
+        fold(6)
+        mm2(quarter[0], 0)
+        mm2(quarter[1], 0)
         fold(7)
-        direction(6)
-        quant_d(0, 1)
-        ileave_d(0, 3, nc.scalar.copy)
-        direction(7, slice(0, HALF))
-        quant_d(0, 2)
-        ileave_d(1, 0, nc.vector.tensor_copy)
-        ileave_d(1, 1, nc.scalar.copy)
-        direction(7, slice(HALF, DI))
-        quant_d(0, 3)
-        quant_d(1, 0)
-        ileave_d(1, 2, nc.vector.tensor_copy)
-        ileave_d(1, 3, nc.scalar.copy)
-        mm2(0, [nc.scalar.copy] * 2)
-        quant_d(1, 1)
-        mm2(1, [nc.scalar.copy] * 2)
-        quant_d(1, 2)
-        mm2(2, [nc.scalar.copy] * 2)
-        quant_d(1, 3)
-        mm2(3, [nc.scalar.copy, nc.vector.tensor_copy])
+        direction(6, slice(0, 2))
+        direction(7, slice(0, 2))
+        ileave_d(1, 0, on_s)
+        ileave_d(1, 1, on_s)
+        direction(6, slice(2, 4))
+        quant_d(0, slice(512, 1024))
+        mm2(quarter[2], 0)
+        mm2(quarter[3], 0)
+        direction(7, slice(2, 4))
+        quant_d(1, quarter[0])
+        mm2(quarter[0], 1)
+        ileave_d(1, 2, on_v)
+        quant_d(1, quarter[1])
+        mm2(quarter[1], 1)
+        store(quarter[0], on_s)
+        ileave_d(1, 3, on_v)
+        quant_d(1, quarter[2])
+        mm2(quarter[2], 1)
+        store(quarter[1], on_s)
+        quant_d(1, quarter[3])
+        mm2(quarter[3], 1)
+        store(quarter[2], on_s)
+        store(quarter[3], on_v)

@@ -137,8 +137,8 @@ def tile_doradirectiongradienttoloradown_w4_kernel(tc, x_bytes, x_scale, g, v, m
         def ileave_g(q, h, copy):
             gi[q, h] = wt([P, 4 * HALF], BF16, "gi", 4)
             copy(
-                gi[q, h][:].rearrange("p (t m j) -> p t m j", t=4, j=4),
-                gr[q][h][:].rearrange("p j (m t) -> p t m j", t=4),
+                gi[q, h][:].rearrange("p (t m j) -> p m j t", t=4, j=4),
+                gr[q][h][:].rearrange("p j (m t) -> p m j t", t=4),
             )
 
         def quant_g(q, h):

@@ -40,22 +40,18 @@ def tile_doradirectiongradienttoloradown_w4_kernel(tc, x_bytes, x_scale, g, v, m
             t = work.tile(shape, dtype, name=name, tag=name, bufs=bufs, align_bytes=64)
             return t
 
-        def bank_mx():
-            t = psum.tile([P, HALF], F32, name="mx_bank", tag="mx_bank", bufs=6)
-            return t
-
-        def bank_v(shape, dtype):
-            t = psum.tile(shape, dtype, name="v_bank", tag="v_bank", bufs=2)
+        def bank(b, shape, dtype):
+            t = psum.tile(shape, dtype, name=f"bank{b}", tag=f"bank{b}", bufs=1)
             return t
 
         xs = kt([P, NQ, 4], F32, "xs")
         xb = [kt([P, 4, DI], U8, f"xb{q}") for q in range(NQ)]
-        gr = [[kt([P, 4, HALF], BF16, f"gr{q}_{h}") for h in range(NG)] for q in range(NQ)]
+        gr = [[kt([P, 2, 4, HALF], BF16, f"gr{w}_{h}") for h in range(NG)] for w in range(2)]
         vr = [[kt([P, 4, HALF], BF16, f"vr{s}_{h}") for h in range(NG)] for s in range(2)]
         xc = kt([P, NQ, DI], U32, "xc")
         xcs = kt([P, NQ, DI], U8, "xcs")
-        gc = kt([P, NQ, DO], U32, "gc")
-        gcs = kt([P, NQ, DO], U8, "gcs")
+        gc = kt([P, 4, 2, 2, 2, P], U32, "gc")
+        gcs = kt([P, 4, 2, 2, 2, P], U8, "gcs")
         dc = kt([P, NG, DI], U32, "dc")
         dcs = kt([P, NG, DI], U8, "dcs")
         ww = kt([P, NG, 2 * R], U8, "ww")
@@ -77,7 +73,7 @@ def tile_doradirectiongradienttoloradown_w4_kernel(tc, x_bytes, x_scale, g, v, m
             nc.sync.dma_start(out=xb[q][:, rows, :], in_=x4[q][:, rows, :])
 
         def load_g(q, h):
-            nc.sync.dma_start(out=gr[q][h][:], in_=g4[q][:, :, HALF * h : HALF * (h + 1)])
+            nc.sync.dma_start(out=gr[q // 2][h][:, q % 2, :, :], in_=g4[q][:, :, HALF * h : HALF * (h + 1)])
 
         def load_v(s, h):
             nc.sync.dma_start(out=vr[s][h][:], in_=v4[s][:, :, HALF * h : HALF * (h + 1)])
@@ -86,10 +82,10 @@ def tile_doradirectiongradienttoloradown_w4_kernel(tc, x_bytes, x_scale, g, v, m
         load_x(0, slice(0, 2))
         load_x(0, slice(2, 4))
         load_x(1)
-        load_g(0, 0)
         load_v(0, 0)
         load_x(2)
         load_v(1, 0)
+        load_g(0, 0)
         load_g(1, 0)
         load_x(3)
         load_v(0, 1)
@@ -116,13 +112,15 @@ def tile_doradirectiongradienttoloradown_w4_kernel(tc, x_bytes, x_scale, g, v, m
         xi = {}
         gi = {}
 
-        def widen(q, on_vector=()):
-            xp[q] = wt([P, 4, DI], BF16, "xp", 2)
-            for j in range(4):
-                if j in on_vector:
-                    nc.vector.tensor_scalar(out=xp[q][:, j, :], in0=xb[q][:, j, :].bitcast(FP8), scalar1=xs[:, q, j : j + 1], scalar2=None, op0=ALU.mult)
-                else:
-                    nc.scalar.activation(xp[q][:, j, :], xb[q][:, j, :].bitcast(FP8), ACT.Copy, scale=xs[:, q, j : j + 1])
+        def widen_s(q, rows):
+            if 0 in rows:
+                xp[q] = wt([P, 4, DI], BF16, "xp", 2)
+            for j in rows:
+                nc.scalar.activation(xp[q][:, j, :], xb[q][:, j, :].bitcast(FP8), ACT.Copy, scale=xs[:, q, j : j + 1])
+
+        def widen_v(q, rows):
+            for j in rows:
+                nc.vector.tensor_scalar(out=xp[q][:, j, :], in0=xb[q][:, j, :].bitcast(FP8), scalar1=xs[:, q, j : j + 1], scalar2=None, op0=ALU.mult)
 
         def ileave_x(q):
             xi[q] = wt([P, 4 * DI], BF16, "xi", 2)
@@ -134,16 +132,18 @@ def tile_doradirectiongradienttoloradown_w4_kernel(tc, x_bytes, x_scale, g, v, m
         def quant_x(q):
             nc.vector.quantize_mx(out=xc[:, q, :].bitcast(E4M3X4), scales=xcs[:, q, :], in_=xi[q][:])
 
-        def ileave_g(q, h, copy):
-            gi[q, h] = wt([P, 4 * HALF], BF16, "gi", 4)
+        def ileave_g(pair, w, copy, qs=slice(0, 2)):
+            h, u = divmod(pair, 2)
+            if qs.start == 0:
+                gi[pair, w] = wt([P, 4 * HALF], BF16, "gi", 4)
             copy(
-                gi[q, h][:].rearrange("p (t m j) -> p m j t", t=4, j=4),
-                gr[q][h][:].rearrange("p j (m t) -> p m j t", t=4),
+                gi[pair, w][:].rearrange("p (e q m j) -> p q m j e", e=2, q=2, j=4)[:, qs],
+                gr[w][h][:].rearrange("p q j (m u e) -> p u q m j e", u=2, e=2)[:, u, qs],
             )
 
-        def quant_g(q, h):
-            cols = slice(HALF * h, HALF * (h + 1))
-            nc.vector.quantize_mx(out=gc[:, q, cols].bitcast(E4M3X4), scales=gcs[:, q, cols], in_=gi[q, h][:])
+        def quant_g(pair, w):
+            nc.vector.quantize_mx(out=gc[:, pair, w].rearrange("p e q m -> p (e q m)").bitcast(E4M3X4),
+                                  scales=gcs[:, pair, w].rearrange("p e q m -> p (e q m)"), in_=gi[pair, w][:])
 
         def v_block(h, t, n):
             return vr[n // 4][h][:, n % 4, t : HALF : 4]
@@ -151,7 +151,7 @@ def tile_doradirectiongradienttoloradown_w4_kernel(tc, x_bytes, x_scale, g, v, m
         grams = {}
 
         def gram(h):
-            grams[h] = bank_v([P, 4, P], F32)
+            grams[h] = bank(h, [P, 4, P], F32)
             for n in range(8):
                 for t in range(4):
                     nc.tensor.matmul(grams[h][:, t, :], lhsT=v_block(h, t, n), rhs=v_block(h, t, n), start=(n == 0 and t == 0), stop=(n == 7 and t == 3))
@@ -165,14 +165,9 @@ def tile_doradirectiongradienttoloradown_w4_kernel(tc, x_bytes, x_scale, g, v, m
 
         def turn_v(k):
             h, t = divmod(k, 4)
-            vt[k] = bank_v([P, DI], BF16)
+            vt[k] = bank((k + 2) % 4, [P, DI], BF16)
             for n in range(8):
                 nc.tensor.transpose(vt[k][:, P * n : P * (n + 1)], v_block(h, t, n), ident[:])
-
-        def park_v(k):
-            parked = kt([P, DI], BF16, f"vt{k}")
-            nc.scalar.copy(parked[:], vt[k][:])
-            vt[k] = parked
 
         def inverse(h):
             nc.vector.reciprocal(r2[:, h, :], n2[:, h, :])
@@ -189,16 +184,16 @@ def tile_doradirectiongradienttoloradown_w4_kernel(tc, x_bytes, x_scale, g, v, m
             for q in passes:
                 for s in range(2):
                     if q == 0:
-                        banks[k, s] = bank_mx()
+                        banks[k, s] = bank(4 + 2 * (k % 2) + s, [P, HALF], F32)
                     nc.tensor.matmul_mx(
                         banks[k, s][:],
-                        lhsT=gc[:, q, P * k : P * (k + 1)].bitcast(E4M3X4), lhsT_scale=gcs[:, q, P * k : P * (k + 1)],
+                        lhsT=gc[:, k // 2, q // 2, k % 2, q % 2, :].bitcast(E4M3X4), lhsT_scale=gcs[:, k // 2, q // 2, k % 2, q % 2, :],
                         rhs=xc[:, q, HALF * s : HALF * (s + 1)].bitcast(E4M3X4), rhs_scale=xcs[:, q, HALF * s : HALF * (s + 1)],
                         start=(q == 0), stop=(q == NQ - 1),
                     )
 
         def mm_pass(q):
-            for k in range(3):
+            for k in range(2):
                 mm1(k, [q])
 
         gs = {}
@@ -235,10 +230,10 @@ def tile_doradirectiongradienttoloradown_w4_kernel(tc, x_bytes, x_scale, g, v, m
 
         outs = {}
 
-        def mm2(cols, h):
+        def mm2(cols, h, b=None):
             blocks = (cols.stop - cols.start) // P
             if h == 0:
-                outs[cols.start] = bank_mx()
+                outs[cols.start] = bank(b, [P, HALF], F32)
             for a in range(blocks):
                 rows = slice(cols.start + P * a, cols.start + P * (a + 1))
                 for r0 in range(0, R, P):
@@ -258,115 +253,116 @@ def tile_doradirectiongradienttoloradown_w4_kernel(tc, x_bytes, x_scale, g, v, m
         on_v, on_s = nc.vector.tensor_copy, nc.scalar.copy
 
         quarter = [slice(256 * c, 256 * (c + 1)) for c in range(4)]
-        widen(0, on_vector=(1, 2, 3))
-        widen(1)
+        eighth = [slice(128 * c, 128 * (c + 1)) for c in range(8)]
+        widen_s(0, [0])
+        widen_v(0, [1, 2, 3])
+        widen_s(1, [0, 1, 2])
         ileave_x(0)
-        ileave_g(0, 0, on_v)
+        widen_v(1, [3])
         quant_x(0)
-        quant_g(0, 0)
         gram(0)
-        gram(1)
-        mm_pass(0)
-        widen(2)
-        ileave_x(1)
-        ileave_g(1, 0, on_v)
-        quant_x(1)
-        norms(0)
-        quant_g(1, 0)
-        turn_v(4)
-        mm_pass(1)
-        widen(3)
-        inverse(0)
-        ileave_x(2)
-        norms(1)
-        quant_x(2)
-        turn_v(6)
-        ileave_g(2, 0, on_s)
-        ileave_g(3, 0, on_s)
-        root(0)
-        park_v(4)
         turn_v(0)
-        inverse(1)
-        ileave_x(3)
-        quant_g(2, 0)
-        mm_pass(2)
-        factor(0)
-        quant_x(3)
-        quant_g(3, 0)
-        mm_pass(3)
-        ileave_g(0, 1, on_s)
-        park_v(6)
         turn_v(1)
-        root(1)
-        ileave_g(1, 1, on_v)
+        gram(1)
+        widen_s(2, range(4))
+        ileave_x(1)
+        ileave_g(0, 0, on_v)
+        quant_x(1)
+        quant_g(0, 0)
+        mm_pass(0)
+        mm_pass(1)
+        widen_s(3, range(4))
+        ileave_x(2)
+        norms(0)
+        quant_x(2)
+        inverse(0)
+        turn_v(2)
+        ileave_g(0, 1, on_s)
+        root(0)
+        ileave_g(1, 0, on_s)
+        ileave_x(3)
         quant_g(0, 1)
+        mm_pass(2)
+        quant_x(3)
+        mm_pass(3)
+        factor(0)
+        norms(1)
+        turn_v(3)
+        ileave_g(1, 1, on_s)
+        quant_g(1, 0)
+        inverse(1)
+        ileave_g(2, 0, on_v)
+        quant_g(1, 1)
         evac(0)
-        factor(1)
+        mm1(2, range(NQ))
         evac(1)
+        root(1)
         mm1(3, range(NQ))
         ileave_g(2, 1, on_s)
         fold(0)
-        quant_g(1, 1)
+        quant_g(2, 0)
         direction(0)
-        turn_v(2)
-        mm1(4, [0, 1])
-        evac(2)
-        ileave_g(3, 1, on_s)
         fold(1)
         quant_g(2, 1)
-        direction(1)
-        mm1(4, [2])
-        turn_v(3)
-        mm1(5, [0, 1, 2])
+        evac(2)
+        mm1(4, range(NQ))
         evac(3)
-        fold(2)
-        direction(2)
-        quant_g(3, 1)
-        mm1(4, [3])
-        mm1(5, [3])
+        turn_v(4)
+        direction(1)
+        factor(1)
+        mm1(5, range(NQ))
         turn_v(5)
-        fold(3)
+        ileave_g(3, 0, on_s)
         evac(4)
+        ileave_g(3, 1, on_s)
+        fold(2)
+        fold(3)
+        direction(2)
+        quant_g(3, 0)
         direction(3)
-        mm1(6, range(NQ))
+        quant_g(3, 1)
         evac(5)
+        mm1(6, range(NQ))
+        turn_v(6)
         mm1(7, range(NQ))
         turn_v(7)
         fold(4)
+        fold(5)
         ileave_d(0, 0, on_s)
         ileave_d(0, 1, on_s)
-        direction(4)
         evac(6)
-        fold(5)
-        quant_d(0, slice(0, 512))
-        direction(5)
-        evac(7)
         ileave_d(0, 2, on_s)
+        evac(7)
         ileave_d(0, 3, on_s)
+        direction(4)
+        direction(5)
         fold(6)
-        mm2(quarter[0], 0)
-        mm2(quarter[1], 0)
+        quant_d(0, slice(0, 512))
+        mm2(quarter[0], 0, 4)
+        mm2(quarter[1], 0, 5)
+        direction(6)
         fold(7)
-        direction(6, slice(0, 2))
-        direction(7, slice(0, 2))
-        ileave_d(1, 0, on_s)
-        ileave_d(1, 1, on_s)
-        direction(6, slice(2, 4))
         quant_d(0, slice(512, 1024))
-        mm2(quarter[2], 0)
-        mm2(quarter[3], 0)
+        mm2(quarter[2], 0, 6)
+        mm2(eighth[6], 0, 7)
+        mm2(eighth[7], 0, 2)
+        direction(7, slice(0, 2))
+        ileave_d(1, 1, on_s)
         direction(7, slice(2, 4))
+        ileave_d(1, 3, on_s)
+        ileave_d(1, 0, on_v)
+        ileave_d(1, 2, on_v)
         quant_d(1, quarter[0])
         mm2(quarter[0], 1)
-        ileave_d(1, 2, on_v)
         quant_d(1, quarter[1])
         mm2(quarter[1], 1)
-        store(quarter[0], on_s)
-        ileave_d(1, 3, on_v)
         quant_d(1, quarter[2])
         mm2(quarter[2], 1)
-        store(quarter[1], on_s)
         quant_d(1, quarter[3])
-        mm2(quarter[3], 1)
+        mm2(eighth[6], 1)
+        mm2(eighth[7], 1)
+        store(quarter[0], on_s)
+        store(quarter[1], on_v)
         store(quarter[2], on_s)
-        store(quarter[3], on_v)
+        store(eighth[6], on_v)
+        store(eighth[7], on_v)

@@ -79,9 +79,11 @@ def tile_doradirectiongradienttoloradown_w4_kernel(tc, x_bytes, x_scale, g, v, m
             nc.sync.dma_start(out=vr[s][h][:], in_=v4[s][:, :, HALF * h : HALF * (h + 1)])
 
         nc.scalar.dma_start(out=xs[:], in_=x_scale.rearrange("(q p j) o -> p q (j o)", p=P, j=4))
-        load_x(0, slice(0, 2))
+        load_x(0, slice(0, 1))
+        load_x(0, slice(1, 2))
         load_x(0, slice(2, 4))
-        load_x(1)
+        load_x(1, slice(0, 2))
+        load_x(1, slice(2, 4))
         load_v(0, 0)
         load_x(2)
         load_v(1, 0)
@@ -112,9 +114,10 @@ def tile_doradirectiongradienttoloradown_w4_kernel(tc, x_bytes, x_scale, g, v, m
         xi = {}
         gi = {}
 
+        def planes(q):
+            xp[q] = wt([P, 4, DI], BF16, "xp", 3)
+
         def widen_s(q, rows):
-            if 0 in rows:
-                xp[q] = wt([P, 4, DI], BF16, "xp", 2)
             for j in rows:
                 nc.scalar.activation(xp[q][:, j, :], xb[q][:, j, :].bitcast(FP8), ACT.Copy, scale=xs[:, q, j : j + 1])
 
@@ -122,15 +125,16 @@ def tile_doradirectiongradienttoloradown_w4_kernel(tc, x_bytes, x_scale, g, v, m
             for j in rows:
                 nc.vector.tensor_scalar(out=xp[q][:, j, :], in0=xb[q][:, j, :].bitcast(FP8), scalar1=xs[:, q, j : j + 1], scalar2=None, op0=ALU.mult)
 
-        def ileave_x(q):
-            xi[q] = wt([P, 4 * DI], BF16, "xi", 2)
+        def ileave_x(q, cols=slice(0, DI)):
+            if cols.start == 0:
+                xi[q] = wt([P, 4 * DI], BF16, "xi", 2)
             nc.vector.tensor_copy(
-                out=xi[q][:].rearrange("p (c i t) -> p c t i", i=4, t=4),
-                in_=xp[q][:].rearrange("p t (c i) -> p c t i", i=4),
+                out=xi[q][:, 4 * cols.start : 4 * cols.stop].rearrange("p (c i t) -> p c t i", i=4, t=4),
+                in_=xp[q][:, :, cols].rearrange("p t (c i) -> p c t i", i=4),
             )
 
-        def quant_x(q):
-            nc.vector.quantize_mx(out=xc[:, q, :].bitcast(E4M3X4), scales=xcs[:, q, :], in_=xi[q][:])
+        def quant_x(q, cols=slice(0, DI)):
+            nc.vector.quantize_mx(out=xc[:, q, cols].bitcast(E4M3X4), scales=xcs[:, q, cols], in_=xi[q][:, 4 * cols.start : 4 * cols.stop])
 
         def ileave_g(pair, w, copy, qs=slice(0, 2)):
             h, u = divmod(pair, 2)
@@ -180,9 +184,9 @@ def tile_doradirectiongradienttoloradown_w4_kernel(tc, x_bytes, x_scale, g, v, m
 
         banks = {}
 
-        def mm1(k, passes):
-            for q in passes:
-                for s in range(2):
+        def mm1(k, passes, sides=(0, 1)):
+            for s in sides:
+                for q in passes:
                     if q == 0:
                         banks[k, s] = bank(4 + 2 * (k % 2) + s, [P, HALF], F32)
                     nc.tensor.matmul_mx(
@@ -192,23 +196,24 @@ def tile_doradirectiongradienttoloradown_w4_kernel(tc, x_bytes, x_scale, g, v, m
                         start=(q == 0), stop=(q == NQ - 1),
                     )
 
-        def mm_pass(q):
+        def mm_pass(q, sides=(0, 1)):
             for k in range(2):
-                mm1(k, [q])
+                mm1(k, [q], sides)
 
         gs = {}
         dvp = {}
         dvi = [kt([P, 4 * DI], BF16, f"dvi{h}") for h in range(NG)]
 
-        def evac(k):
+        def evac(k, sides=(0, 1)):
             h, t = divmod(k, 4)
-            gs[k] = wt([P, DI], F32, "gs", 4)
-            for s in range(2):
+            for s in sides:
+                if s == 0:
+                    gs[k] = wt([P, DI], F32, "gs", 4)
                 nc.scalar.activation(gs[k][:, HALF * s : HALF * (s + 1)], banks[k, s][:], ACT.Copy, scale=nbeta[:, h, t : t + 1])
 
         def fold(k):
             h, t = divmod(k, 4)
-            dump = wt([P, DI], F32, "fold_dump", 2)
+            dump = wt([P, DI], F32, "xi", 2)
             nc.vector.scalar_tensor_tensor(out=dump[:], in0=gs[k][:], scalar=r2[:, h, t : t + 1], in1=vt[k][:], op0=ALU.mult, op1=ALU.mult, accum_out=gam[:, h, t : t + 1])
 
         def direction(k, chunks=slice(0, 4)):
@@ -254,23 +259,27 @@ def tile_doradirectiongradienttoloradown_w4_kernel(tc, x_bytes, x_scale, g, v, m
 
         quarter = [slice(256 * c, 256 * (c + 1)) for c in range(4)]
         eighth = [slice(128 * c, 128 * (c + 1)) for c in range(8)]
-        widen_s(0, [0])
-        widen_v(0, [1, 2, 3])
-        widen_s(1, [0, 1, 2])
+        planes(0)
+        planes(1)
+        widen_s(0, [0, 3])
+        widen_v(0, [1, 2])
+        widen_v(1, [0, 1])
+        widen_s(1, [2, 3])
         ileave_x(0)
-        widen_v(1, [3])
+        planes(2)
+        widen_s(2, range(4))
+        ileave_x(1)
         quant_x(0)
         gram(0)
         turn_v(0)
         turn_v(1)
         gram(1)
-        widen_s(2, range(4))
-        ileave_x(1)
         ileave_g(0, 0, on_v)
         quant_x(1)
         quant_g(0, 0)
         mm_pass(0)
         mm_pass(1)
+        planes(3)
         widen_s(3, range(4))
         ileave_x(2)
         norms(0)
@@ -278,8 +287,8 @@ def tile_doradirectiongradienttoloradown_w4_kernel(tc, x_bytes, x_scale, g, v, m
         inverse(0)
         turn_v(2)
         ileave_g(0, 1, on_s)
-        root(0)
         ileave_g(1, 0, on_s)
+        root(0)
         ileave_x(3)
         quant_g(0, 1)
         mm_pass(2)
@@ -289,12 +298,14 @@ def tile_doradirectiongradienttoloradown_w4_kernel(tc, x_bytes, x_scale, g, v, m
         norms(1)
         turn_v(3)
         ileave_g(1, 1, on_s)
+        ileave_g(2, 0, on_s, slice(0, 1))
         quant_g(1, 0)
         inverse(1)
-        ileave_g(2, 0, on_v)
+        ileave_g(2, 0, on_v, slice(1, 2))
         quant_g(1, 1)
         evac(0)
-        mm1(2, range(NQ))
+        mm1(2, [0, 1])
+        mm1(2, [2, 3])
         evac(1)
         root(1)
         mm1(3, range(NQ))
@@ -320,13 +331,14 @@ def tile_doradirectiongradienttoloradown_w4_kernel(tc, x_bytes, x_scale, g, v, m
         direction(2)
         quant_g(3, 0)
         direction(3)
-        quant_g(3, 1)
         evac(5)
-        mm1(6, range(NQ))
+        mm1(6, [0, 1])
+        fold(4)
+        quant_g(3, 1)
+        mm1(6, [2, 3])
         turn_v(6)
         mm1(7, range(NQ))
         turn_v(7)
-        fold(4)
         fold(5)
         ileave_d(0, 0, on_s)
         ileave_d(0, 1, on_s)
@@ -342,27 +354,27 @@ def tile_doradirectiongradienttoloradown_w4_kernel(tc, x_bytes, x_scale, g, v, m
         mm2(quarter[1], 0, 5)
         direction(6)
         fold(7)
+        direction(7, slice(0, 1))
+        ileave_d(1, 0, on_s)
+        direction(7, slice(1, 4))
+        ileave_d(1, 1, on_s)
         quant_d(0, slice(512, 1024))
         mm2(quarter[2], 0, 6)
         mm2(eighth[6], 0, 7)
         mm2(eighth[7], 0, 2)
-        direction(7, slice(0, 2))
-        ileave_d(1, 1, on_s)
-        direction(7, slice(2, 4))
-        ileave_d(1, 3, on_s)
-        ileave_d(1, 0, on_v)
         ileave_d(1, 2, on_v)
         quant_d(1, quarter[0])
         mm2(quarter[0], 1)
-        quant_d(1, quarter[1])
-        mm2(quarter[1], 1)
+        ileave_d(1, 3, on_v)
+        store(quarter[0], on_s)
         quant_d(1, quarter[2])
         mm2(quarter[2], 1)
+        quant_d(1, quarter[1])
+        mm2(quarter[1], 1)
         quant_d(1, quarter[3])
         mm2(eighth[6], 1)
         mm2(eighth[7], 1)
-        store(quarter[0], on_s)
-        store(quarter[1], on_v)
         store(quarter[2], on_s)
-        store(eighth[6], on_v)
+        store(quarter[1], on_v)
+        store(eighth[6], on_s)
         store(eighth[7], on_v)

@@ -79,8 +79,7 @@ def tile_doradirectiongradienttoloradown_w4_kernel(tc, x_bytes, x_scale, g, v, m
             nc.sync.dma_start(out=vr[s][h][:], in_=v4[s][:, :, HALF * h : HALF * (h + 1)])
 
         nc.scalar.dma_start(out=xs[:], in_=x_scale.rearrange("(q p j) o -> p q (j o)", p=P, j=4))
-        load_x(0, slice(0, 1))
-        load_x(0, slice(1, 2))
+        load_x(0, slice(0, 2))
         load_x(0, slice(2, 4))
         load_x(1, slice(0, 2))
         load_x(1, slice(2, 4))
@@ -154,9 +153,10 @@ def tile_doradirectiongradienttoloradown_w4_kernel(tc, x_bytes, x_scale, g, v, m
 
         grams = {}
 
-        def gram(h):
-            grams[h] = bank(h, [P, 4, P], F32)
-            for n in range(8):
+        def gram(h, s):
+            if s == 0:
+                grams[h] = bank(h, [P, 4, P], F32)
+            for n in range(4 * s, 4 * s + 4):
                 for t in range(4):
                     nc.tensor.matmul(grams[h][:, t, :], lhsT=v_block(h, t, n), rhs=v_block(h, t, n), start=(n == 0 and t == 0), stop=(n == 7 and t == 3))
 
@@ -167,11 +167,13 @@ def tile_doradirectiongradienttoloradown_w4_kernel(tc, x_bytes, x_scale, g, v, m
 
         vt = {}
 
-        def turn_v(k):
+        def turn_v(k, sides=(0, 1)):
             h, t = divmod(k, 4)
-            vt[k] = bank((k + 2) % 4, [P, DI], BF16)
-            for n in range(8):
-                nc.tensor.transpose(vt[k][:, P * n : P * (n + 1)], v_block(h, t, n), ident[:])
+            for s in sides:
+                if s == 0:
+                    vt[k] = bank((k + 2) % 4, [P, DI], BF16)
+                for n in range(4 * s, 4 * s + 4):
+                    nc.tensor.transpose(vt[k][:, P * n : P * (n + 1)], v_block(h, t, n), ident[:])
 
         def inverse(h):
             nc.vector.reciprocal(r2[:, h, :], n2[:, h, :])
@@ -185,8 +187,8 @@ def tile_doradirectiongradienttoloradown_w4_kernel(tc, x_bytes, x_scale, g, v, m
         banks = {}
 
         def mm1(k, passes, sides=(0, 1)):
-            for s in sides:
-                for q in passes:
+            for q in passes:
+                for s in sides:
                     if q == 0:
                         banks[k, s] = bank(4 + 2 * (k % 2) + s, [P, HALF], F32)
                     nc.tensor.matmul_mx(
@@ -270,15 +272,16 @@ def tile_doradirectiongradienttoloradown_w4_kernel(tc, x_bytes, x_scale, g, v, m
         widen_s(2, range(4))
         ileave_x(1)
         quant_x(0)
-        gram(0)
-        turn_v(0)
-        turn_v(1)
-        gram(1)
+        for s in range(2):
+            gram(0, s)
+            turn_v(0, [s])
+            turn_v(1, [s])
+        gram(1, 0)
+        gram(1, 1)
         ileave_g(0, 0, on_v)
         quant_x(1)
         quant_g(0, 0)
         mm_pass(0)
-        mm_pass(1)
         planes(3)
         widen_s(3, range(4))
         ileave_x(2)
@@ -286,8 +289,11 @@ def tile_doradirectiongradienttoloradown_w4_kernel(tc, x_bytes, x_scale, g, v, m
         quant_x(2)
         inverse(0)
         turn_v(2)
-        ileave_g(0, 1, on_s)
+        mm_pass(1)
+        norms(1)
+        turn_v(3)
         ileave_g(1, 0, on_s)
+        ileave_g(0, 1, on_s)
         root(0)
         ileave_x(3)
         quant_g(0, 1)
@@ -295,14 +301,13 @@ def tile_doradirectiongradienttoloradown_w4_kernel(tc, x_bytes, x_scale, g, v, m
         quant_x(3)
         mm_pass(3)
         factor(0)
-        norms(1)
-        turn_v(3)
         ileave_g(1, 1, on_s)
         ileave_g(2, 0, on_s, slice(0, 1))
         quant_g(1, 0)
         inverse(1)
         ileave_g(2, 0, on_v, slice(1, 2))
         quant_g(1, 1)
+        quant_g(2, 0)
         evac(0)
         mm1(2, [0, 1])
         mm1(2, [2, 3])
@@ -311,15 +316,14 @@ def tile_doradirectiongradienttoloradown_w4_kernel(tc, x_bytes, x_scale, g, v, m
         mm1(3, range(NQ))
         ileave_g(2, 1, on_s)
         fold(0)
-        quant_g(2, 0)
-        direction(0)
         fold(1)
+        direction(0)
         quant_g(2, 1)
         evac(2)
         mm1(4, range(NQ))
         evac(3)
-        turn_v(4)
         direction(1)
+        turn_v(4)
         factor(1)
         mm1(5, range(NQ))
         turn_v(5)
@@ -339,42 +343,43 @@ def tile_doradirectiongradienttoloradown_w4_kernel(tc, x_bytes, x_scale, g, v, m
         turn_v(6)
         mm1(7, range(NQ))
         turn_v(7)
+        direction(4)
         fold(5)
         ileave_d(0, 0, on_s)
-        ileave_d(0, 1, on_s)
         evac(6)
+        ileave_d(0, 1, on_s)
         ileave_d(0, 2, on_s)
         evac(7)
         ileave_d(0, 3, on_s)
-        direction(4)
         direction(5)
         fold(6)
         quant_d(0, slice(0, 512))
-        mm2(quarter[0], 0, 4)
-        mm2(quarter[1], 0, 5)
         direction(6)
         fold(7)
-        direction(7, slice(0, 1))
-        ileave_d(1, 0, on_s)
-        direction(7, slice(1, 4))
-        ileave_d(1, 1, on_s)
         quant_d(0, slice(512, 1024))
         mm2(quarter[2], 0, 6)
-        mm2(eighth[6], 0, 7)
-        mm2(eighth[7], 0, 2)
-        ileave_d(1, 2, on_v)
+        mm2(eighth[6], 0, 2)
+        mm2(eighth[7], 0, 3)
+        mm2(quarter[0], 0, 4)
+        mm2(quarter[1], 0, 5)
+        direction(7, slice(0, 1))
+        direction(7, slice(1, 2))
+        ileave_d(1, 1, on_s)
+        ileave_d(1, 0, on_v)
+        direction(7, slice(2, 4))
+        ileave_d(1, 3, on_s)
         quant_d(1, quarter[0])
         mm2(quarter[0], 1)
-        ileave_d(1, 3, on_v)
+        ileave_d(1, 2, on_v)
+        quant_d(1, quarter[1])
+        mm2(quarter[1], 1)
         store(quarter[0], on_s)
         quant_d(1, quarter[2])
         mm2(quarter[2], 1)
-        quant_d(1, quarter[1])
-        mm2(quarter[1], 1)
         quant_d(1, quarter[3])
         mm2(eighth[6], 1)
         mm2(eighth[7], 1)
-        store(quarter[2], on_s)
         store(quarter[1], on_v)
-        store(eighth[6], on_s)
-        store(eighth[7], on_v)
+        store(quarter[2], on_s)
+        store(eighth[6], on_v)
+        store(eighth[7], on_s)

@@ -128,8 +128,8 @@ def tile_doradirectiongradienttoloradown_w4_kernel(tc, x_bytes, x_scale, g, v, m
             if cols.start == 0:
                 xi[q] = wt([P, 4 * DI], BF16, "xi", 2)
             nc.vector.tensor_copy(
-                out=xi[q][:, 4 * cols.start : 4 * cols.stop].rearrange("p (c i t) -> p c t i", i=4, t=4),
-                in_=xp[q][:, :, cols].rearrange("p t (c i) -> p c t i", i=4),
+                out=xi[q][:, 4 * cols.start : 4 * cols.stop].rearrange("p (c i t) -> p c t i", i=2, t=4),
+                in_=xp[q][:, :, cols].rearrange("p t (c i) -> p c t i", i=2),
             )
 
         def quant_x(q, cols=slice(0, DI)):
@@ -228,8 +228,8 @@ def tile_doradirectiongradienttoloradown_w4_kernel(tc, x_bytes, x_scale, g, v, m
 
         def ileave_d(h, c, copy):
             copy(
-                dvi[h][:, 4 * QUART * c : 4 * QUART * (c + 1)].rearrange("p (c i t) -> p c t i", i=4, t=4),
-                dvp[h][:, c, :, :].rearrange("p t (c i) -> p c t i", i=4),
+                dvi[h][:, 4 * QUART * c : 4 * QUART * (c + 1)].rearrange("p (c i t) -> p c t i", i=2, t=4),
+                dvp[h][:, c, :, :].rearrange("p t (c i) -> p c t i", i=2),
             )
 
         def quant_d(h, cols):

@@ -22,6 +22,9 @@ NQ = T // 512
 NG = DO // 512
 HALF = 512
 QUART = 256
+NT = DO // P
+G_SHARE = 192
+SPLIT = 224
 
 
 def tile_doradirectiongradienttoloradown_w4_kernel(tc, x_bytes, x_scale, g, v, m, b_words, b_scales, out):
@@ -46,7 +49,7 @@ def tile_doradirectiongradienttoloradown_w4_kernel(tc, x_bytes, x_scale, g, v, m
 
         xs = kt([P, NQ, 4], F32, "xs")
         xb = [kt([P, 4, DI], U8, f"xb{q}") for q in range(NQ)]
-        gr = [[kt([P, 2, 4, HALF], BF16, f"gr{w}_{h}") for h in range(NG)] for w in range(2)]
+        gr = [[kt([P, 4, 2, HALF], BF16, f"gr{w}_{h}") for h in range(NG)] for w in range(2)]
         vr = [[kt([P, 4, HALF], BF16, f"vr{s}_{h}") for h in range(NG)] for s in range(2)]
         xc = kt([P, NQ, DI], U32, "xc")
         xcs = kt([P, NQ, DI], U8, "xcs")
@@ -57,11 +60,12 @@ def tile_doradirectiongradienttoloradown_w4_kernel(tc, x_bytes, x_scale, g, v, m
         ww = kt([P, NG, 2 * R], U8, "ww")
         ws = kt([P, NG, R], U8, "ws")
         mt = kt([P, NG, 4], BF16, "mt")
-        n2 = kt([P, NG, 4], F32, "n2")
-        r2 = kt([P, NG, 4], F32, "r2")
-        rn = kt([P, NG, 4], F32, "rn")
-        nbeta = kt([P, NG, 4], F32, "nbeta")
-        gam = kt([P, NG, 4], F32, "gam")
+        negm = kt([P, NT], F32, "negm")
+        n2 = kt([P, NT], F32, "n2")
+        r2 = kt([P, NT], F32, "r2")
+        rn = kt([P, NT], F32, "rn")
+        nbeta = kt([P, NT], F32, "nbeta")
+        gam = kt([P, NT], F32, "gam")
         ident = kt([P, P], BF16, "ident")
         warm = kt([P, 1], F32, "warm")
 
@@ -73,7 +77,7 @@ def tile_doradirectiongradienttoloradown_w4_kernel(tc, x_bytes, x_scale, g, v, m
             nc.sync.dma_start(out=xb[q][:, rows, :], in_=x4[q][:, rows, :])
 
         def load_g(q, h):
-            nc.sync.dma_start(out=gr[q // 2][h][:, q % 2, :, :], in_=g4[q][:, :, HALF * h : HALF * (h + 1)])
+            nc.sync.dma_start(out=gr[q // 2][h][:, :, q % 2, :], in_=g4[q][:, :, HALF * h : HALF * (h + 1)])
 
         def load_v(s, h):
             nc.sync.dma_start(out=vr[s][h][:], in_=v4[s][:, :, HALF * h : HALF * (h + 1)])
@@ -81,24 +85,23 @@ def tile_doradirectiongradienttoloradown_w4_kernel(tc, x_bytes, x_scale, g, v, m
         nc.scalar.dma_start(out=xs[:], in_=x_scale.rearrange("(q p j) o -> p q (j o)", p=P, j=4))
         load_x(0, slice(0, 2))
         load_x(0, slice(2, 4))
-        load_x(1, slice(0, 2))
-        load_x(1, slice(2, 4))
-        load_v(0, 0)
-        load_x(2)
-        load_v(1, 0)
+        load_x(1)
         load_g(0, 0)
         load_g(1, 0)
+        load_x(2)
         load_x(3)
-        load_v(0, 1)
-        load_v(1, 1)
         load_g(2, 0)
         load_g(3, 0)
+        load_v(0, 0)
+        load_v(1, 0)
         nc.gpsimd.memset(warm[:], 1.0)
         make_identity(nc, ident[:])
         nc.gpsimd.memset(ws[:].rearrange("p g n -> p (g n)").bitcast(I32), 0)
         nc.sync.dma_start(out=mt[:], in_=m.rearrange("(h p t) -> p h t", p=P, t=4))
         for q in range(NQ):
             load_g(q, 1)
+        load_v(0, 1)
+        load_v(1, 1)
         nc.sync.dma_start(out=ww[:].rearrange("p g n -> p (g n)").bitcast(I32).rearrange("p (g n) -> p g n", g=NG),
                           in_=b_words.bitcast(I32).rearrange("g p n -> p g n"))
         ws32 = ws[:].rearrange("p g n -> p (g n)").bitcast(I32).rearrange("p (g n) -> p g n", g=NG)
@@ -107,82 +110,91 @@ def tile_doradirectiongradienttoloradown_w4_kernel(tc, x_bytes, x_scale, g, v, m
             nc.sync.dma_start(out=ws32[32 * quad : 32 * quad + 4, :, :],
                               in_=bs32[:, 4 * quad : 4 * quad + 4, :].rearrange("g q n -> q g n"))
 
-        nc.scalar.activation(warm[:], warm[:], ACT.Sqrt)
+        nc.scalar.activation(warm[:], warm[:], ACT.Abs_reciprocal_sqrt)
 
         xp = {}
         xi = {}
         gi = {}
+        staged = {}
+
+        def on_g(out, in_):
+            nc.gpsimd.tensor_scalar(out=out, in0=in_, scalar1=1.0, scalar2=0.0, op0=ALU.mult, op1=ALU.add)
+
+        on_v, on_s = nc.vector.tensor_copy, nc.scalar.copy
 
         def planes(q):
             xp[q] = wt([P, 4, DI], BF16, "xp", 3)
 
-        def widen_s(q, rows):
-            for j in rows:
-                nc.scalar.activation(xp[q][:, j, :], xb[q][:, j, :].bitcast(FP8), ACT.Copy, scale=xs[:, q, j : j + 1])
+        def widen_s(q, j):
+            nc.scalar.activation(xp[q][:, j, :], xb[q][:, j, :].bitcast(FP8), ACT.Copy, scale=xs[:, q, j : j + 1])
 
-        def widen_v(q, rows):
-            for j in rows:
-                nc.vector.tensor_scalar(out=xp[q][:, j, :], in0=xb[q][:, j, :].bitcast(FP8), scalar1=xs[:, q, j : j + 1], scalar2=None, op0=ALU.mult)
+        def widen_v(q, j):
+            nc.vector.tensor_scalar(out=xp[q][:, j, :], in0=xb[q][:, j, :].bitcast(FP8), scalar1=xs[:, q, j : j + 1], scalar2=None, op0=ALU.mult)
 
-        def ileave_x(q, cols=slice(0, DI)):
-            if cols.start == 0:
-                xi[q] = wt([P, 4 * DI], BF16, "xi", 2)
+        def open_xi(q):
+            xi[q] = wt([P, 4 * DI], BF16, "xi", 2)
+
+        def stage_x(q, c, b):
+            staged[q, c] = bank(b, [P, 4 * QUART], BF16)
+            for a in range(2):
+                cols = slice(QUART * c + P * a, QUART * c + P * (a + 1))
+                nc.tensor.matmul(staged[q, c][:, HALF * a : HALF * (a + 1)], lhsT=ident[:], rhs=xp[q][:, :, cols].rearrange("p t c -> p c t"), start=True, stop=True)
+
+        def unstage_x(q, c):
+            nc.scalar.copy(xi[q][:, 4 * QUART * c : 4 * QUART * (c + 1)], staged[q, c][:])
+
+        def ileave_x(q, s):
+            cols = slice(HALF * s, HALF * (s + 1))
             nc.vector.tensor_copy(
                 out=xi[q][:, 4 * cols.start : 4 * cols.stop].rearrange("p (c i t) -> p c t i", i=2, t=4),
                 in_=xp[q][:, :, cols].rearrange("p t (c i) -> p c t i", i=2),
             )
 
-        def quant_x(q, cols=slice(0, DI)):
+        def quant_x(q, s):
+            cols = slice(HALF * s, HALF * (s + 1))
             nc.vector.quantize_mx(out=xc[:, q, cols].bitcast(E4M3X4), scales=xcs[:, q, cols], in_=xi[q][:, 4 * cols.start : 4 * cols.stop])
 
-        def ileave_g(pair, w, copy, qs=slice(0, 2)):
+        unit = [kt([P, DI], F32, f"unit{a}") for a in range(6)]
+        for n, a in enumerate([0, 1, 2, 2, 5, 1, 5, 3, 5, 1]):
+            gi[n] = unit[a][:].bitcast(BF16)
+
+        def ileave_g(n, copy, part=slice(0, 2 * P)):
+            pair, w = divmod(n, 2)
             h, u = divmod(pair, 2)
-            if qs.start == 0:
-                gi[pair, w] = wt([P, 4 * HALF], BF16, "gi", 4)
             copy(
-                gi[pair, w][:].rearrange("p (e q m j) -> p q m j e", e=2, q=2, j=4)[:, qs],
-                gr[w][h][:].rearrange("p q j (m u e) -> p u q m j e", u=2, e=2)[:, u, qs],
+                gi[n].rearrange("p (e n j) -> p n j e", e=2, j=4)[:, part],
+                gr[w][h][:].rearrange("p j q c -> p j (q c)").rearrange("p j (n u e) -> p u n j e", u=2, e=2)[:, u, part],
             )
 
-        def quant_g(pair, w):
+        def quant_g(n):
+            pair, w = divmod(n, 2)
             nc.vector.quantize_mx(out=gc[:, pair, w].rearrange("p e q m -> p (e q m)").bitcast(E4M3X4),
-                                  scales=gcs[:, pair, w].rearrange("p e q m -> p (e q m)"), in_=gi[pair, w][:])
+                                  scales=gcs[:, pair, w].rearrange("p e q m -> p (e q m)"), in_=gi[n])
 
         def v_block(h, t, n):
             return vr[n // 4][h][:, n % 4, t : HALF : 4]
 
-        grams = {}
-
-        def gram(h, s):
-            if s == 0:
-                grams[h] = bank(h, [P, 4, P], F32)
-            for n in range(4 * s, 4 * s + 4):
-                for t in range(4):
-                    nc.tensor.matmul(grams[h][:, t, :], lhsT=v_block(h, t, n), rhs=v_block(h, t, n), start=(n == 0 and t == 0), stop=(n == 7 and t == 3))
-
-        def norms(h):
-            for t in range(4):
-                dump = wt([P, P], F32, "norm_dump", 4)
-                nc.vector.scalar_tensor_tensor(out=dump[:], in0=grams[h][:, t, :], scalar=1.0, in1=ident[:], op0=ALU.mult, op1=ALU.mult, accum_out=n2[:, h, t : t + 1])
-
         vt = {}
 
-        def turn_v(k, sides=(0, 1)):
+        def turn_v(k):
             h, t = divmod(k, 4)
-            for s in sides:
-                if s == 0:
-                    vt[k] = bank((k + 2) % 4, [P, DI], BF16)
-                for n in range(4 * s, 4 * s + 4):
-                    nc.tensor.transpose(vt[k][:, P * n : P * (n + 1)], v_block(h, t, n), ident[:])
+            vt[k] = bank(k % 4, [P, DI], BF16)
+            for n in range(8):
+                nc.tensor.transpose(vt[k][:, P * n : P * (n + 1)], v_block(h, t, n), ident[:])
 
-        def inverse(h):
-            nc.vector.reciprocal(r2[:, h, :], n2[:, h, :])
+        def squares(k):
+            dump = wt([P, DI], BF16, "square_dump", 2)
+            nc.scalar.activation(dump[:], vt[k][:], ACT.Square, accum_out=n2[:, k : k + 1])
 
-        def root(h):
-            nc.scalar.activation(rn[:, h, :], r2[:, h, :], ACT.Sqrt)
+        def root(pair):
+            two = slice(2 * pair, 2 * pair + 2)
+            nc.scalar.activation(rn[:, two], n2[:, two], ACT.Abs_reciprocal_sqrt)
 
-        def factor(h):
-            nc.vector.scalar_tensor_tensor(out=nbeta[:, h, :], in0=rn[:, h, :], scalar=-1.0, in1=mt[:, h, :], op0=ALU.mult, op1=ALU.mult)
+        def factors(pair):
+            two = slice(2 * pair, 2 * pair + 2)
+            for k in range(two.start, two.stop):
+                nc.scalar.activation(nbeta[:, k : k + 1], negm[:, k : k + 1], ACT.Copy, scale=rn[:, k : k + 1])
+            nc.scalar.activation(r2[:, two], rn[:, two], ACT.Square)
 
         banks = {}
 
@@ -198,188 +210,212 @@ def tile_doradirectiongradienttoloradown_w4_kernel(tc, x_bytes, x_scale, g, v, m
                         start=(q == 0), stop=(q == NQ - 1),
                     )
 
-        def mm_pass(q, sides=(0, 1)):
-            for k in range(2):
-                mm1(k, [q], sides)
-
         gs = {}
-        dvp = {}
-        dvi = [kt([P, 4 * DI], BF16, f"dvi{h}") for h in range(NG)]
+        dv0 = kt([P, 2, 4, HALF], BF16, "dv0")
+        dv1 = kt([P, 4, 4, QUART], BF16, "dv1")
+        di1 = kt([P, 4 * DI], BF16, "di1")
 
         def evac(k, sides=(0, 1)):
-            h, t = divmod(k, 4)
+            gs[k] = unit[k % 4]
             for s in sides:
-                if s == 0:
-                    gs[k] = wt([P, DI], F32, "gs", 4)
-                nc.scalar.activation(gs[k][:, HALF * s : HALF * (s + 1)], banks[k, s][:], ACT.Copy, scale=nbeta[:, h, t : t + 1])
+                nc.scalar.activation(gs[k][:, HALF * s : HALF * (s + 1)], banks[k, s][:], ACT.Copy, scale=nbeta[:, k : k + 1])
 
         def fold(k):
-            h, t = divmod(k, 4)
-            dump = wt([P, DI], F32, "xi", 2)
-            nc.vector.scalar_tensor_tensor(out=dump[:], in0=gs[k][:], scalar=r2[:, h, t : t + 1], in1=vt[k][:], op0=ALU.mult, op1=ALU.mult, accum_out=gam[:, h, t : t + 1])
+            dump = unit[4 + k % 2]
+            nc.vector.scalar_tensor_tensor(out=dump[:], in0=gs[k][:], scalar=r2[:, k : k + 1], in1=vt[k][:], op0=ALU.mult, op1=ALU.mult, accum_out=gam[:, k : k + 1])
 
         def direction(k, chunks=slice(0, 4)):
             h, t = divmod(k, 4)
-            if t == 0:
-                dvp[h] = wt([P, 4, 4, QUART], BF16, "dvp", 2)
+            width = QUART if h else HALF
             nc.vector.scalar_tensor_tensor(
-                out=dvp[h][:, chunks, t, :], in0=vt[k][:].rearrange("p (c i) -> p c i", i=QUART)[:, chunks, :], scalar=gam[:, h, t : t + 1],
-                in1=gs[k][:].rearrange("p (c i) -> p c i", i=QUART)[:, chunks, :], op0=ALU.mult, op1=ALU.subtract)
+                out=(dv1 if h else dv0)[:, chunks, t, :], in0=vt[k][:].rearrange("p (c i) -> p c i", i=width)[:, chunks, :], scalar=gam[:, k : k + 1],
+                in1=gs[k][:].rearrange("p (c i) -> p c i", i=width)[:, chunks, :], op0=ALU.mult, op1=ALU.subtract)
 
-        def ileave_d(h, c, copy):
+        def ileave_d0(s, copy, part):
             copy(
-                dvi[h][:, 4 * QUART * c : 4 * QUART * (c + 1)].rearrange("p (c i t) -> p c t i", i=2, t=4),
-                dvp[h][:, c, :, :].rearrange("p t (c i) -> p c t i", i=2),
+                gi[8 + s].rearrange("p (c i t) -> p c t i", i=2, t=4)[:, part],
+                dv0[:, s, :, :].rearrange("p t (c i) -> p c t i", i=2)[:, part],
             )
 
-        def quant_d(h, cols):
-            nc.vector.quantize_mx(out=dc[:, h, cols].bitcast(E4M3X4), scales=dcs[:, h, cols], in_=dvi[h][:, 4 * cols.start : 4 * cols.stop])
+        def ileave_d1(c, copy):
+            copy(
+                di1[:, 4 * QUART * c : 4 * QUART * (c + 1)].rearrange("p (c i t) -> p c t i", i=2, t=4),
+                dv1[:, c, :, :].rearrange("p t (c i) -> p c t i", i=2),
+            )
+
+        def quant_d0(s):
+            cols = slice(HALF * s, HALF * (s + 1))
+            nc.vector.quantize_mx(out=dc[:, 0, cols].bitcast(E4M3X4), scales=dcs[:, 0, cols], in_=gi[8 + s])
+
+        def quant_d1(c):
+            cols = slice(QUART * c, QUART * (c + 1))
+            nc.vector.quantize_mx(out=dc[:, 1, cols].bitcast(E4M3X4), scales=dcs[:, 1, cols], in_=di1[:, 4 * cols.start : 4 * cols.stop])
 
         outs = {}
 
-        def mm2(cols, h, b=None):
-            blocks = (cols.stop - cols.start) // P
+        def mm2(c, h, b=None):
             if h == 0:
-                outs[cols.start] = bank(b, [P, HALF], F32)
-            for a in range(blocks):
-                rows = slice(cols.start + P * a, cols.start + P * (a + 1))
-                for r0 in range(0, R, P):
-                    nc.tensor.matmul_mx(
-                        outs[cols.start][:, R * a + r0 : R * a + r0 + P],
-                        lhsT=dc[:, h, rows].bitcast(E4M3X4), lhsT_scale=dcs[:, h, rows],
-                        rhs=ww[:, h, 2 * r0 : 2 * (r0 + P)].bitcast(E2M1X4), rhs_scale=ws[:, h, r0 : r0 + P],
-                        start=(h == 0 and a == 0 and r0 == 0), stop=(h == NG - 1 and a == blocks - 1 and r0 == R - P),
-                    )
+                outs[c] = bank(b, [P, HALF], F32)
+            for a in range(2):
+                rows = slice(QUART * c + P * a, QUART * c + P * (a + 1))
+                nc.tensor.matmul_mx(
+                    outs[c][:, R * a : R * (a + 1)],
+                    lhsT=dc[:, h, rows].bitcast(E4M3X4), lhsT_scale=dcs[:, h, rows],
+                    rhs=ww[:, h, :].bitcast(E2M1X4), rhs_scale=ws[:, h, :],
+                    start=(h == 0 and a == 0), stop=(h == NG - 1 and a == 1),
+                )
 
-        def store(cols, copy):
-            blocks = (cols.stop - cols.start) // P
-            res = kt([P, blocks * R], F32, f"res{cols.start}")
-            copy(res[:], outs[cols.start][:, 0 : blocks * R])
-            nc.sync.dma_start(out=out[cols, :].rearrange("(a p) r -> p a r", p=P), in_=res[:].rearrange("p (a r) -> p a r", r=R))
+        def store(c, copy):
+            res = kt([P, 2 * R], F32, f"res{c}")
+            copy(res[:], outs[c][:])
+            nc.sync.dma_start(out=out[QUART * c : QUART * (c + 1), :].rearrange("(a p) r -> p a r", p=P), in_=res[:].rearrange("p (a r) -> p a r", r=R))
 
-        on_v, on_s = nc.vector.tensor_copy, nc.scalar.copy
-
-        quarter = [slice(256 * c, 256 * (c + 1)) for c in range(4)]
-        eighth = [slice(128 * c, 128 * (c + 1)) for c in range(8)]
         planes(0)
         planes(1)
-        widen_s(0, [0, 3])
-        widen_v(0, [1, 2])
-        widen_v(1, [0, 1])
-        widen_s(1, [2, 3])
-        ileave_x(0)
+        widen_v(0, 0)
+        widen_v(0, 1)
+        widen_s(0, 2)
+        widen_v(0, 3)
+        widen_s(1, 0)
+        widen_v(1, 1)
+        widen_v(1, 2)
+        widen_v(1, 3)
+        open_xi(0)
+        for c in range(4):
+            stage_x(0, c, c)
+        ileave_g(0, on_v)
         planes(2)
-        widen_s(2, range(4))
-        ileave_x(1)
-        quant_x(0)
-        for s in range(2):
-            gram(0, s)
-            turn_v(0, [s])
-            turn_v(1, [s])
-        gram(1, 0)
-        gram(1, 1)
-        ileave_g(0, 0, on_v)
-        quant_x(1)
-        quant_g(0, 0)
-        mm_pass(0)
+        unstage_x(0, 0)
+        unstage_x(0, 1)
+        widen_v(2, 0)
+        unstage_x(0, 2)
+        unstage_x(0, 3)
+        open_xi(1)
+        for c in range(4):
+            stage_x(1, c, c)
+        quant_x(0, 0)
+        quant_g(0)
+        quant_x(0, 1)
+        widen_s(2, 1)
+        widen_v(2, 2)
+        widen_v(2, 3)
+        unstage_x(1, 0)
+        unstage_x(1, 1)
+        unstage_x(1, 2)
+        unstage_x(1, 3)
+        ileave_g(1, on_v)
+        mm1(0, [0])
+        mm1(1, [0])
         planes(3)
-        widen_s(3, range(4))
-        ileave_x(2)
-        norms(0)
-        quant_x(2)
-        inverse(0)
+        widen_s(3, 0)
+        quant_x(1, 0)
+        quant_x(1, 1)
+        open_xi(2)
+        for c in range(4):
+            stage_x(2, c, c)
+        mm1(0, [1])
+        widen_v(3, 1)
+        unstage_x(2, 0)
+        unstage_x(2, 1)
+        widen_v(3, 2)
+        quant_g(1)
+        widen_s(3, 3)
+        turn_v(0)
+        turn_v(1)
+        unstage_x(2, 2)
+        unstage_x(2, 3)
+        quant_x(2, 0)
+        open_xi(3)
+        stage_x(3, 0, 2)
+        stage_x(3, 1, 3)
+        mm1(1, [1])
+        ileave_x(3, 1)
+        quant_x(2, 1)
+        mm1(0, [2])
+        mm1(1, [2])
+        nc.scalar.activation(negm[:], mt[:].rearrange("p h t -> p (h t)"), ACT.Copy, scale=-1.0)
+        squares(0)
+        unstage_x(3, 0)
+        unstage_x(3, 1)
+        squares(1)
+        quant_x(3, 1)
+        quant_x(3, 0)
         turn_v(2)
-        mm_pass(1)
-        norms(1)
+        mm1(0, [3], (1, 0))
+        mm1(1, [3])
         turn_v(3)
-        ileave_g(1, 0, on_s)
-        ileave_g(0, 1, on_s)
         root(0)
-        ileave_x(3)
-        quant_g(0, 1)
-        mm_pass(2)
-        quant_x(3)
-        mm_pass(3)
-        factor(0)
-        ileave_g(1, 1, on_s)
-        ileave_g(2, 0, on_s, slice(0, 1))
-        quant_g(1, 0)
-        inverse(1)
-        ileave_g(2, 0, on_v, slice(1, 2))
-        quant_g(1, 1)
-        quant_g(2, 0)
-        evac(0)
-        mm1(2, [0, 1])
-        mm1(2, [2, 3])
-        evac(1)
-        root(1)
-        mm1(3, range(NQ))
-        ileave_g(2, 1, on_s)
-        fold(0)
-        fold(1)
-        direction(0)
-        quant_g(2, 1)
-        evac(2)
-        mm1(4, range(NQ))
-        evac(3)
-        direction(1)
-        turn_v(4)
-        factor(1)
-        mm1(5, range(NQ))
-        turn_v(5)
-        ileave_g(3, 0, on_s)
-        evac(4)
-        ileave_g(3, 1, on_s)
-        fold(2)
-        fold(3)
-        direction(2)
-        quant_g(3, 0)
-        direction(3)
-        evac(5)
-        mm1(6, [0, 1])
-        fold(4)
-        quant_g(3, 1)
-        mm1(6, [2, 3])
-        turn_v(6)
-        mm1(7, range(NQ))
-        turn_v(7)
-        direction(4)
-        fold(5)
-        ileave_d(0, 0, on_s)
-        evac(6)
-        ileave_d(0, 1, on_s)
-        ileave_d(0, 2, on_s)
-        evac(7)
-        ileave_d(0, 3, on_s)
-        direction(5)
-        fold(6)
-        quant_d(0, slice(0, 512))
-        direction(6)
-        fold(7)
-        quant_d(0, slice(512, 1024))
-        mm2(quarter[2], 0, 6)
-        mm2(eighth[6], 0, 2)
-        mm2(eighth[7], 0, 3)
-        mm2(quarter[0], 0, 4)
-        mm2(quarter[1], 0, 5)
-        direction(7, slice(0, 1))
-        direction(7, slice(1, 2))
-        ileave_d(1, 1, on_s)
-        ileave_d(1, 0, on_v)
-        direction(7, slice(2, 4))
-        ileave_d(1, 3, on_s)
-        quant_d(1, quarter[0])
-        mm2(quarter[0], 1)
-        ileave_d(1, 2, on_v)
-        quant_d(1, quarter[1])
-        mm2(quarter[1], 1)
-        store(quarter[0], on_s)
-        quant_d(1, quarter[2])
-        mm2(quarter[2], 1)
-        quant_d(1, quarter[3])
-        mm2(eighth[6], 1)
-        mm2(eighth[7], 1)
-        store(quarter[1], on_v)
-        store(quarter[2], on_s)
-        store(eighth[6], on_v)
-        store(eighth[7], on_s)
+        factors(0)
+        ileave_g(2, on_v)
+        evac(0, (1, 0))
+        quant_g(2)
+
+        def share(n, copy, part):
+            if n < 8:
+                ileave_g(n, copy, part)
+            else:
+                ileave_d0(n - 8, copy, part)
+
+        def quant(n):
+            if n < 8:
+                quant_g(n)
+            else:
+                quant_d0(n - 8)
+
+        mine, rest = slice(0, G_SHARE), slice(G_SHARE, 2 * P)
+        for pair in range(4):
+            a, b = 2 * pair, 2 * pair + 1
+            n = 2 * pair + 3
+            share(n, on_g, mine)
+            evac(b)
+            if pair < 3:
+                mm1(a + 2, [0, 1])
+                mm1(b + 2, [0, 1])
+            share(n, on_s, rest)
+            fold(a)
+            fold(b)
+            if pair < 3:
+                squares(a + 2)
+            quant(n)
+            if pair == 3:
+                break
+            mm1(a + 2, [2, 3])
+            mm1(b + 2, [2, 3])
+            share(n + 1, on_g, mine)
+            squares(b + 2)
+            share(n + 1, on_s, slice(G_SHARE, SPLIT))
+            root(pair + 1)
+            share(n + 1, on_s, slice(SPLIT, 2 * P))
+            factors(pair + 1)
+            direction(a, slice(0, 4 if a >= 4 else 2))
+            direction(b, slice(0, 4 if a >= 4 else 2))
+            evac(a + 2)
+            quant(n + 1)
+            if pair < 2:
+                turn_v(a + 4)
+                turn_v(b + 4)
+            else:
+                mm2(0, 0, 0)
+                mm2(1, 0, 1)
+        mm2(2, 0, 4)
+        mm2(3, 0, 5)
+        for c in range(4):
+            direction(6, slice(c, c + 1))
+            direction(7, slice(c, c + 1))
+            if c == 0:
+                ileave_d1(0, on_g)
+            elif c < 3:
+                ileave_d1(c, on_s)
+        quant_d1(0)
+        mm2(0, 1)
+        ileave_d1(3, on_v)
+        quant_d1(1)
+        mm2(1, 1)
+        quant_d1(3)
+        mm2(3, 1)
+        store(0, on_s)
+        quant_d1(2)
+        mm2(2, 1)
+        store(1, on_s)
+        store(3, on_v)
+        store(2, on_s)

@@ -23,8 +23,6 @@ NG = DO // 512
 HALF = 512
 QUART = 256
 NT = DO // P
-G_SHARE = 192
-SPLIT = 224
 
 
 def tile_doradirectiongradienttoloradown_w4_kernel(tc, x_bytes, x_scale, g, v, m, b_words, b_scales, out):
@@ -49,18 +47,17 @@ def tile_doradirectiongradienttoloradown_w4_kernel(tc, x_bytes, x_scale, g, v, m
 
         xs = kt([P, NQ, 4], F32, "xs")
         xb = [kt([P, 4, DI], U8, f"xb{q}") for q in range(NQ)]
-        gr = [[kt([P, 4, 2, HALF], BF16, f"gr{w}_{h}") for h in range(NG)] for w in range(2)]
+        gr = [[kt([P, 4, HALF], BF16, f"gr{q}_{h}") for h in range(NG)] for q in range(NQ)]
         vr = [[kt([P, 4, HALF], BF16, f"vr{s}_{h}") for h in range(NG)] for s in range(2)]
         xc = kt([P, NQ, DI], U32, "xc")
         xcs = kt([P, NQ, DI], U8, "xcs")
-        gc = kt([P, 4, 2, 2, 2, P], U32, "gc")
-        gcs = kt([P, 4, 2, 2, 2, P], U8, "gcs")
+        gc = kt([P, 4, NQ, 2, P], U32, "gc")
+        gcs = kt([P, 4, NQ, 2, P], U8, "gcs")
         dc = kt([P, NG, DI], U32, "dc")
         dcs = kt([P, NG, DI], U8, "dcs")
         ww = kt([P, NG, 2 * R], U8, "ww")
         ws = kt([P, NG, R], U8, "ws")
         mt = kt([P, NG, 4], BF16, "mt")
-        negm = kt([P, NT], F32, "negm")
         n2 = kt([P, NT], F32, "n2")
         r2 = kt([P, NT], F32, "r2")
         rn = kt([P, NT], F32, "rn")
@@ -77,7 +74,7 @@ def tile_doradirectiongradienttoloradown_w4_kernel(tc, x_bytes, x_scale, g, v, m
             nc.sync.dma_start(out=xb[q][:, rows, :], in_=x4[q][:, rows, :])
 
         def load_g(q, h):
-            nc.sync.dma_start(out=gr[q // 2][h][:, :, q % 2, :], in_=g4[q][:, :, HALF * h : HALF * (h + 1)])
+            nc.sync.dma_start(out=gr[q][h][:], in_=g4[q][:, :, HALF * h : HALF * (h + 1)])
 
         def load_v(s, h):
             nc.sync.dma_start(out=vr[s][h][:], in_=v4[s][:, :, HALF * h : HALF * (h + 1)])
@@ -85,23 +82,24 @@ def tile_doradirectiongradienttoloradown_w4_kernel(tc, x_bytes, x_scale, g, v, m
         nc.scalar.dma_start(out=xs[:], in_=x_scale.rearrange("(q p j) o -> p q (j o)", p=P, j=4))
         load_x(0, slice(0, 2))
         load_x(0, slice(2, 4))
-        load_x(1)
+        load_x(1, slice(0, 2))
+        load_x(1, slice(2, 4))
+        load_v(0, 0)
+        load_x(2)
+        load_v(1, 0)
         load_g(0, 0)
         load_g(1, 0)
-        load_x(2)
         load_x(3)
+        load_v(0, 1)
+        load_v(1, 1)
         load_g(2, 0)
         load_g(3, 0)
-        load_v(0, 0)
-        load_v(1, 0)
         nc.gpsimd.memset(warm[:], 1.0)
         make_identity(nc, ident[:])
         nc.gpsimd.memset(ws[:].rearrange("p g n -> p (g n)").bitcast(I32), 0)
         nc.sync.dma_start(out=mt[:], in_=m.rearrange("(h p t) -> p h t", p=P, t=4))
         for q in range(NQ):
             load_g(q, 1)
-        load_v(0, 1)
-        load_v(1, 1)
         nc.sync.dma_start(out=ww[:].rearrange("p g n -> p (g n)").bitcast(I32).rearrange("p (g n) -> p g n", g=NG),
                           in_=b_words.bitcast(I32).rearrange("g p n -> p g n"))
         ws32 = ws[:].rearrange("p g n -> p (g n)").bitcast(I32).rearrange("p (g n) -> p g n", g=NG)
@@ -115,7 +113,6 @@ def tile_doradirectiongradienttoloradown_w4_kernel(tc, x_bytes, x_scale, g, v, m
         xp = {}
         xi = {}
         gi = {}
-        staged = {}
 
         def on_g(out, in_):
             nc.gpsimd.tensor_scalar(out=out, in0=in_, scalar1=1.0, scalar2=0.0, op0=ALU.mult, op1=ALU.add)
@@ -134,15 +131,6 @@ def tile_doradirectiongradienttoloradown_w4_kernel(tc, x_bytes, x_scale, g, v, m
         def open_xi(q):
             xi[q] = wt([P, 4 * DI], BF16, "xi", 2)
 
-        def stage_x(q, c, b):
-            staged[q, c] = bank(b, [P, 4 * QUART], BF16)
-            for a in range(2):
-                cols = slice(QUART * c + P * a, QUART * c + P * (a + 1))
-                nc.tensor.matmul(staged[q, c][:, HALF * a : HALF * (a + 1)], lhsT=ident[:], rhs=xp[q][:, :, cols].rearrange("p t c -> p c t"), start=True, stop=True)
-
-        def unstage_x(q, c):
-            nc.scalar.copy(xi[q][:, 4 * QUART * c : 4 * QUART * (c + 1)], staged[q, c][:])
-
         def ileave_x(q, s):
             cols = slice(HALF * s, HALF * (s + 1))
             nc.vector.tensor_copy(
@@ -154,22 +142,23 @@ def tile_doradirectiongradienttoloradown_w4_kernel(tc, x_bytes, x_scale, g, v, m
             cols = slice(HALF * s, HALF * (s + 1))
             nc.vector.quantize_mx(out=xc[:, q, cols].bitcast(E4M3X4), scales=xcs[:, q, cols], in_=xi[q][:, 4 * cols.start : 4 * cols.stop])
 
-        unit = [kt([P, DI], F32, f"unit{a}") for a in range(6)]
-        for n, a in enumerate([0, 1, 2, 2, 5, 1, 5, 3, 5, 1]):
-            gi[n] = unit[a][:].bitcast(BF16)
+        relay = kt([P, DI], BF16, "relay")
 
-        def ileave_g(n, copy, part=slice(0, 2 * P)):
-            pair, w = divmod(n, 2)
+        def g_rows(pair, q):
             h, u = divmod(pair, 2)
-            copy(
-                gi[n].rearrange("p (e n j) -> p n j e", e=2, j=4)[:, part],
-                gr[w][h][:].rearrange("p j q c -> p j (q c)").rearrange("p j (n u e) -> p u n j e", u=2, e=2)[:, u, part],
-            )
+            return gr[q][h][:].rearrange("p j (m u e) -> p u m j e", u=2, e=2)[:, u]
 
-        def quant_g(n):
-            pair, w = divmod(n, 2)
-            nc.vector.quantize_mx(out=gc[:, pair, w].rearrange("p e q m -> p (e q m)").bitcast(E4M3X4),
-                                  scales=gcs[:, pair, w].rearrange("p e q m -> p (e q m)"), in_=gi[n])
+        def ileave_g(pair, q, copy):
+            gi[pair, q] = wt([P, DI], BF16, "gi", 4)
+            copy(gi[pair, q][:].rearrange("p (e m j) -> p m j e", e=2, j=4), g_rows(pair, q))
+
+        def relay_g(pair, q):
+            gi[pair, q] = relay
+            on_g(relay[:].rearrange("p (e m j) -> p e m j", e=2, j=4), g_rows(pair, q).rearrange("p m j e -> p e m j"))
+
+        def quant_g(pair, q):
+            nc.vector.quantize_mx(out=gc[:, pair, q].rearrange("p e m -> p (e m)").bitcast(E4M3X4),
+                                  scales=gcs[:, pair, q].rearrange("p e m -> p (e m)"), in_=gi[pair, q][:])
 
         def v_block(h, t, n):
             return vr[n // 4][h][:, n % 4, t : HALF : 4]
@@ -182,19 +171,28 @@ def tile_doradirectiongradienttoloradown_w4_kernel(tc, x_bytes, x_scale, g, v, m
             for n in range(8):
                 nc.tensor.transpose(vt[k][:, P * n : P * (n + 1)], v_block(h, t, n), ident[:])
 
-        def squares(k):
-            dump = wt([P, DI], BF16, "square_dump", 2)
-            nc.scalar.activation(dump[:], vt[k][:], ACT.Square, accum_out=n2[:, k : k + 1])
+        grams = {}
 
-        def root(pair):
-            two = slice(2 * pair, 2 * pair + 2)
-            nc.scalar.activation(rn[:, two], n2[:, two], ACT.Abs_reciprocal_sqrt)
+        def gram(h, s):
+            if s == 0:
+                grams[h] = bank(2 + h, [P, 4, P], F32)
+            for n in range(4 * s, 4 * s + 4):
+                for t in range(4):
+                    nc.tensor.matmul(grams[h][:, t, :], lhsT=v_block(h, t, n), rhs=v_block(h, t, n), start=(n == 0 and t == 0), stop=(n == 7 and t == 3))
 
-        def factors(pair):
-            two = slice(2 * pair, 2 * pair + 2)
-            for k in range(two.start, two.stop):
-                nc.scalar.activation(nbeta[:, k : k + 1], negm[:, k : k + 1], ACT.Copy, scale=rn[:, k : k + 1])
-            nc.scalar.activation(r2[:, two], rn[:, two], ACT.Square)
+        def norms(h):
+            for t in range(4):
+                dump = wt([P, P], F32, "norm_dump", 4)
+                nc.vector.scalar_tensor_tensor(out=dump[:], in0=grams[h][:, t, :], scalar=1.0, in1=ident[:], op0=ALU.mult, op1=ALU.mult, accum_out=n2[:, 4 * h + t : 4 * h + t + 1])
+
+        def root(h):
+            four = slice(4 * h, 4 * h + 4)
+            nc.scalar.activation(rn[:, four], n2[:, four], ACT.Abs_reciprocal_sqrt)
+
+        def factors(h):
+            four = slice(4 * h, 4 * h + 4)
+            nc.vector.scalar_tensor_tensor(out=nbeta[:, four], in0=rn[:, four], scalar=-1.0, in1=mt[:, h, :], op0=ALU.mult, op1=ALU.mult)
+            nc.scalar.activation(r2[:, four], rn[:, four], ACT.Square)
 
         banks = {}
 
@@ -205,51 +203,41 @@ def tile_doradirectiongradienttoloradown_w4_kernel(tc, x_bytes, x_scale, g, v, m
                         banks[k, s] = bank(4 + 2 * (k % 2) + s, [P, HALF], F32)
                     nc.tensor.matmul_mx(
                         banks[k, s][:],
-                        lhsT=gc[:, k // 2, q // 2, k % 2, q % 2, :].bitcast(E4M3X4), lhsT_scale=gcs[:, k // 2, q // 2, k % 2, q % 2, :],
+                        lhsT=gc[:, k // 2, q, k % 2, :].bitcast(E4M3X4), lhsT_scale=gcs[:, k // 2, q, k % 2, :],
                         rhs=xc[:, q, HALF * s : HALF * (s + 1)].bitcast(E4M3X4), rhs_scale=xcs[:, q, HALF * s : HALF * (s + 1)],
                         start=(q == 0), stop=(q == NQ - 1),
                     )
 
         gs = {}
-        dv0 = kt([P, 2, 4, HALF], BF16, "dv0")
-        dv1 = kt([P, 4, 4, QUART], BF16, "dv1")
-        di1 = kt([P, 4 * DI], BF16, "di1")
+        dv = [kt([P, 4, 4, QUART], BF16, f"dv{h}") for h in range(NG)]
+        di = {}
 
         def evac(k, sides=(0, 1)):
-            gs[k] = unit[k % 4]
+            gs[k] = wt([P, DI], F32, "gs", 4)
             for s in sides:
                 nc.scalar.activation(gs[k][:, HALF * s : HALF * (s + 1)], banks[k, s][:], ACT.Copy, scale=nbeta[:, k : k + 1])
 
         def fold(k):
-            dump = unit[4 + k % 2]
+            dump = wt([P, DI], F32, "xi", 2)
             nc.vector.scalar_tensor_tensor(out=dump[:], in0=gs[k][:], scalar=r2[:, k : k + 1], in1=vt[k][:], op0=ALU.mult, op1=ALU.mult, accum_out=gam[:, k : k + 1])
 
         def direction(k, chunks=slice(0, 4)):
             h, t = divmod(k, 4)
-            width = QUART if h else HALF
             nc.vector.scalar_tensor_tensor(
-                out=(dv1 if h else dv0)[:, chunks, t, :], in0=vt[k][:].rearrange("p (c i) -> p c i", i=width)[:, chunks, :], scalar=gam[:, k : k + 1],
-                in1=gs[k][:].rearrange("p (c i) -> p c i", i=width)[:, chunks, :], op0=ALU.mult, op1=ALU.subtract)
+                out=dv[h][:, chunks, t, :], in0=vt[k][:].rearrange("p (c i) -> p c i", i=QUART)[:, chunks, :], scalar=gam[:, k : k + 1],
+                in1=gs[k][:].rearrange("p (c i) -> p c i", i=QUART)[:, chunks, :], op0=ALU.mult, op1=ALU.subtract)
 
-        def ileave_d0(s, copy, part):
-            copy(
-                gi[8 + s].rearrange("p (c i t) -> p c t i", i=2, t=4)[:, part],
-                dv0[:, s, :, :].rearrange("p t (c i) -> p c t i", i=2)[:, part],
-            )
+        def ileave_d(h, c, copy):
+            di[h, c] = wt([P, DI], BF16, "gi", 4)
+            copy(di[h, c][:].rearrange("p (c i t) -> p c t i", i=2, t=4), dv[h][:, c, :, :].rearrange("p t (c i) -> p c t i", i=2))
 
-        def ileave_d1(c, copy):
-            copy(
-                di1[:, 4 * QUART * c : 4 * QUART * (c + 1)].rearrange("p (c i t) -> p c t i", i=2, t=4),
-                dv1[:, c, :, :].rearrange("p t (c i) -> p c t i", i=2),
-            )
+        def relay_d(h, c):
+            di[h, c] = relay
+            on_g(relay[:].rearrange("p (c t) -> p c t", t=4), dv[h][:, c, :, :].rearrange("p t c -> p c t"))
 
-        def quant_d0(s):
-            cols = slice(HALF * s, HALF * (s + 1))
-            nc.vector.quantize_mx(out=dc[:, 0, cols].bitcast(E4M3X4), scales=dcs[:, 0, cols], in_=gi[8 + s])
-
-        def quant_d1(c):
+        def quant_d(h, c):
             cols = slice(QUART * c, QUART * (c + 1))
-            nc.vector.quantize_mx(out=dc[:, 1, cols].bitcast(E4M3X4), scales=dcs[:, 1, cols], in_=di1[:, 4 * cols.start : 4 * cols.stop])
+            nc.vector.quantize_mx(out=dc[:, h, cols].bitcast(E4M3X4), scales=dcs[:, h, cols], in_=di[h, c][:])
 
         outs = {}
 
@@ -272,129 +260,116 @@ def tile_doradirectiongradienttoloradown_w4_kernel(tc, x_bytes, x_scale, g, v, m
 
         planes(0)
         planes(1)
-        widen_v(0, 0)
+        widen_s(0, 0)
+        widen_s(0, 3)
         widen_v(0, 1)
-        widen_s(0, 2)
-        widen_v(0, 3)
-        widen_s(1, 0)
+        widen_v(0, 2)
+        widen_v(1, 0)
         widen_v(1, 1)
-        widen_v(1, 2)
-        widen_v(1, 3)
+        widen_s(1, 2)
+        widen_s(1, 3)
         open_xi(0)
-        for c in range(4):
-            stage_x(0, c, c)
-        ileave_g(0, on_v)
+        ileave_x(0, 0)
+        ileave_x(0, 1)
         planes(2)
-        unstage_x(0, 0)
-        unstage_x(0, 1)
-        widen_v(2, 0)
-        unstage_x(0, 2)
-        unstage_x(0, 3)
+        for j in range(4):
+            widen_s(2, j)
         open_xi(1)
-        for c in range(4):
-            stage_x(1, c, c)
+        ileave_x(1, 0)
+        ileave_x(1, 1)
         quant_x(0, 0)
-        quant_g(0)
         quant_x(0, 1)
-        widen_s(2, 1)
-        widen_v(2, 2)
-        widen_v(2, 3)
-        unstage_x(1, 0)
-        unstage_x(1, 1)
-        unstage_x(1, 2)
-        unstage_x(1, 3)
-        ileave_g(1, on_v)
-        mm1(0, [0])
-        mm1(1, [0])
-        planes(3)
-        widen_s(3, 0)
-        quant_x(1, 0)
-        quant_x(1, 1)
-        open_xi(2)
-        for c in range(4):
-            stage_x(2, c, c)
-        mm1(0, [1])
-        widen_v(3, 1)
-        unstage_x(2, 0)
-        unstage_x(2, 1)
-        widen_v(3, 2)
-        quant_g(1)
-        widen_s(3, 3)
+        for s in range(2):
+            gram(0, s)
         turn_v(0)
         turn_v(1)
-        unstage_x(2, 2)
-        unstage_x(2, 3)
+        gram(1, 0)
+        gram(1, 1)
+        ileave_g(0, 0, on_s)
+        quant_x(1, 0)
+        quant_x(1, 1)
+        planes(3)
+        for j in range(4):
+            widen_s(3, j)
+        open_xi(2)
+        ileave_x(2, 0)
+        norms(0)
+        ileave_x(2, 1)
+        quant_g(0, 0)
+        mm1(0, [0])
+        mm1(1, [0])
+        turn_v(2)
         quant_x(2, 0)
-        open_xi(3)
-        stage_x(3, 0, 2)
-        stage_x(3, 1, 3)
-        mm1(1, [1])
-        ileave_x(3, 1)
         quant_x(2, 1)
+        root(0)
+        ileave_g(0, 1, on_s)
+        open_xi(3)
+        ileave_x(3, 0)
+        factors(0)
+        quant_g(0, 1)
+        mm1(0, [1])
+        mm1(1, [1])
+        ileave_g(0, 2, on_s)
+        ileave_x(3, 1)
+        ileave_g(0, 3, on_s)
+        quant_g(0, 2)
         mm1(0, [2])
         mm1(1, [2])
-        nc.scalar.activation(negm[:], mt[:].rearrange("p h t -> p (h t)"), ACT.Copy, scale=-1.0)
-        squares(0)
-        unstage_x(3, 0)
-        unstage_x(3, 1)
-        squares(1)
-        quant_x(3, 1)
         quant_x(3, 0)
-        turn_v(2)
-        mm1(0, [3], (1, 0))
+        quant_g(0, 3)
+        quant_x(3, 1)
+        mm1(0, [3])
         mm1(1, [3])
+        ileave_g(1, 0, on_s)
+        gi[1, 1] = relay
+        on_v(relay[:].rearrange("p (e m j) -> p m j e", e=2, j=4), g_rows(1, 1))
+        norms(1)
         turn_v(3)
-        root(0)
-        factors(0)
-        ileave_g(2, on_v)
-        evac(0, (1, 0))
-        quant_g(2)
+        quant_g(1, 0)
+        quant_g(1, 1)
+        evac(0)
+        root(1)
 
-        def share(n, copy, part):
-            if n < 8:
-                ileave_g(n, copy, part)
-            else:
-                ileave_d0(n - 8, copy, part)
-
-        def quant(n):
-            if n < 8:
-                quant_g(n)
-            else:
-                quant_d0(n - 8)
-
-        mine, rest = slice(0, G_SHARE), slice(G_SHARE, 2 * P)
         for pair in range(4):
             a, b = 2 * pair, 2 * pair + 1
-            n = 2 * pair + 3
-            share(n, on_g, mine)
             evac(b)
             if pair < 3:
                 mm1(a + 2, [0, 1])
                 mm1(b + 2, [0, 1])
-            share(n, on_s, rest)
+                relay_g(pair + 1, 3)
+                ileave_g(pair + 1, 2, on_s)
+            else:
+                relay_d(0, 3)
+                ileave_d(0, 2, on_s)
             fold(a)
             fold(b)
-            if pair < 3:
-                squares(a + 2)
-            quant(n)
             if pair == 3:
+                quant_d(0, 2)
+                quant_d(0, 3)
                 break
+            if pair == 0:
+                factors(1)
+            quant_g(pair + 1, 2)
+            quant_g(pair + 1, 3)
             mm1(a + 2, [2, 3])
             mm1(b + 2, [2, 3])
-            share(n + 1, on_g, mine)
-            squares(b + 2)
-            share(n + 1, on_s, slice(G_SHARE, SPLIT))
-            root(pair + 1)
-            share(n + 1, on_s, slice(SPLIT, 2 * P))
-            factors(pair + 1)
-            direction(a, slice(0, 4 if a >= 4 else 2))
-            direction(b, slice(0, 4 if a >= 4 else 2))
-            evac(a + 2)
-            quant(n + 1)
             if pair < 2:
+                relay_g(pair + 2, 1)
+                ileave_g(pair + 2, 0, on_s)
+            else:
+                relay_d(0, 1)
+                ileave_d(0, 0, on_s)
+            direction(a)
+            direction(b)
+            evac(a + 2)
+            if pair < 2:
+                quant_g(pair + 2, 0)
+                quant_g(pair + 2, 1)
                 turn_v(a + 4)
                 turn_v(b + 4)
             else:
+                quant_d(0, 0)
+                quant_d(0, 1)
                 mm2(0, 0, 0)
                 mm2(1, 0, 1)
         mm2(2, 0, 4)
@@ -403,18 +378,18 @@ def tile_doradirectiongradienttoloradown_w4_kernel(tc, x_bytes, x_scale, g, v, m
             direction(6, slice(c, c + 1))
             direction(7, slice(c, c + 1))
             if c == 0:
-                ileave_d1(0, on_g)
+                relay_d(1, 0)
             elif c < 3:
-                ileave_d1(c, on_s)
-        quant_d1(0)
+                ileave_d(1, c, on_s)
+        quant_d(1, 0)
         mm2(0, 1)
-        ileave_d1(3, on_v)
-        quant_d1(1)
+        ileave_d(1, 3, on_v)
+        quant_d(1, 1)
         mm2(1, 1)
-        quant_d1(3)
+        quant_d(1, 3)
         mm2(3, 1)
         store(0, on_s)
-        quant_d1(2)
+        quant_d(1, 2)
         mm2(2, 1)
         store(1, on_s)
         store(3, on_v)

@@ -169,7 +169,7 @@ def tile_doradirectiongradienttoloradown_w4_kernel(tc, x_bytes, x_scale, g, v, m
             h, t = divmod(k, 4)
             vt[k] = bank(k % 4, [P, DI], BF16)
             for n in range(8):
-                nc.tensor.transpose(vt[k][:, P * n : P * (n + 1)], v_block(h, t, n), ident[:])
+                nc.tensor.matmul(vt[k][:, P * n : P * (n + 1)], lhsT=v_block(h, t, n), rhs=ident[:], start=True, stop=True, is_transpose=k < 2)
 
         grams = {}
 
@@ -323,72 +323,64 @@ def tile_doradirectiongradienttoloradown_w4_kernel(tc, x_bytes, x_scale, g, v, m
         ileave_g(1, 0, on_s)
         gi[1, 1] = relay
         on_v(relay[:].rearrange("p (e m j) -> p m j e", e=2, j=4), g_rows(1, 1))
-        norms(1)
-        turn_v(3)
         quant_g(1, 0)
         quant_g(1, 1)
         evac(0)
-        root(1)
 
-        for pair in range(4):
-            a, b = 2 * pair, 2 * pair + 1
-            evac(b)
-            if pair < 3:
-                mm1(a + 2, [0, 1])
-                mm1(b + 2, [0, 1])
-                relay_g(pair + 1, 3)
-                ileave_g(pair + 1, 2, on_s)
+        for k in range(NT):
+            pair, q = divmod(2 * k + 6, NQ)
+            if k < 5:
+                relay_g(pair, q + 1)
+                ileave_g(pair, q, on_s)
+            elif k < 7:
+                relay_d(0, q + 1)
+                ileave_d(0, q, on_s)
+            if k + 1 < NT:
+                evac(k + 1)
+            if k == 0:
+                mm1(2, [0, 1])
+                norms(1)
+                root(1)
             else:
-                relay_d(0, 3)
-                ileave_d(0, 2, on_s)
-            fold(a)
-            fold(b)
-            if pair == 3:
-                quant_d(0, 2)
-                quant_d(0, 3)
-                break
-            if pair == 0:
+                direction(k - 1)
+            fold(k)
+            if k == 1:
                 factors(1)
-            quant_g(pair + 1, 2)
-            quant_g(pair + 1, 3)
-            mm1(a + 2, [2, 3])
-            mm1(b + 2, [2, 3])
-            if pair < 2:
-                relay_g(pair + 2, 1)
-                ileave_g(pair + 2, 0, on_s)
-            else:
-                relay_d(0, 1)
-                ileave_d(0, 0, on_s)
-            direction(a)
-            direction(b)
-            evac(a + 2)
-            if pair < 2:
-                quant_g(pair + 2, 0)
-                quant_g(pair + 2, 1)
-                turn_v(a + 4)
-                turn_v(b + 4)
-            else:
+            if k < 5:
+                quant_g(pair, q)
+                quant_g(pair, q + 1)
+            elif k == 5:
                 quant_d(0, 0)
                 quant_d(0, 1)
-                mm2(0, 0, 0)
-                mm2(1, 0, 1)
-        mm2(2, 0, 4)
-        mm2(3, 0, 5)
-        for c in range(4):
-            direction(6, slice(c, c + 1))
-            direction(7, slice(c, c + 1))
-            if c == 0:
-                relay_d(1, 0)
-            elif c < 3:
-                ileave_d(1, c, on_s)
+            else:
+                quant_d(0, k - 4)
+            if k == 0:
+                turn_v(3)
+                mm1(2, [2, 3])
+                mm1(3, range(NQ))
+            elif k in (1, 3):
+                turn_v(k + 3)
+                mm1(k + 3, [0, 1])
+            elif k in (2, 4):
+                mm1(k + 2, [2, 3])
+                turn_v(k + 3)
+                mm1(k + 3, range(NQ))
+        for c, b in ((3, 1), (0, 0), (1, 4), (2, 5)):
+            mm2(c, 0, b)
+        direction(7, slice(0, 1))
+        ileave_d(1, 0, on_s)
+        direction(7, slice(1, 2))
+        direction(7, slice(2, 4))
+        ileave_d(1, 2, on_s)
+        ileave_d(1, 1, on_v)
         quant_d(1, 0)
         mm2(0, 1)
         ileave_d(1, 3, on_v)
         quant_d(1, 1)
         mm2(1, 1)
+        store(0, on_s)
         quant_d(1, 3)
         mm2(3, 1)
-        store(0, on_s)
         quant_d(1, 2)
         mm2(2, 1)
         store(1, on_s)

@@ -23,6 +23,7 @@ NG = DO // 512
 HALF = 512
 QUART = 256
 NT = DO // P
+TRANSPOSED = (3, 4)
 
 
 def tile_doradirectiongradienttoloradown_w4_kernel(tc, x_bytes, x_scale, g, v, m, b_words, b_scales, out):
@@ -164,21 +165,25 @@ def tile_doradirectiongradienttoloradown_w4_kernel(tc, x_bytes, x_scale, g, v, m
             return vr[n // 4][h][:, n % 4, t : HALF : 4]
 
         vt = {}
-
-        def turn_v(k):
-            h, t = divmod(k, 4)
-            vt[k] = bank(k % 4, [P, DI], BF16)
-            for n in range(8):
-                nc.tensor.matmul(vt[k][:, P * n : P * (n + 1)], lhsT=v_block(h, t, n), rhs=ident[:], start=True, stop=True, is_transpose=k < 2)
-
         grams = {}
 
-        def gram(h, s):
-            if s == 0:
-                grams[h] = bank(2 + h, [P, 4, P], F32)
-            for n in range(4 * s, 4 * s + 4):
+        def turn_block(k, n):
+            h, t = divmod(k, 4)
+            if n == 0:
+                vt[k] = bank(k % 4, [P, DI], BF16)
+            nc.tensor.matmul(vt[k][:, P * n : P * (n + 1)], lhsT=v_block(h, t, n), rhs=ident[:], start=True, stop=True, is_transpose=k in TRANSPOSED)
+
+        def turn_v(k):
+            for n in range(8):
+                turn_block(k, n)
+
+        def gram(h, b, turned=()):
+            grams[h] = bank(b, [P, 4, P], F32)
+            for n in range(8):
                 for t in range(4):
                     nc.tensor.matmul(grams[h][:, t, :], lhsT=v_block(h, t, n), rhs=v_block(h, t, n), start=(n == 0 and t == 0), stop=(n == 7 and t == 3))
+                    if 4 * h + t in turned:
+                        turn_block(4 * h + t, n)
 
         def norms(h):
             for t in range(4):
@@ -279,12 +284,8 @@ def tile_doradirectiongradienttoloradown_w4_kernel(tc, x_bytes, x_scale, g, v, m
         ileave_x(1, 1)
         quant_x(0, 0)
         quant_x(0, 1)
-        for s in range(2):
-            gram(0, s)
-        turn_v(0)
-        turn_v(1)
-        gram(1, 0)
-        gram(1, 1)
+        gram(0, 6, (0, 1, 2))
+        gram(1, 3)
         ileave_g(0, 0, on_s)
         quant_x(1, 0)
         quant_x(1, 1)
@@ -293,32 +294,33 @@ def tile_doradirectiongradienttoloradown_w4_kernel(tc, x_bytes, x_scale, g, v, m
             widen_s(3, j)
         open_xi(2)
         ileave_x(2, 0)
-        norms(0)
         ileave_x(2, 1)
         quant_g(0, 0)
+        quant_x(2, 0)
+        norms(0)
         mm1(0, [0])
         mm1(1, [0])
-        turn_v(2)
-        quant_x(2, 0)
         quant_x(2, 1)
-        root(0)
         ileave_g(0, 1, on_s)
+        root(0)
         open_xi(3)
         ileave_x(3, 0)
-        factors(0)
         quant_g(0, 1)
         mm1(0, [1])
         mm1(1, [1])
         ileave_g(0, 2, on_s)
         ileave_x(3, 1)
+        factors(0)
         ileave_g(0, 3, on_s)
         quant_g(0, 2)
         mm1(0, [2])
-        mm1(1, [2])
         quant_x(3, 0)
         quant_g(0, 3)
         quant_x(3, 1)
-        mm1(0, [3])
+        mm1(0, [3], (0,))
+        mm1(1, [2], (0,))
+        mm1(0, [3], (1,))
+        mm1(1, [2], (1,))
         mm1(1, [3])
         ileave_g(1, 0, on_s)
         gi[1, 1] = relay
@@ -365,7 +367,7 @@ def tile_doradirectiongradienttoloradown_w4_kernel(tc, x_bytes, x_scale, g, v, m
                 mm1(k + 2, [2, 3])
                 turn_v(k + 3)
                 mm1(k + 3, range(NQ))
-        for c, b in ((3, 1), (0, 0), (1, 4), (2, 5)):
+        for c, b in ((0, 2), (1, 0), (2, 4), (3, 5)):
             mm2(c, 0, b)
         direction(7, slice(0, 1))
         ileave_d(1, 0, on_s)
@@ -375,14 +377,14 @@ def tile_doradirectiongradienttoloradown_w4_kernel(tc, x_bytes, x_scale, g, v, m
         ileave_d(1, 1, on_v)
         quant_d(1, 0)
         mm2(0, 1)
-        ileave_d(1, 3, on_v)
         quant_d(1, 1)
         mm2(1, 1)
+        ileave_d(1, 3, on_v)
         store(0, on_s)
-        quant_d(1, 3)
-        mm2(3, 1)
         quant_d(1, 2)
         mm2(2, 1)
+        quant_d(1, 3)
+        mm2(3, 1)
         store(1, on_s)
-        store(3, on_v)
-        store(2, on_s)
+        store(2, on_v)
+        store(3, on_s)

@@ -23,7 +23,7 @@ NG = DO // 512
 HALF = 512
 QUART = 256
 NT = DO // P
-TRANSPOSED = (3, 4)
+TRANSPOSED = (2, 3, 4)
 
 
 def tile_doradirectiongradienttoloradown_w4_kernel(tc, x_bytes, x_scale, g, v, m, b_words, b_scales, out):
@@ -236,6 +236,11 @@ def tile_doradirectiongradienttoloradown_w4_kernel(tc, x_bytes, x_scale, g, v, m
             di[h, c] = wt([P, DI], BF16, "gi", 4)
             copy(di[h, c][:].rearrange("p (c i t) -> p c t i", i=2, t=4), dv[h][:, c, :, :].rearrange("p t (c i) -> p c t i", i=2))
 
+        def ileave_pair(c, u, copy):
+            if u == 0:
+                di[1, c] = kt([P, DI], BF16, f"di{c}")
+            copy(di[1, c][:].rearrange("p (c u e) -> p u c e", u=2, e=2)[:, u], dv[1][:, c, 2 * u : 2 * u + 2, :].rearrange("p e c -> p c e"))
+
         def relay_d(h, c):
             di[h, c] = relay
             on_g(relay[:].rearrange("p (c t) -> p c t", t=4), dv[h][:, c, :, :].rearrange("p t c -> p c t"))
@@ -337,7 +342,12 @@ def tile_doradirectiongradienttoloradown_w4_kernel(tc, x_bytes, x_scale, g, v, m
             elif k < 7:
                 relay_d(0, q + 1)
                 ileave_d(0, q, on_s)
-            if k + 1 < NT:
+            if k == 7:
+                ileave_pair(0, 0, on_s)
+                evac(7)
+                for c in range(1, 4):
+                    ileave_pair(c, 0, on_s)
+            elif k < 6:
                 evac(k + 1)
             if k == 0:
                 mm1(2, [0, 1])
@@ -370,21 +380,21 @@ def tile_doradirectiongradienttoloradown_w4_kernel(tc, x_bytes, x_scale, g, v, m
         for c, b in ((0, 2), (1, 0), (2, 4), (3, 5)):
             mm2(c, 0, b)
         direction(7, slice(0, 1))
-        ileave_d(1, 0, on_s)
         direction(7, slice(1, 2))
+        ileave_pair(1, 1, on_s)
+        ileave_pair(0, 1, on_v)
         direction(7, slice(2, 4))
-        ileave_d(1, 2, on_s)
-        ileave_d(1, 1, on_v)
+        ileave_pair(2, 1, on_s)
         quant_d(1, 0)
         mm2(0, 1)
+        ileave_pair(3, 1, on_v)
         quant_d(1, 1)
         mm2(1, 1)
-        ileave_d(1, 3, on_v)
+        quant_d(1, 3)
+        mm2(3, 1)
         store(0, on_s)
         quant_d(1, 2)
         mm2(2, 1)
-        quant_d(1, 3)
-        mm2(3, 1)
-        store(1, on_s)
-        store(2, on_v)
+        store(1, on_v)
         store(3, on_s)
+        store(2, on_v)

@@ -23,7 +23,7 @@ NG = DO // 512
 HALF = 512
 QUART = 256
 NT = DO // P
-TRANSPOSED = (2, 3, 4)
+TRANSPOSED = (2, 3)
 
 
 def tile_doradirectiongradienttoloradown_w4_kernel(tc, x_bytes, x_scale, g, v, m, b_words, b_scales, out):
@@ -46,7 +46,7 @@ def tile_doradirectiongradienttoloradown_w4_kernel(tc, x_bytes, x_scale, g, v, m
             t = psum.tile(shape, dtype, name=f"bank{b}", tag=f"bank{b}", bufs=1)
             return t
 
-        xs = kt([P, NQ, 4], F32, "xs")
+        xs = [kt([P, 4], F32, "xs_first"), kt([P, NQ - 1, 4], F32, "xs_rest")]
         xb = [kt([P, 4, DI], U8, f"xb{q}") for q in range(NQ)]
         gr = [[kt([P, 4, HALF], BF16, f"gr{q}_{h}") for h in range(NG)] for q in range(NQ)]
         vr = [[kt([P, 4, HALF], BF16, f"vr{s}_{h}") for h in range(NG)] for s in range(2)]
@@ -80,7 +80,9 @@ def tile_doradirectiongradienttoloradown_w4_kernel(tc, x_bytes, x_scale, g, v, m
         def load_v(s, h):
             nc.sync.dma_start(out=vr[s][h][:], in_=v4[s][:, :, HALF * h : HALF * (h + 1)])
 
-        nc.scalar.dma_start(out=xs[:], in_=x_scale.rearrange("(q p j) o -> p q (j o)", p=P, j=4))
+        s4 = x_scale.rearrange("(q p j) o -> p q (j o)", p=P, j=4)
+        nc.scalar.dma_start(out=xs[0][:], in_=s4[:, 0, :])
+        nc.scalar.dma_start(out=xs[1][:], in_=s4[:, 1:NQ, :])
         load_x(0, slice(0, 2))
         load_x(0, slice(2, 4))
         load_x(1, slice(0, 2))
@@ -120,27 +122,28 @@ def tile_doradirectiongradienttoloradown_w4_kernel(tc, x_bytes, x_scale, g, v, m
 
         on_v, on_s = nc.vector.tensor_copy, nc.scalar.copy
 
+        def scale(q, j):
+            return xs[0][:, j : j + 1] if q == 0 else xs[1][:, q - 1, j : j + 1]
+
         def planes(q):
             xp[q] = wt([P, 4, DI], BF16, "xp", 3)
 
         def widen_s(q, j):
-            nc.scalar.activation(xp[q][:, j, :], xb[q][:, j, :].bitcast(FP8), ACT.Copy, scale=xs[:, q, j : j + 1])
+            nc.scalar.activation(xp[q][:, j, :], xb[q][:, j, :].bitcast(FP8), ACT.Copy, scale=scale(q, j))
 
         def widen_v(q, j):
-            nc.vector.tensor_scalar(out=xp[q][:, j, :], in0=xb[q][:, j, :].bitcast(FP8), scalar1=xs[:, q, j : j + 1], scalar2=None, op0=ALU.mult)
+            nc.vector.tensor_scalar(out=xp[q][:, j, :], in0=xb[q][:, j, :].bitcast(FP8), scalar1=scale(q, j), scalar2=None, op0=ALU.mult)
 
         def open_xi(q):
             xi[q] = wt([P, 4 * DI], BF16, "xi", 2)
 
-        def ileave_x(q, s):
-            cols = slice(HALF * s, HALF * (s + 1))
+        def ileave_x(q, cols=slice(0, DI)):
             nc.vector.tensor_copy(
                 out=xi[q][:, 4 * cols.start : 4 * cols.stop].rearrange("p (c i t) -> p c t i", i=2, t=4),
                 in_=xp[q][:, :, cols].rearrange("p t (c i) -> p c t i", i=2),
             )
 
-        def quant_x(q, s):
-            cols = slice(HALF * s, HALF * (s + 1))
+        def quant_x(q, cols=slice(0, DI)):
             nc.vector.quantize_mx(out=xc[:, q, cols].bitcast(E4M3X4), scales=xcs[:, q, cols], in_=xi[q][:, 4 * cols.start : 4 * cols.stop])
 
         relay = kt([P, DI], BF16, "relay")
@@ -251,22 +254,22 @@ def tile_doradirectiongradienttoloradown_w4_kernel(tc, x_bytes, x_scale, g, v, m
 
         outs = {}
 
-        def mm2(c, h, b=None):
+        def mm2(n, h, b=None):
+            rows = slice(P * n, P * (n + 1))
             if h == 0:
-                outs[c] = bank(b, [P, HALF], F32)
-            for a in range(2):
-                rows = slice(QUART * c + P * a, QUART * c + P * (a + 1))
-                nc.tensor.matmul_mx(
-                    outs[c][:, R * a : R * (a + 1)],
-                    lhsT=dc[:, h, rows].bitcast(E4M3X4), lhsT_scale=dcs[:, h, rows],
-                    rhs=ww[:, h, :].bitcast(E2M1X4), rhs_scale=ws[:, h, :],
-                    start=(h == 0 and a == 0), stop=(h == NG - 1 and a == 1),
-                )
+                outs[n] = bank(b, [P, R], F32)
+            nc.tensor.matmul_mx(outs[n][:], lhsT=dc[:, h, rows].bitcast(E4M3X4), lhsT_scale=dcs[:, h, rows],
+                                rhs=ww[:, h, :].bitcast(E2M1X4), rhs_scale=ws[:, h, :], start=(h == 0), stop=(h == NG - 1))
 
-        def store(c, copy):
-            res = kt([P, 2 * R], F32, f"res{c}")
-            copy(res[:], outs[c][:])
-            nc.sync.dma_start(out=out[QUART * c : QUART * (c + 1), :].rearrange("(a p) r -> p a r", p=P), in_=res[:].rearrange("p (a r) -> p a r", r=R))
+        def finish(c):
+            quant_d(1, c)
+            mm2(2 * c, 1)
+            mm2(2 * c + 1, 1)
+
+        def store(n, copy):
+            res = kt([P, R], F32, f"res{n}")
+            copy(res[:], outs[n][:])
+            nc.sync.dma_start(out=out[P * n : P * (n + 1), :], in_=res[:])
 
         planes(0)
         planes(1)
@@ -279,49 +282,43 @@ def tile_doradirectiongradienttoloradown_w4_kernel(tc, x_bytes, x_scale, g, v, m
         widen_s(1, 2)
         widen_s(1, 3)
         open_xi(0)
-        ileave_x(0, 0)
-        ileave_x(0, 1)
+        ileave_x(0)
         planes(2)
         for j in range(4):
             widen_s(2, j)
         open_xi(1)
-        ileave_x(1, 0)
-        ileave_x(1, 1)
-        quant_x(0, 0)
-        quant_x(0, 1)
+        ileave_x(1)
+        quant_x(0)
         gram(0, 6, (0, 1, 2))
         gram(1, 3)
         ileave_g(0, 0, on_s)
-        quant_x(1, 0)
-        quant_x(1, 1)
+        quant_x(1)
         planes(3)
         for j in range(4):
             widen_s(3, j)
         open_xi(2)
-        ileave_x(2, 0)
-        ileave_x(2, 1)
+        ileave_x(2)
         quant_g(0, 0)
-        quant_x(2, 0)
         norms(0)
         mm1(0, [0])
         mm1(1, [0])
-        quant_x(2, 1)
+        quant_x(2)
         ileave_g(0, 1, on_s)
         root(0)
         open_xi(3)
-        ileave_x(3, 0)
+        ileave_x(3, slice(0, HALF))
         quant_g(0, 1)
         mm1(0, [1])
         mm1(1, [1])
         ileave_g(0, 2, on_s)
-        ileave_x(3, 1)
+        ileave_x(3, slice(HALF, DI))
         factors(0)
         ileave_g(0, 3, on_s)
         quant_g(0, 2)
         mm1(0, [2])
-        quant_x(3, 0)
+        quant_x(3, slice(0, HALF))
         quant_g(0, 3)
-        quant_x(3, 1)
+        quant_x(3, slice(HALF, DI))
         mm1(0, [3], (0,))
         mm1(1, [2], (0,))
         mm1(0, [3], (1,))
@@ -377,24 +374,22 @@ def tile_doradirectiongradienttoloradown_w4_kernel(tc, x_bytes, x_scale, g, v, m
                 mm1(k + 2, [2, 3])
                 turn_v(k + 3)
                 mm1(k + 3, range(NQ))
-        for c, b in ((0, 2), (1, 0), (2, 4), (3, 5)):
-            mm2(c, 0, b)
+        for n, b in ((0, 2), (1, 0), (2, 1), (3, 4), (4, 7), (6, 5), (7, 6)):
+            mm2(n, 0, b)
         direction(7, slice(0, 1))
         direction(7, slice(1, 2))
         ileave_pair(1, 1, on_s)
         ileave_pair(0, 1, on_v)
         direction(7, slice(2, 4))
+        mm2(5, 0, 3)
         ileave_pair(2, 1, on_s)
-        quant_d(1, 0)
-        mm2(0, 1)
+        finish(0)
         ileave_pair(3, 1, on_v)
-        quant_d(1, 1)
-        mm2(1, 1)
-        quant_d(1, 3)
-        mm2(3, 1)
+        finish(1)
+        finish(3)
         store(0, on_s)
-        quant_d(1, 2)
-        mm2(2, 1)
-        store(1, on_v)
-        store(3, on_s)
-        store(2, on_v)
+        store(1, on_s)
+        finish(2)
+        for n in (2, 6, 4):
+            store(n, on_s)
+            store(n + 1, on_v)

@@ -266,10 +266,16 @@ def tile_doradirectiongradienttoloradown_w4_kernel(tc, x_bytes, x_scale, g, v, m
             mm2(2 * c, 1)
             mm2(2 * c + 1, 1)
 
-        def store(n, copy):
-            res = kt([P, R], F32, f"res{n}")
-            copy(res[:], outs[n][:])
+        def store_block(n):
+            res = kt([P, R], F32, f"res_block{n}")
+            on_s(res[:], outs[n][:])
             nc.sync.dma_start(out=out[P * n : P * (n + 1), :], in_=res[:])
+
+        def store_chunk(c):
+            res = kt([P, 2, R], F32, f"res_chunk{c}")
+            on_s(res[:, 0, :], outs[2 * c][:])
+            on_v(res[:, 1, :], outs[2 * c + 1][:])
+            nc.sync.dma_start(out=out[QUART * c : QUART * (c + 1), :].rearrange("(a p) r -> p a r", p=P), in_=res[:])
 
         planes(0)
         planes(1)
@@ -373,7 +379,10 @@ def tile_doradirectiongradienttoloradown_w4_kernel(tc, x_bytes, x_scale, g, v, m
             elif k in (2, 4):
                 mm1(k + 2, [2, 3])
                 turn_v(k + 3)
-                mm1(k + 3, range(NQ))
+                mm1(k + 3, range(NQ) if k == 2 else [0, 1])
+                if k == 4:
+                    for s in range(2):
+                        mm1(7, [2, 3], (s,))
         for n, b in ((0, 2), (1, 0), (2, 1), (3, 4), (4, 7), (6, 5), (7, 6)):
             mm2(n, 0, b)
         direction(7, slice(0, 1))
@@ -387,9 +396,8 @@ def tile_doradirectiongradienttoloradown_w4_kernel(tc, x_bytes, x_scale, g, v, m
         ileave_pair(3, 1, on_v)
         finish(1)
         finish(3)
-        store(0, on_s)
-        store(1, on_s)
+        store_block(0)
+        store_block(1)
         finish(2)
-        for n in (2, 6, 4):
-            store(n, on_s)
-            store(n + 1, on_v)
+        for c in (1, 3, 2):
+            store_chunk(c)

@@ -23,7 +23,7 @@ NG = DO // 512
 HALF = 512
 QUART = 256
 NT = DO // P
-TRANSPOSED = (2, 3)
+TRANSPOSED = (1, 2)
 
 
 def tile_doradirectiongradienttoloradown_w4_kernel(tc, x_bytes, x_scale, g, v, m, b_words, b_scales, out):
@@ -295,7 +295,9 @@ def tile_doradirectiongradienttoloradown_w4_kernel(tc, x_bytes, x_scale, g, v, m
         open_xi(1)
         ileave_x(1)
         quant_x(0)
-        gram(0, 6, (0, 1, 2))
+        gram(0, 6, (0,))
+        turn_v(1)
+        turn_v(2)
         gram(1, 3)
         ileave_g(0, 0, on_s)
         quant_x(1)
@@ -344,7 +346,9 @@ def tile_doradirectiongradienttoloradown_w4_kernel(tc, x_bytes, x_scale, g, v, m
                 ileave_g(pair, q, on_s)
             elif k < 7:
                 relay_d(0, q + 1)
-                ileave_d(0, q, on_s)
+            if k == 5:
+                ileave_d(0, 0, on_s)
+                ileave_d(0, 2, on_s)
             if k == 7:
                 ileave_pair(0, 0, on_s)
                 evac(7)
@@ -373,16 +377,20 @@ def tile_doradirectiongradienttoloradown_w4_kernel(tc, x_bytes, x_scale, g, v, m
                 turn_v(3)
                 mm1(2, [2, 3])
                 mm1(3, range(NQ))
-            elif k in (1, 3):
-                turn_v(k + 3)
-                mm1(k + 3, [0, 1])
-            elif k in (2, 4):
-                mm1(k + 2, [2, 3])
-                turn_v(k + 3)
-                mm1(k + 3, range(NQ) if k == 2 else [0, 1])
-                if k == 4:
-                    for s in range(2):
-                        mm1(7, [2, 3], (s,))
+            elif k == 1:
+                mm1(4, [0, 1])
+                turn_v(4)
+            elif k == 2:
+                mm1(4, [2, 3])
+                mm1(5, range(NQ))
+                turn_v(5)
+            elif k == 3:
+                mm1(6, [0, 1])
+            elif k == 4:
+                mm1(6, [2, 3])
+                turn_v(6)
+                mm1(7, range(NQ))
+                turn_v(7)
         for n, b in ((0, 2), (1, 0), (2, 1), (3, 4), (4, 7), (6, 5), (7, 6)):
             mm2(n, 0, b)
         direction(7, slice(0, 1))

@@ -24,6 +24,7 @@ HALF = 512
 QUART = 256
 NT = DO // P
 TRANSPOSED = (1, 2)
+PACKED = 7
 
 
 def tile_doradirectiongradienttoloradown_w4_kernel(tc, x_bytes, x_scale, g, v, m, b_words, b_scales, out):
@@ -48,12 +49,16 @@ def tile_doradirectiongradienttoloradown_w4_kernel(tc, x_bytes, x_scale, g, v, m
 
         xs = [kt([P, 4], F32, "xs_first"), kt([P, NQ - 1, 4], F32, "xs_rest")]
         xb = [kt([P, 4, DI], U8, f"xb{q}") for q in range(NQ)]
-        gr = [[kt([P, 4, HALF], BF16, f"gr{q}_{h}") for h in range(NG)] for q in range(NQ)]
+        g_first = kt([P, 4, HALF], BF16, "g_first")
+        g_rest = kt([P, NQ - 1, 4, HALF], BF16, "g_rest")
+        g_second = kt([P, NQ, 4, HALF], BF16, "g_second")
         vr = [[kt([P, 4, HALF], BF16, f"vr{s}_{h}") for h in range(NG)] for s in range(2)]
         xc = kt([P, NQ, DI], U32, "xc")
         xcs = kt([P, NQ, DI], U8, "xcs")
-        gc = kt([P, 4, NQ, 2, P], U32, "gc")
-        gcs = kt([P, 4, NQ, 2, P], U8, "gcs")
+        gc = kt([P, NT, NQ, P], U32, "gc")
+        gcs = kt([P, NT, NQ, P], U8, "gcs")
+        pc = kt([P, NQ + 1, 2, P], U32, "pc")
+        pcs = kt([P, NQ + 1, 2, P], U8, "pcs")
         dc = kt([P, NG, DI], U32, "dc")
         dcs = kt([P, NG, DI], U8, "dcs")
         ww = kt([P, NG, 2 * R], U8, "ww")
@@ -74,8 +79,13 @@ def tile_doradirectiongradienttoloradown_w4_kernel(tc, x_bytes, x_scale, g, v, m
         def load_x(q, rows=slice(0, 4)):
             nc.sync.dma_start(out=xb[q][:, rows, :], in_=x4[q][:, rows, :])
 
+        def g_pass(q, h):
+            if h == 1:
+                return g_second[:, q]
+            return g_first[:] if q == 0 else g_rest[:, q - 1]
+
         def load_g(q, h):
-            nc.sync.dma_start(out=gr[q][h][:], in_=g4[q][:, :, HALF * h : HALF * (h + 1)])
+            nc.sync.dma_start(out=g_pass(q, h), in_=g4[q][:, :, HALF * h : HALF * (h + 1)])
 
         def load_v(s, h):
             nc.sync.dma_start(out=vr[s][h][:], in_=v4[s][:, :, HALF * h : HALF * (h + 1)])
@@ -146,26 +156,43 @@ def tile_doradirectiongradienttoloradown_w4_kernel(tc, x_bytes, x_scale, g, v, m
         def quant_x(q, cols=slice(0, DI)):
             nc.vector.quantize_mx(out=xc[:, q, cols].bitcast(E4M3X4), scales=xcs[:, q, cols], in_=xi[q][:, 4 * cols.start : 4 * cols.stop])
 
-        relay = kt([P, DI], BF16, "relay")
+        relay = kt([P, 3 * HALF], BF16, "relay")
 
-        def g_rows(pair, q):
-            h, u = divmod(pair, 2)
-            return gr[q][h][:].rearrange("p j (m u e) -> p u m j e", u=2, e=2)[:, u]
-
-        def ileave_g(pair, q, copy):
+        def ileave_g(pair, q):
             gi[pair, q] = wt([P, DI], BF16, "gi", 4)
-            copy(gi[pair, q][:].rearrange("p (e m j) -> p m j e", e=2, j=4), g_rows(pair, q))
-
-        def relay_g(pair, q):
-            gi[pair, q] = relay
-            on_g(relay[:].rearrange("p (e m j) -> p e m j", e=2, j=4), g_rows(pair, q).rearrange("p m j e -> p e m j"))
+            on_s(gi[pair, q][:].rearrange("p (e m j) -> p m j e", e=2, j=4), g_pass(q, 0).rearrange("p j (m u e) -> p u m j e", u=2, e=2)[:, pair])
 
         def quant_g(pair, q):
-            nc.vector.quantize_mx(out=gc[:, pair, q].rearrange("p e m -> p (e m)").bitcast(E4M3X4),
-                                  scales=gcs[:, pair, q].rearrange("p e m -> p (e m)"), in_=gi[pair, q][:])
+            slot = NQ * pair + q
+            nc.vector.quantize_mx(out=pc[:, slot].rearrange("p e m -> p (e m)").bitcast(E4M3X4),
+                                  scales=pcs[:, slot].rearrange("p e m -> p (e m)"), in_=gi[pair, q][:])
+
+        def ileave_t(k, lo, hi, copy):
+            h, t = divmod(k, 4)
+            rows = g_second[:, lo:hi] if h == 1 else g_rest[:, lo - 1 : hi - 1]
+            if copy is on_g:
+                gi[k, lo, hi] = relay[:, 0 : HALF * (hi - lo)]
+            else:
+                gi[k, lo, hi] = wt([P, HALF * (hi - lo)], BF16, "gi", 4)[:]
+            copy(gi[k, lo, hi].rearrange("p (q m j) -> p q m j", m=P, j=4), rows.rearrange("p q j (m t) -> p t q m j", t=4)[:, t])
+
+        def quant_t(k, lo, hi):
+            nc.vector.quantize_mx(out=gc[:, k, lo:hi].rearrange("p q m -> p (q m)").bitcast(E4M3X4),
+                                  scales=gcs[:, k, lo:hi].rearrange("p q m -> p (q m)"), in_=gi[k, lo, hi])
+
+        def g_codes(k, q):
+            if k < 2 or (k < 4 and q == 0):
+                slot = NQ * (k // 2) + q
+                return pc[:, slot, k % 2, :], pcs[:, slot, k % 2, :]
+            return gc[:, k, q, :], gcs[:, k, q, :]
 
         def v_block(h, t, n):
             return vr[n // 4][h][:, n % 4, t : HALF : 4]
+
+        vp = [kt([P, 4, P], BF16, f"vp{s}") for s in range(2)]
+
+        def pack_v(s):
+            on_s(vp[s][:], vr[s][1][:].rearrange("p n (m t) -> p t n m", t=4)[:, PACKED % 4])
 
         vt = {}
         grams = {}
@@ -174,7 +201,7 @@ def tile_doradirectiongradienttoloradown_w4_kernel(tc, x_bytes, x_scale, g, v, m
             h, t = divmod(k, 4)
             if n == 0:
                 vt[k] = bank(k % 4, [P, DI], BF16)
-            nc.tensor.matmul(vt[k][:, P * n : P * (n + 1)], lhsT=v_block(h, t, n), rhs=ident[:], start=True, stop=True, is_transpose=k in TRANSPOSED)
+            nc.tensor.matmul(vt[k][:, P * n : P * (n + 1)], lhsT=vp[n // 4][:, n % 4, :] if k == PACKED else v_block(h, t, n), rhs=ident[:], start=True, stop=True, is_transpose=k in TRANSPOSED)
 
         def turn_v(k):
             for n in range(8):
@@ -188,8 +215,8 @@ def tile_doradirectiongradienttoloradown_w4_kernel(tc, x_bytes, x_scale, g, v, m
                     if 4 * h + t in turned:
                         turn_block(4 * h + t, n)
 
-        def norms(h):
-            for t in range(4):
+        def norms(h, tiles=range(4)):
+            for t in tiles:
                 dump = wt([P, P], F32, "norm_dump", 4)
                 nc.vector.scalar_tensor_tensor(out=dump[:], in0=grams[h][:, t, :], scalar=1.0, in1=ident[:], op0=ALU.mult, op1=ALU.mult, accum_out=n2[:, 4 * h + t : 4 * h + t + 1])
 
@@ -211,7 +238,7 @@ def tile_doradirectiongradienttoloradown_w4_kernel(tc, x_bytes, x_scale, g, v, m
                         banks[k, s] = bank(4 + 2 * (k % 2) + s, [P, HALF], F32)
                     nc.tensor.matmul_mx(
                         banks[k, s][:],
-                        lhsT=gc[:, k // 2, q, k % 2, :].bitcast(E4M3X4), lhsT_scale=gcs[:, k // 2, q, k % 2, :],
+                        lhsT=g_codes(k, q)[0].bitcast(E4M3X4), lhsT_scale=g_codes(k, q)[1],
                         rhs=xc[:, q, HALF * s : HALF * (s + 1)].bitcast(E4M3X4), rhs_scale=xcs[:, q, HALF * s : HALF * (s + 1)],
                         start=(q == 0), stop=(q == NQ - 1),
                     )
@@ -245,8 +272,8 @@ def tile_doradirectiongradienttoloradown_w4_kernel(tc, x_bytes, x_scale, g, v, m
             copy(di[1, c][:].rearrange("p (c u e) -> p u c e", u=2, e=2)[:, u], dv[1][:, c, 2 * u : 2 * u + 2, :].rearrange("p e c -> p c e"))
 
         def relay_d(h, c):
-            di[h, c] = relay
-            on_g(relay[:].rearrange("p (c t) -> p c t", t=4), dv[h][:, c, :, :].rearrange("p t c -> p c t"))
+            di[h, c] = relay[:, 0:DI]
+            on_g(di[h, c].rearrange("p (c t) -> p c t", t=4), dv[h][:, c, :, :].rearrange("p t c -> p c t"))
 
         def quant_d(h, c):
             cols = slice(QUART * c, QUART * (c + 1))
@@ -299,7 +326,7 @@ def tile_doradirectiongradienttoloradown_w4_kernel(tc, x_bytes, x_scale, g, v, m
         turn_v(1)
         turn_v(2)
         gram(1, 3)
-        ileave_g(0, 0, on_s)
+        ileave_g(0, 0)
         quant_x(1)
         planes(3)
         for j in range(4):
@@ -311,17 +338,17 @@ def tile_doradirectiongradienttoloradown_w4_kernel(tc, x_bytes, x_scale, g, v, m
         mm1(0, [0])
         mm1(1, [0])
         quant_x(2)
-        ileave_g(0, 1, on_s)
+        ileave_g(0, 1)
         root(0)
         open_xi(3)
         ileave_x(3, slice(0, HALF))
         quant_g(0, 1)
         mm1(0, [1])
         mm1(1, [1])
-        ileave_g(0, 2, on_s)
+        ileave_g(0, 2)
         ileave_x(3, slice(HALF, DI))
         factors(0)
-        ileave_g(0, 3, on_s)
+        ileave_g(0, 3)
         quant_g(0, 2)
         mm1(0, [2])
         quant_x(3, slice(0, HALF))
@@ -332,23 +359,27 @@ def tile_doradirectiongradienttoloradown_w4_kernel(tc, x_bytes, x_scale, g, v, m
         mm1(0, [3], (1,))
         mm1(1, [2], (1,))
         mm1(1, [3])
-        ileave_g(1, 0, on_s)
-        gi[1, 1] = relay
-        on_v(relay[:].rearrange("p (e m j) -> p m j e", e=2, j=4), g_rows(1, 1))
+        gi[1, 0] = relay[:, 0:DI]
+        on_s(gi[1, 0].rearrange("p (e m j) -> p m j e", e=2, j=4), g_pass(0, 0).rearrange("p j (m u e) -> p u m j e", u=2, e=2)[:, 1])
+        norms(1, [0])
         quant_g(1, 0)
-        quant_g(1, 1)
         evac(0)
 
         for k in range(NT):
-            pair, q = divmod(2 * k + 6, NQ)
-            if k < 5:
-                relay_g(pair, q + 1)
-                ileave_g(pair, q, on_s)
-            elif k < 7:
-                relay_d(0, q + 1)
-            if k == 5:
-                ileave_d(0, 0, on_s)
-                ileave_d(0, 2, on_s)
+            if k == 0:
+                ileave_t(2, 1, 3, on_g)
+                ileave_t(2, 3, 4, on_s)
+                ileave_t(3, 1, 2, on_s)
+            elif k < 6:
+                ileave_t(k + 2, 2, 4, on_g)
+            else:
+                relay_d(0, 2 * k - 11)
+            if 1 <= k < 5:
+                ileave_t(k + 3, 0, 2, on_s)
+            if k in (3, 4):
+                pack_v(k - 3)
+            if k in (5, 6):
+                ileave_d(0, 2 * k - 10, on_s)
             if k == 7:
                 ileave_pair(0, 0, on_s)
                 evac(7)
@@ -357,40 +388,41 @@ def tile_doradirectiongradienttoloradown_w4_kernel(tc, x_bytes, x_scale, g, v, m
             elif k < 6:
                 evac(k + 1)
             if k == 0:
-                mm1(2, [0, 1])
-                norms(1)
+                mm1(2, [0])
+                norms(1, [1, 2, 3])
                 root(1)
             else:
                 direction(k - 1)
             fold(k)
             if k == 1:
                 factors(1)
-            if k < 5:
-                quant_g(pair, q)
-                quant_g(pair, q + 1)
+            if k == 0:
+                quant_t(2, 3, 4)
+                quant_t(3, 1, 2)
+                quant_t(2, 1, 3)
+                turn_v(3)
+                mm1(2, [1, 2, 3])
+                mm1(3, [0, 1])
+            elif k < 5:
+                quant_t(k + 3, 0, 2)
+                quant_t(k + 2, 2, 4)
+                mm1(k + 2, [2, 3])
+                if k > 2:
+                    turn_v(k + 2)
+                mm1(k + 3, [0, 1])
+                if k == 1:
+                    turn_v(4)
             elif k == 5:
                 quant_d(0, 0)
+                quant_t(7, 2, 4)
+                for s in range(2):
+                    mm1(7, [2, 3], (s,))
+                turn_v(7)
+            elif k == 6:
+                quant_d(0, 2)
                 quant_d(0, 1)
             else:
-                quant_d(0, k - 4)
-            if k == 0:
-                turn_v(3)
-                mm1(2, [2, 3])
-                mm1(3, range(NQ))
-            elif k == 1:
-                mm1(4, [0, 1])
-                turn_v(4)
-            elif k == 2:
-                mm1(4, [2, 3])
-                mm1(5, range(NQ))
-                turn_v(5)
-            elif k == 3:
-                mm1(6, [0, 1])
-            elif k == 4:
-                mm1(6, [2, 3])
-                turn_v(6)
-                mm1(7, range(NQ))
-                turn_v(7)
+                quant_d(0, 3)
         for n, b in ((0, 2), (1, 0), (2, 1), (3, 4), (4, 7), (6, 5), (7, 6)):
             mm2(n, 0, b)
         direction(7, slice(0, 1))

@@ -24,7 +24,6 @@ HALF = 512
 QUART = 256
 NT = DO // P
 TRANSPOSED = (1, 2)
-PACKED = 7
 
 
 def tile_doradirectiongradienttoloradown_w4_kernel(tc, x_bytes, x_scale, g, v, m, b_words, b_scales, out):
@@ -49,16 +48,13 @@ def tile_doradirectiongradienttoloradown_w4_kernel(tc, x_bytes, x_scale, g, v, m
 
         xs = [kt([P, 4], F32, "xs_first"), kt([P, NQ - 1, 4], F32, "xs_rest")]
         xb = [kt([P, 4, DI], U8, f"xb{q}") for q in range(NQ)]
-        g_first = kt([P, 4, HALF], BF16, "g_first")
-        g_rest = kt([P, NQ - 1, 4, HALF], BF16, "g_rest")
-        g_second = kt([P, NQ, 4, HALF], BF16, "g_second")
+        g_early = [[kt([P, 4, HALF], BF16, f"g{q}_{h}") for q in range(2)] for h in range(NG)]
+        g_late = [kt([P, 2, 4, HALF], BF16, f"g_late{h}") for h in range(NG)]
         vr = [[kt([P, 4, HALF], BF16, f"vr{s}_{h}") for h in range(NG)] for s in range(2)]
         xc = kt([P, NQ, DI], U32, "xc")
         xcs = kt([P, NQ, DI], U8, "xcs")
-        gc = kt([P, NT, NQ, P], U32, "gc")
-        gcs = kt([P, NT, NQ, P], U8, "gcs")
-        pc = kt([P, NQ + 1, 2, P], U32, "pc")
-        pcs = kt([P, NQ + 1, 2, P], U8, "pcs")
+        gc = kt([P, 4, NQ, 2, P], U32, "gc")
+        gcs = kt([P, 4, NQ, 2, P], U8, "gcs")
         dc = kt([P, NG, DI], U32, "dc")
         dcs = kt([P, NG, DI], U8, "dcs")
         ww = kt([P, NG, 2 * R], U8, "ww")
@@ -80,9 +76,7 @@ def tile_doradirectiongradienttoloradown_w4_kernel(tc, x_bytes, x_scale, g, v, m
             nc.sync.dma_start(out=xb[q][:, rows, :], in_=x4[q][:, rows, :])
 
         def g_pass(q, h):
-            if h == 1:
-                return g_second[:, q]
-            return g_first[:] if q == 0 else g_rest[:, q - 1]
+            return g_early[h][q][:] if q < 2 else g_late[h][:, q - 2]
 
         def load_g(q, h):
             nc.sync.dma_start(out=g_pass(q, h), in_=g4[q][:, :, HALF * h : HALF * (h + 1)])
@@ -156,43 +150,29 @@ def tile_doradirectiongradienttoloradown_w4_kernel(tc, x_bytes, x_scale, g, v, m
         def quant_x(q, cols=slice(0, DI)):
             nc.vector.quantize_mx(out=xc[:, q, cols].bitcast(E4M3X4), scales=xcs[:, q, cols], in_=xi[q][:, 4 * cols.start : 4 * cols.stop])
 
-        relay = kt([P, 3 * HALF], BF16, "relay")
+        relay = kt([P, DI], BF16, "relay")
 
-        def ileave_g(pair, q):
-            gi[pair, q] = wt([P, DI], BF16, "gi", 4)
-            on_s(gi[pair, q][:].rearrange("p (e m j) -> p m j e", e=2, j=4), g_pass(q, 0).rearrange("p j (m u e) -> p u m j e", u=2, e=2)[:, pair])
+        def ileave_g(pair, q, to=None):
+            h, u = divmod(pair, 2)
+            gi[pair, q] = wt([P, DI], BF16, "gi", 4) if to is None else to
+            on_s(gi[pair, q][:].rearrange("p (e m j) -> p m j e", e=2, j=4), g_pass(q, h).rearrange("p j (m u e) -> p u m j e", u=2, e=2)[:, u])
 
-        def quant_g(pair, q):
-            slot = NQ * pair + q
-            nc.vector.quantize_mx(out=pc[:, slot].rearrange("p e m -> p (e m)").bitcast(E4M3X4),
-                                  scales=pcs[:, slot].rearrange("p e m -> p (e m)"), in_=gi[pair, q][:])
-
-        def ileave_t(k, lo, hi, copy):
+        def relay_g(k):
             h, t = divmod(k, 4)
-            rows = g_second[:, lo:hi] if h == 1 else g_rest[:, lo - 1 : hi - 1]
-            if copy is on_g:
-                gi[k, lo, hi] = relay[:, 0 : HALF * (hi - lo)]
-            else:
-                gi[k, lo, hi] = wt([P, HALF * (hi - lo)], BF16, "gi", 4)[:]
-            copy(gi[k, lo, hi].rearrange("p (q m j) -> p q m j", m=P, j=4), rows.rearrange("p q j (m t) -> p t q m j", t=4)[:, t])
+            gi[k // 2, 2 + k % 2] = relay
+            on_g(relay[:].rearrange("p (q m j) -> p q m j", q=2, j=4), g_late[h][:].rearrange("p q j (m t) -> p t q m j", t=4)[:, t])
 
-        def quant_t(k, lo, hi):
-            nc.vector.quantize_mx(out=gc[:, k, lo:hi].rearrange("p q m -> p (q m)").bitcast(E4M3X4),
-                                  scales=gcs[:, k, lo:hi].rearrange("p q m -> p (q m)"), in_=gi[k, lo, hi])
+        def quant_g(pair, slot):
+            nc.vector.quantize_mx(out=gc[:, pair, slot].rearrange("p e m -> p (e m)").bitcast(E4M3X4),
+                                  scales=gcs[:, pair, slot].rearrange("p e m -> p (e m)"), in_=gi[pair, slot][:])
 
         def g_codes(k, q):
-            if k < 2 or (k < 4 and q == 0):
-                slot = NQ * (k // 2) + q
-                return pc[:, slot, k % 2, :], pcs[:, slot, k % 2, :]
-            return gc[:, k, q, :], gcs[:, k, q, :]
+            pair, e = divmod(k, 2)
+            slot, part = (q, e) if pair == 0 or q < 2 else (2 + e, q - 2)
+            return gc[:, pair, slot, part, :], gcs[:, pair, slot, part, :]
 
         def v_block(h, t, n):
             return vr[n // 4][h][:, n % 4, t : HALF : 4]
-
-        vp = [kt([P, 4, P], BF16, f"vp{s}") for s in range(2)]
-
-        def pack_v(s):
-            on_s(vp[s][:], vr[s][1][:].rearrange("p n (m t) -> p t n m", t=4)[:, PACKED % 4])
 
         vt = {}
         grams = {}
@@ -201,7 +181,7 @@ def tile_doradirectiongradienttoloradown_w4_kernel(tc, x_bytes, x_scale, g, v, m
             h, t = divmod(k, 4)
             if n == 0:
                 vt[k] = bank(k % 4, [P, DI], BF16)
-            nc.tensor.matmul(vt[k][:, P * n : P * (n + 1)], lhsT=vp[n // 4][:, n % 4, :] if k == PACKED else v_block(h, t, n), rhs=ident[:], start=True, stop=True, is_transpose=k in TRANSPOSED)
+            nc.tensor.matmul(vt[k][:, P * n : P * (n + 1)], lhsT=v_block(h, t, n), rhs=ident[:], start=True, stop=True, is_transpose=k in TRANSPOSED)
 
         def turn_v(k):
             for n in range(8):
@@ -359,26 +339,20 @@ def tile_doradirectiongradienttoloradown_w4_kernel(tc, x_bytes, x_scale, g, v, m
         mm1(0, [3], (1,))
         mm1(1, [2], (1,))
         mm1(1, [3])
-        gi[1, 0] = relay[:, 0:DI]
-        on_s(gi[1, 0].rearrange("p (e m j) -> p m j e", e=2, j=4), g_pass(0, 0).rearrange("p j (m u e) -> p u m j e", u=2, e=2)[:, 1])
+        ileave_g(1, 0, relay)
         norms(1, [0])
         quant_g(1, 0)
         evac(0)
 
         for k in range(NT):
-            if k == 0:
-                ileave_t(2, 1, 3, on_g)
-                ileave_t(2, 3, 4, on_s)
-                ileave_t(3, 1, 2, on_s)
-            elif k < 6:
-                ileave_t(k + 2, 2, 4, on_g)
+            pair, q = divmod(k + 3, 2)
+            if k < 6:
+                relay_g(k + 2)
             else:
                 relay_d(0, 2 * k - 11)
-            if 1 <= k < 5:
-                ileave_t(k + 3, 0, 2, on_s)
-            if k in (3, 4):
-                pack_v(k - 3)
-            if k in (5, 6):
+            if k < 5:
+                ileave_g(pair, q)
+            elif k < 7:
                 ileave_d(0, 2 * k - 10, on_s)
             if k == 7:
                 ileave_pair(0, 0, on_s)
@@ -396,33 +370,32 @@ def tile_doradirectiongradienttoloradown_w4_kernel(tc, x_bytes, x_scale, g, v, m
             fold(k)
             if k == 1:
                 factors(1)
+            if k < 5:
+                quant_g(pair, q)
+            elif k < 7:
+                quant_d(0, 2 * k - 10)
+            if k < 6:
+                quant_g(k // 2 + 1, 2 + k % 2)
+            else:
+                quant_d(0, 2 * k - 11)
             if k == 0:
-                quant_t(2, 3, 4)
-                quant_t(3, 1, 2)
-                quant_t(2, 1, 3)
                 turn_v(3)
-                mm1(2, [1, 2, 3])
-                mm1(3, [0, 1])
-            elif k < 5:
-                quant_t(k + 3, 0, 2)
-                quant_t(k + 2, 2, 4)
-                mm1(k + 2, [2, 3])
-                if k > 2:
-                    turn_v(k + 2)
+            if k in (0, 2, 4):
+                mm1(k + 2, [1, 2, 3])
+                if k == 4:
+                    turn_v(6)
                 mm1(k + 3, [0, 1])
+            elif k in (1, 3):
+                mm1(k + 2, [2, 3])
+                if k == 3:
+                    turn_v(5)
+                mm1(k + 3, [0])
                 if k == 1:
                     turn_v(4)
             elif k == 5:
-                quant_d(0, 0)
-                quant_t(7, 2, 4)
                 for s in range(2):
                     mm1(7, [2, 3], (s,))
                 turn_v(7)
-            elif k == 6:
-                quant_d(0, 2)
-                quant_d(0, 1)
-            else:
-                quant_d(0, 3)
         for n, b in ((0, 2), (1, 0), (2, 1), (3, 4), (4, 7), (6, 5), (7, 6)):
             mm2(n, 0, b)
         direction(7, slice(0, 1))

@@ -70,7 +70,8 @@ def tile_doradirectiongradienttoloradown_w4_kernel(tc, x_bytes, x_scale, g, v, m
 
         g4 = g.rearrange("(q p j) o -> q p j o", p=P, j=4)
         x4 = x_bytes.rearrange("(q p j) i -> q p j i", p=P, j=4)
-        v4 = v.rearrange("(s n p) o -> s p n o", p=P, n=4)
+        v4 = v.rearrange("(s p n) o -> s p n o", p=P, n=4)
+        out4 = out.rearrange("(s p n) r -> s p n r", p=P, n=4)
 
         def load_x(q, rows=slice(0, 4)):
             nc.sync.dma_start(out=xb[q][:, rows, :], in_=x4[q][:, rows, :])
@@ -230,7 +231,7 @@ def tile_doradirectiongradienttoloradown_w4_kernel(tc, x_bytes, x_scale, g, v, m
         def evac(k, sides=(0, 1)):
             gs[k] = wt([P, DI], F32, "gs", 4)
             for s in sides:
-                nc.scalar.activation(gs[k][:, HALF * s : HALF * (s + 1)], banks[k, s][:], ACT.Copy, scale=nbeta[:, k : k + 1])
+                nc.scalar.activation(gs[k][:, HALF * s : HALF * (s + 1)].rearrange("p (n r) -> p n r", n=4), banks[k, s][:].rearrange("p (r n) -> p n r", n=4), ACT.Copy, scale=nbeta[:, k : k + 1])
 
         def fold(k):
             dump = wt([P, DI], F32, "xi", 2)
@@ -276,13 +277,13 @@ def tile_doradirectiongradienttoloradown_w4_kernel(tc, x_bytes, x_scale, g, v, m
         def store_block(n):
             res = kt([P, R], F32, f"res_block{n}")
             on_s(res[:], outs[n][:])
-            nc.sync.dma_start(out=out[P * n : P * (n + 1), :], in_=res[:])
+            nc.sync.dma_start(out=out4[n // 4][:, n % 4, :], in_=res[:])
 
         def store_chunk(c):
             res = kt([P, 2, R], F32, f"res_chunk{c}")
             on_s(res[:, 0, :], outs[2 * c][:])
             on_v(res[:, 1, :], outs[2 * c + 1][:])
-            nc.sync.dma_start(out=out[QUART * c : QUART * (c + 1), :].rearrange("(a p) r -> p a r", p=P), in_=res[:])
+            nc.sync.dma_start(out=out4[c // 2][:, 2 * (c % 2) : 2 * (c % 2) + 2, :], in_=res[:])
 
         planes(0)
         planes(1)

@@ -50,7 +50,7 @@ def tile_doradirectiongradienttoloradown_w4_kernel(tc, x_bytes, x_scale, g, v, m
         xb = [kt([P, 4, DI], U8, f"xb{q}") for q in range(NQ)]
         g_early = [[kt([P, 4, HALF], BF16, f"g{q}_{h}") for q in range(2)] for h in range(NG)]
         g_late = [kt([P, 2, 4, HALF], BF16, f"g_late{h}") for h in range(NG)]
-        vr = [[kt([P, 4, HALF], BF16, f"vr{s}_{h}") for h in range(NG)] for s in range(2)]
+        vr = [kt([P, 2, DO], BF16, f"vr{a}") for a in range(4)]
         xc = kt([P, NQ, DI], U32, "xc")
         xcs = kt([P, NQ, DI], U8, "xcs")
         gc = kt([P, 4, NQ, 2, P], U32, "gc")
@@ -82,8 +82,8 @@ def tile_doradirectiongradienttoloradown_w4_kernel(tc, x_bytes, x_scale, g, v, m
         def load_g(q, h):
             nc.sync.dma_start(out=g_pass(q, h), in_=g4[q][:, :, HALF * h : HALF * (h + 1)])
 
-        def load_v(s, h):
-            nc.sync.dma_start(out=vr[s][h][:], in_=v4[s][:, :, HALF * h : HALF * (h + 1)])
+        def load_v(a):
+            nc.sync.dma_start(out=vr[a][:], in_=v4[a // 2][:, 2 * (a % 2) : 2 * (a % 2) + 2, :])
 
         s4 = x_scale.rearrange("(q p j) o -> p q (j o)", p=P, j=4)
         nc.scalar.dma_start(out=xs[0][:], in_=s4[:, 0, :])
@@ -92,16 +92,17 @@ def tile_doradirectiongradienttoloradown_w4_kernel(tc, x_bytes, x_scale, g, v, m
         load_x(0, slice(2, 4))
         load_x(1, slice(0, 2))
         load_x(1, slice(2, 4))
-        load_v(0, 0)
-        load_x(2)
-        load_v(1, 0)
+        load_v(0)
+        load_x(2, slice(0, 2))
+        load_v(1)
+        load_x(2, slice(2, 4))
+        load_v(2)
         load_g(0, 0)
-        load_g(1, 0)
-        load_x(3)
-        load_v(0, 1)
-        load_v(1, 1)
-        load_g(2, 0)
-        load_g(3, 0)
+        load_x(3, slice(0, 2))
+        load_v(3)
+        load_x(3, slice(2, 4))
+        for q in range(1, NQ):
+            load_g(q, 0)
         nc.gpsimd.memset(warm[:], 1.0)
         make_identity(nc, ident[:])
         nc.gpsimd.memset(ws[:].rearrange("p g n -> p (g n)").bitcast(I32), 0)
@@ -173,7 +174,7 @@ def tile_doradirectiongradienttoloradown_w4_kernel(tc, x_bytes, x_scale, g, v, m
             return gc[:, pair, slot, part, :], gcs[:, pair, slot, part, :]
 
         def v_block(h, t, n):
-            return vr[n // 4][h][:, n % 4, t : HALF : 4]
+            return vr[n // 2][:, n % 2, HALF * h + t : HALF * (h + 1) : 4]
 
         vt = {}
         grams = {}
@@ -188,13 +189,13 @@ def tile_doradirectiongradienttoloradown_w4_kernel(tc, x_bytes, x_scale, g, v, m
             for n in range(8):
                 turn_block(k, n)
 
-        def gram(h, b, turned=()):
-            grams[h] = bank(b, [P, 4, P], F32)
-            for n in range(8):
-                for t in range(4):
-                    nc.tensor.matmul(grams[h][:, t, :], lhsT=v_block(h, t, n), rhs=v_block(h, t, n), start=(n == 0 and t == 0), stop=(n == 7 and t == 3))
-                    if 4 * h + t in turned:
-                        turn_block(4 * h + t, n)
+        def gram(h, n):
+            if n == 0:
+                grams[h] = bank((6, 3)[h], [P, 4, P], F32)
+            for t in range(4):
+                nc.tensor.matmul(grams[h][:, t, :], lhsT=v_block(h, t, n), rhs=v_block(h, t, n), start=(n == 0 and t == 0), stop=(n == 7 and t == 3))
+                if h == 0 and t == 0:
+                    turn_block(0, n)
 
         def norms(h, tiles=range(4)):
             for t in tiles:
@@ -303,10 +304,12 @@ def tile_doradirectiongradienttoloradown_w4_kernel(tc, x_bytes, x_scale, g, v, m
         open_xi(1)
         ileave_x(1)
         quant_x(0)
-        gram(0, 6, (0,))
+        for a in range(4):
+            for h in range(NG):
+                gram(h, 2 * a)
+                gram(h, 2 * a + 1)
         turn_v(1)
         turn_v(2)
-        gram(1, 3)
         ileave_g(0, 0)
         quant_x(1)
         planes(3)
@@ -315,10 +318,10 @@ def tile_doradirectiongradienttoloradown_w4_kernel(tc, x_bytes, x_scale, g, v, m
         open_xi(2)
         ileave_x(2)
         quant_g(0, 0)
-        norms(0)
         mm1(0, [0])
-        mm1(1, [0])
         quant_x(2)
+        norms(0)
+        mm1(1, [0])
         ileave_g(0, 1)
         root(0)
         open_xi(3)

@@ -24,6 +24,8 @@ HALF = 512
 QUART = 256
 NT = DO // P
 TRANSPOSED = (1, 2)
+FUSED = 690
+STRIP = FUSED // 5
 
 
 def tile_doradirectiongradienttoloradown_w4_kernel(tc, x_bytes, x_scale, g, v, m, b_words, b_scales, out):
@@ -46,11 +48,11 @@ def tile_doradirectiongradienttoloradown_w4_kernel(tc, x_bytes, x_scale, g, v, m
             t = psum.tile(shape, dtype, name=f"bank{b}", tag=f"bank{b}", bufs=1)
             return t
 
-        xs = [kt([P, 4], F32, "xs_first"), kt([P, NQ - 1, 4], F32, "xs_rest")]
+        xs = kt([P, NQ, 4], F32, "xs")
         xb = [kt([P, 4, DI], U8, f"xb{q}") for q in range(NQ)]
         g_early = [[kt([P, 4, HALF], BF16, f"g{q}_{h}") for q in range(2)] for h in range(NG)]
         g_late = [kt([P, 2, 4, HALF], BF16, f"g_late{h}") for h in range(NG)]
-        vr = [kt([P, 2, DO], BF16, f"vr{a}") for a in range(4)]
+        vr = [[kt([P, 4, HALF], BF16, f"vr{h}_{a}") for a in range(2)] for h in range(NG)]
         xc = kt([P, NQ, DI], U32, "xc")
         xcs = kt([P, NQ, DI], U8, "xcs")
         gc = kt([P, 4, NQ, 2, P], U32, "gc")
@@ -60,12 +62,13 @@ def tile_doradirectiongradienttoloradown_w4_kernel(tc, x_bytes, x_scale, g, v, m
         ww = kt([P, NG, 2 * R], U8, "ww")
         ws = kt([P, NG, R], U8, "ws")
         mt = kt([P, NG, 4], BF16, "mt")
-        n2 = kt([P, NT], F32, "n2")
         r2 = kt([P, NT], F32, "r2")
         rn = kt([P, NT], F32, "rn")
         nbeta = kt([P, NT], F32, "nbeta")
         gam = kt([P, NT], F32, "gam")
         ident = kt([P, P], BF16, "ident")
+        pick = kt([P, 4, 32], F32, "pick")
+        ones = kt([P, 1], F32, "ones")
         warm = kt([P, 1], F32, "warm")
 
         g4 = g.rearrange("(q p j) o -> q p j o", p=P, j=4)
@@ -82,29 +85,26 @@ def tile_doradirectiongradienttoloradown_w4_kernel(tc, x_bytes, x_scale, g, v, m
         def load_g(q, h):
             nc.sync.dma_start(out=g_pass(q, h), in_=g4[q][:, :, HALF * h : HALF * (h + 1)])
 
-        def load_v(a):
-            nc.sync.dma_start(out=vr[a][:], in_=v4[a // 2][:, 2 * (a % 2) : 2 * (a % 2) + 2, :])
+        def load_v(h):
+            for a in range(2):
+                nc.sync.dma_start(out=vr[h][a][:], in_=v4[a][:, :, HALF * h : HALF * (h + 1)])
 
-        s4 = x_scale.rearrange("(q p j) o -> p q (j o)", p=P, j=4)
-        nc.scalar.dma_start(out=xs[0][:], in_=s4[:, 0, :])
-        nc.scalar.dma_start(out=xs[1][:], in_=s4[:, 1:NQ, :])
+        nc.scalar.dma_start(out=xs[:], in_=x_scale.rearrange("(q p j) o -> p q (j o)", p=P, j=4))
         load_x(0, slice(0, 2))
         load_x(0, slice(2, 4))
-        load_x(1, slice(0, 2))
-        load_x(1, slice(2, 4))
+        load_x(1)
         load_v(0)
-        load_x(2, slice(0, 2))
-        load_v(1)
-        load_x(2, slice(2, 4))
-        load_v(2)
         load_g(0, 0)
-        load_x(3, slice(0, 2))
-        load_v(3)
-        load_x(3, slice(2, 4))
-        for q in range(1, NQ):
-            load_g(q, 0)
+        load_x(2)
+        load_g(1, 0)
+        load_x(3)
+        load_g(2, 0)
+        load_g(3, 0)
+        load_v(1)
         nc.gpsimd.memset(warm[:], 1.0)
         make_identity(nc, ident[:])
+        nc.gpsimd.tensor_copy(out=pick[:], in_=ident[:].rearrange("j (m t) -> j t m", t=4))
+        nc.gpsimd.memset(ones[:], 1.0)
         nc.gpsimd.memset(ws[:].rearrange("p g n -> p (g n)").bitcast(I32), 0)
         nc.sync.dma_start(out=mt[:], in_=m.rearrange("(h p t) -> p h t", p=P, t=4))
         for q in range(NQ):
@@ -128,36 +128,37 @@ def tile_doradirectiongradienttoloradown_w4_kernel(tc, x_bytes, x_scale, g, v, m
 
         on_v, on_s = nc.vector.tensor_copy, nc.scalar.copy
 
-        def scale(q, j):
-            return xs[0][:, j : j + 1] if q == 0 else xs[1][:, q - 1, j : j + 1]
+        spread = [kt([P, STRIP, 4], F32, f"spread{q}") for q in range(NQ)]
 
-        def planes(q):
-            xp[q] = wt([P, 4, DI], BF16, "xp", 3)
+        def spread_scales(q, copy):
+            copy(spread[q][:], xs[:, q, :].unsqueeze(1).to_broadcast([P, STRIP, 4]))
 
-        def widen_s(q, j):
-            nc.scalar.activation(xp[q][:, j, :], xb[q][:, j, :].bitcast(FP8), ACT.Copy, scale=scale(q, j))
-
-        def widen_v(q, j):
-            nc.vector.tensor_scalar(out=xp[q][:, j, :], in0=xb[q][:, j, :].bitcast(FP8), scalar1=scale(q, j), scalar2=None, op0=ALU.mult)
+        def widen(q):
+            xp[q] = wt([P, 4, DI - FUSED], BF16, "xp", 2)
+            for j in range(4):
+                nc.scalar.activation(xp[q][:, j, :], xb[q][:, j, FUSED:DI].bitcast(FP8), ACT.Copy, scale=xs[:, q, j : j + 1])
 
         def open_xi(q):
             xi[q] = wt([P, 4 * DI], BF16, "xi", 2)
 
-        def ileave_x(q, cols=slice(0, DI)):
-            nc.vector.tensor_copy(
-                out=xi[q][:, 4 * cols.start : 4 * cols.stop].rearrange("p (c i t) -> p c t i", i=2, t=4),
-                in_=xp[q][:, :, cols].rearrange("p t (c i) -> p c t i", i=2),
-            )
+        def fused_x(q):
+            for c in range(0, FUSED, STRIP):
+                nc.vector.tensor_tensor(
+                    out=xi[q][:, 4 * c : 4 * (c + STRIP)].rearrange("p (c t) -> p c t", t=4),
+                    in0=xb[q][:, :, c : c + STRIP].bitcast(FP8).rearrange("p t c -> p c t"), in1=spread[q][:], op=ALU.mult)
+
+        def ileave_x(q):
+            on_s(xi[q][:, 4 * FUSED : 4 * DI].rearrange("p (c i t) -> p c t i", i=2, t=4), xp[q][:].rearrange("p t (c i) -> p c t i", i=2))
 
         def quant_x(q, cols=slice(0, DI)):
             nc.vector.quantize_mx(out=xc[:, q, cols].bitcast(E4M3X4), scales=xcs[:, q, cols], in_=xi[q][:, 4 * cols.start : 4 * cols.stop])
 
         relay = kt([P, DI], BF16, "relay")
 
-        def ileave_g(pair, q, to=None):
+        def ileave_g(pair, q, to=None, copy=on_s):
             h, u = divmod(pair, 2)
             gi[pair, q] = wt([P, DI], BF16, "gi", 4) if to is None else to
-            on_s(gi[pair, q][:].rearrange("p (e m j) -> p m j e", e=2, j=4), g_pass(q, h).rearrange("p j (m u e) -> p u m j e", u=2, e=2)[:, u])
+            copy(gi[pair, q][:].rearrange("p (e m j) -> p m j e", e=2, j=4), g_pass(q, h).rearrange("p j (m u e) -> p u m j e", u=2, e=2)[:, u])
 
         def relay_g(k):
             h, t = divmod(k, 4)
@@ -174,7 +175,7 @@ def tile_doradirectiongradienttoloradown_w4_kernel(tc, x_bytes, x_scale, g, v, m
             return gc[:, pair, slot, part, :], gcs[:, pair, slot, part, :]
 
         def v_block(h, t, n):
-            return vr[n // 2][:, n % 2, HALF * h + t : HALF * (h + 1) : 4]
+            return vr[h][n // 4][:, n % 4, t:HALF:4]
 
         vt = {}
         grams = {}
@@ -189,22 +190,28 @@ def tile_doradirectiongradienttoloradown_w4_kernel(tc, x_bytes, x_scale, g, v, m
             for n in range(8):
                 turn_block(k, n)
 
-        def gram(h, n):
-            if n == 0:
-                grams[h] = bank((6, 3)[h], [P, 4, P], F32)
-            for t in range(4):
-                nc.tensor.matmul(grams[h][:, t, :], lhsT=v_block(h, t, n), rhs=v_block(h, t, n), start=(n == 0 and t == 0), stop=(n == 7 and t == 3))
-                if h == 0 and t == 0:
-                    turn_block(0, n)
+        def gram(h):
+            grams[h] = bank((6, 3)[h], [P, 4, P], F32)
+            for n in range(8):
+                for b in range(4):
+                    block = vr[h][n // 4][:, n % 4, P * b : P * (b + 1)]
+                    nc.tensor.matmul(grams[h][:, b, :], lhsT=block, rhs=block, start=(n == 0 and b == 0), stop=(n == 7 and b == 3))
 
-        def norms(h, tiles=range(4)):
-            for t in tiles:
-                dump = wt([P, P], F32, "norm_dump", 4)
-                nc.vector.scalar_tensor_tensor(out=dump[:], in0=grams[h][:, t, :], scalar=1.0, in1=ident[:], op0=ALU.mult, op1=ALU.mult, accum_out=n2[:, 4 * h + t : 4 * h + t + 1])
+        diag = {}
+        n2 = {}
+
+        def diagonals(h):
+            diag[h] = kt([P, 4, P], F32, f"diag{h}")
+            nc.vector.tensor_tensor(out=diag[h][:].rearrange("j t (b m) -> j t b m", b=4), in0=grams[h][:].rearrange("j b (m t) -> j t b m", t=4),
+                                    in1=pick[:].unsqueeze(2).to_broadcast([P, 4, 4, 32]), op=ALU.mult)
+
+        def norms(h):
+            n2[h] = bank((6, 3)[h], [P, 4], F32)
+            for t in range(4):
+                nc.tensor.matmul(n2[h][:, t : t + 1], lhsT=diag[h][:, t, :], rhs=ones[:], start=True, stop=True)
 
         def root(h):
-            four = slice(4 * h, 4 * h + 4)
-            nc.scalar.activation(rn[:, four], n2[:, four], ACT.Abs_reciprocal_sqrt)
+            nc.scalar.activation(rn[:, 4 * h : 4 * h + 4], n2[h][:], ACT.Abs_reciprocal_sqrt)
 
         def factors(h):
             four = slice(4 * h, 4 * h + 4)
@@ -286,66 +293,56 @@ def tile_doradirectiongradienttoloradown_w4_kernel(tc, x_bytes, x_scale, g, v, m
             on_v(res[:, 1, :], outs[2 * c + 1][:])
             nc.sync.dma_start(out=out4[c // 2][:, 2 * (c % 2) : 2 * (c % 2) + 2, :], in_=res[:])
 
-        planes(0)
-        planes(1)
-        widen_s(0, 0)
-        widen_s(0, 3)
-        widen_v(0, 1)
-        widen_v(0, 2)
-        widen_v(1, 0)
-        widen_v(1, 1)
-        widen_s(1, 2)
-        widen_s(1, 3)
-        open_xi(0)
-        ileave_x(0)
-        planes(2)
-        for j in range(4):
-            widen_s(2, j)
-        open_xi(1)
-        ileave_x(1)
-        quant_x(0)
-        for a in range(4):
-            for h in range(NG):
-                gram(h, 2 * a)
-                gram(h, 2 * a + 1)
+        for q in range(3):
+            spread_scales(q, on_v)
+        spread_scales(3, on_s)
+        for q in range(2):
+            widen(q)
+            open_xi(q)
+            fused_x(q)
+            ileave_x(q)
+        ileave_g(0, 0)
+        gram(0)
+        turn_v(0)
         turn_v(1)
         turn_v(2)
-        ileave_g(0, 0)
-        quant_x(1)
-        planes(3)
-        for j in range(4):
-            widen_s(3, j)
-        open_xi(2)
-        ileave_x(2)
+        quant_x(0)
+        diagonals(0)
         quant_g(0, 0)
-        mm1(0, [0])
-        quant_x(2)
         norms(0)
-        mm1(1, [0])
+        mm1(0, [0])
+        widen(2)
+        open_xi(2)
+        fused_x(2)
         ileave_g(0, 1)
         root(0)
-        open_xi(3)
-        ileave_x(3, slice(0, HALF))
+        ileave_x(2)
+        mm1(1, [0])
+        quant_x(1)
         quant_g(0, 1)
         mm1(0, [1])
         mm1(1, [1])
+        gram(1)
+        open_xi(3)
         ileave_g(0, 2)
-        ileave_x(3, slice(HALF, DI))
-        factors(0)
+        widen(3)
+        fused_x(3)
         ileave_g(0, 3)
+        ileave_x(3)
         quant_g(0, 2)
+        quant_x(2)
+        factors(0)
         mm1(0, [2])
+        mm1(1, [2])
         quant_x(3, slice(0, HALF))
         quant_g(0, 3)
         quant_x(3, slice(HALF, DI))
-        mm1(0, [3], (0,))
-        mm1(1, [2], (0,))
-        mm1(0, [3], (1,))
-        mm1(1, [2], (1,))
+        mm1(0, [3])
         mm1(1, [3])
         ileave_g(1, 0, relay)
-        norms(1, [0])
+        diagonals(1)
         quant_g(1, 0)
+        norms(1)
         evac(0)
 
         for k in range(NT):
@@ -356,6 +353,8 @@ def tile_doradirectiongradienttoloradown_w4_kernel(tc, x_bytes, x_scale, g, v, m
                 relay_d(0, 2 * k - 11)
             if k < 5:
                 ileave_g(pair, q)
+                if k == 0:
+                    root(1)
             elif k < 7:
                 ileave_d(0, 2 * k - 10, on_s)
             if k == 7:
@@ -367,8 +366,6 @@ def tile_doradirectiongradienttoloradown_w4_kernel(tc, x_bytes, x_scale, g, v, m
                 evac(k + 1)
             if k == 0:
                 mm1(2, [0])
-                norms(1, [1, 2, 3])
-                root(1)
             else:
                 direction(k - 1)
             fold(k)

@@ -23,10 +23,8 @@ NG = DO // 512
 HALF = 512
 QUART = 256
 NT = DO // P
-TRANSPOSED = (1, 2)
-FUSED = 690
-STRIP = FUSED // 5
-
+TRANSPOSED = (0, 2, 3, 7)
+SHARE = 512
 
 def tile_doradirectiongradienttoloradown_w4_kernel(tc, x_bytes, x_scale, g, v, m, b_words, b_scales, out):
     nc = tc.nc
@@ -48,7 +46,7 @@ def tile_doradirectiongradienttoloradown_w4_kernel(tc, x_bytes, x_scale, g, v, m
             t = psum.tile(shape, dtype, name=f"bank{b}", tag=f"bank{b}", bufs=1)
             return t
 
-        xs = kt([P, NQ, 4], F32, "xs")
+        xs = [kt([P, 4], F32, "xs_first"), kt([P, NQ - 1, 4], F32, "xs_rest")]
         xb = [kt([P, 4, DI], U8, f"xb{q}") for q in range(NQ)]
         g_early = [[kt([P, 4, HALF], BF16, f"g{q}_{h}") for q in range(2)] for h in range(NG)]
         g_late = [kt([P, 2, 4, HALF], BF16, f"g_late{h}") for h in range(NG)]
@@ -85,22 +83,26 @@ def tile_doradirectiongradienttoloradown_w4_kernel(tc, x_bytes, x_scale, g, v, m
         def load_g(q, h):
             nc.sync.dma_start(out=g_pass(q, h), in_=g4[q][:, :, HALF * h : HALF * (h + 1)])
 
-        def load_v(h):
-            for a in range(2):
-                nc.sync.dma_start(out=vr[h][a][:], in_=v4[a][:, :, HALF * h : HALF * (h + 1)])
+        def load_v(h, a):
+            nc.sync.dma_start(out=vr[h][a][:], in_=v4[a][:, :, HALF * h : HALF * (h + 1)])
 
-        nc.scalar.dma_start(out=xs[:], in_=x_scale.rearrange("(q p j) o -> p q (j o)", p=P, j=4))
+        s4 = x_scale.rearrange("(q p j) o -> p q (j o)", p=P, j=4)
+        nc.scalar.dma_start(out=xs[0][:], in_=s4[:, 0, :])
+        nc.scalar.dma_start(out=xs[1][:], in_=s4[:, 1:NQ, :])
         load_x(0, slice(0, 2))
         load_x(0, slice(2, 4))
-        load_x(1)
-        load_v(0)
-        load_g(0, 0)
+        load_x(1, slice(0, 2))
+        load_x(1, slice(2, 4))
+        load_v(0, 0)
         load_x(2)
+        load_v(0, 1)
+        load_g(0, 0)
         load_g(1, 0)
         load_x(3)
+        load_v(1, 0)
+        load_v(1, 1)
         load_g(2, 0)
         load_g(3, 0)
-        load_v(1)
         nc.gpsimd.memset(warm[:], 1.0)
         make_identity(nc, ident[:])
         nc.gpsimd.tensor_copy(out=pick[:], in_=ident[:].rearrange("j (m t) -> j t m", t=4))
@@ -128,27 +130,31 @@ def tile_doradirectiongradienttoloradown_w4_kernel(tc, x_bytes, x_scale, g, v, m
 
         on_v, on_s = nc.vector.tensor_copy, nc.scalar.copy
 
-        spread = [kt([P, STRIP, 4], F32, f"spread{q}") for q in range(NQ)]
+        def scale(q, j):
+            return xs[0][:, j : j + 1] if q == 0 else xs[1][:, q - 1, j : j + 1]
 
-        def spread_scales(q, copy):
-            copy(spread[q][:], xs[:, q, :].unsqueeze(1).to_broadcast([P, STRIP, 4]))
+        def planes(q, side=0, width=DI):
+            xp[q, side] = wt([P, 4, width], BF16, "xp", 3)
 
-        def widen(q):
-            xp[q] = wt([P, 4, DI - FUSED], BF16, "xp", 2)
+        def widen_s(q, j, cols=slice(0, DI)):
+            nc.scalar.activation(xp[q, 0][:, j, cols], xb[q][:, j, cols].bitcast(FP8), ACT.Copy, scale=scale(q, j))
+
+        def widen_v(q, j, cols=slice(0, DI)):
+            nc.vector.tensor_scalar(out=xp[q, 0][:, j, cols], in0=xb[q][:, j, cols].bitcast(FP8), scalar1=scale(q, j), scalar2=None, op0=ALU.mult)
+
+        def widen_side(q, side):
+            planes(q, side, HALF)
             for j in range(4):
-                nc.scalar.activation(xp[q][:, j, :], xb[q][:, j, FUSED:DI].bitcast(FP8), ACT.Copy, scale=xs[:, q, j : j + 1])
+                nc.scalar.activation(xp[q, side][:, j, :], xb[q][:, j, HALF * side : HALF * (side + 1)].bitcast(FP8), ACT.Copy, scale=scale(q, j))
 
         def open_xi(q):
             xi[q] = wt([P, 4 * DI], BF16, "xi", 2)
 
-        def fused_x(q):
-            for c in range(0, FUSED, STRIP):
-                nc.vector.tensor_tensor(
-                    out=xi[q][:, 4 * c : 4 * (c + STRIP)].rearrange("p (c t) -> p c t", t=4),
-                    in0=xb[q][:, :, c : c + STRIP].bitcast(FP8).rearrange("p t c -> p c t"), in1=spread[q][:], op=ALU.mult)
-
-        def ileave_x(q):
-            on_s(xi[q][:, 4 * FUSED : 4 * DI].rearrange("p (c i t) -> p c t i", i=2, t=4), xp[q][:].rearrange("p t (c i) -> p c t i", i=2))
+        def ileave_x(q, side=0, width=DI):
+            nc.vector.tensor_copy(
+                out=xi[q][:, 4 * HALF * side : 4 * (HALF * side + width)].rearrange("p (c i t) -> p c t i", i=2, t=4),
+                in_=xp[q, side][:].rearrange("p t (c i) -> p c t i", i=2),
+            )
 
         def quant_x(q, cols=slice(0, DI)):
             nc.vector.quantize_mx(out=xc[:, q, cols].bitcast(E4M3X4), scales=xcs[:, q, cols], in_=xi[q][:, 4 * cols.start : 4 * cols.stop])
@@ -159,6 +165,19 @@ def tile_doradirectiongradienttoloradown_w4_kernel(tc, x_bytes, x_scale, g, v, m
             h, u = divmod(pair, 2)
             gi[pair, q] = wt([P, DI], BF16, "gi", 4) if to is None else to
             copy(gi[pair, q][:].rearrange("p (e m j) -> p m j e", e=2, j=4), g_pass(q, h).rearrange("p j (m u e) -> p u m j e", u=2, e=2)[:, u])
+
+        staged = {}
+
+        def stage_g(q, b):
+            staged[q] = bank(b, [P, 2, P, 4], BF16)
+            pairs = g_pass(q, 0).rearrange("p j (m u e) -> p u e m j", u=2, e=2)[:, 0]
+            for e in range(2):
+                for j in (0, 2):
+                    nc.tensor.matmul(staged[q][:, e, :, j : j + 2], lhsT=ident[:], rhs=pairs[:, e, :, j : j + 2], start=True, stop=True)
+
+        def unstage_g(q):
+            gi[0, q] = wt([P, DI], BF16, "gi", 4)
+            on_s(gi[0, q][:], staged[q][:].rearrange("p e m j -> p (e m j)"))
 
         def relay_g(k):
             h, t = divmod(k, 4)
@@ -293,51 +312,64 @@ def tile_doradirectiongradienttoloradown_w4_kernel(tc, x_bytes, x_scale, g, v, m
             on_v(res[:, 1, :], outs[2 * c + 1][:])
             nc.sync.dma_start(out=out4[c // 2][:, 2 * (c % 2) : 2 * (c % 2) + 2, :], in_=res[:])
 
-        for q in range(3):
-            spread_scales(q, on_v)
-        spread_scales(3, on_s)
-        for q in range(2):
-            widen(q)
-            open_xi(q)
-            fused_x(q)
-            ileave_x(q)
-        ileave_g(0, 0)
-        gram(0)
-        turn_v(0)
-        turn_v(1)
-        turn_v(2)
+        planes(0)
+        planes(1)
+        widen_s(0, 0)
+        widen_s(0, 3)
+        widen_v(0, 1)
+        widen_v(0, 2)
+        widen_v(1, 0)
+        widen_v(1, 1, slice(0, SHARE))
+        widen_s(1, 1, slice(SHARE, DI))
+        widen_s(1, 2)
+        widen_s(1, 3)
+        open_xi(0)
+        ileave_x(0)
+        planes(2)
+        for j in range(4):
+            widen_s(2, j)
+        open_xi(1)
+        ileave_x(1)
         quant_x(0)
-        diagonals(0)
-        quant_g(0, 0)
-        norms(0)
-        mm1(0, [0])
-        widen(2)
-        open_xi(2)
-        fused_x(2)
-        ileave_g(0, 1)
-        root(0)
-        ileave_x(2)
-        mm1(1, [0])
+        gram(0)
+        stage_g(0, 7)
+        turn_v(0)
+        stage_g(1, 5)
+        turn_v(1)
         quant_x(1)
+        diagonals(0)
+        norms(0)
+        gram(1)
+        turn_v(2)
+        unstage_g(0)
+        widen_side(3, 0)
+        unstage_g(1)
+        root(0)
+        open_xi(2)
+        ileave_x(2)
+        widen_side(3, 1)
+        quant_g(0, 0)
+        quant_x(2)
+        mm1(0, [0])
+        mm1(1, [0])
+        open_xi(3)
+        ileave_x(3, 0, HALF)
         quant_g(0, 1)
         mm1(0, [1])
         mm1(1, [1])
-        gram(1)
-        open_xi(3)
         ileave_g(0, 2)
-        widen(3)
-        fused_x(3)
-        ileave_g(0, 3)
-        ileave_x(3)
-        quant_g(0, 2)
-        quant_x(2)
+        ileave_x(3, 1, HALF)
         factors(0)
+        ileave_g(0, 3)
+        quant_g(0, 2)
         mm1(0, [2])
-        mm1(1, [2])
         quant_x(3, slice(0, HALF))
         quant_g(0, 3)
         quant_x(3, slice(HALF, DI))
-        mm1(0, [3])
+        mm1(0, [3], (0,))
+        mm1(1, [2], (0,))
+        mm1(0, [3], (1,))
+        mm1(1, [2], (1,))
         mm1(1, [3])
         ileave_g(1, 0, relay)
         diagonals(1)

@@ -224,6 +224,19 @@ def tile_doradirectiongradienttoloradown_w4_kernel(tc, x_bytes, x_scale, g, v, m
             nc.vector.tensor_tensor(out=diag[h][:].rearrange("j t (b m) -> j t b m", b=4), in0=grams[h][:].rearrange("j b (m t) -> j t b m", t=4),
                                     in1=pick[:].unsqueeze(2).to_broadcast([P, 4, 4, 32]), op=ALU.mult)
 
+        n2_raw = kt([P, 4], F32, "n2_raw")
+        n2_late = kt([P, 4], F32, "n2_late")
+
+        n2[1] = n2_late
+
+        def diagonal_late(b):
+            dump = wt([P, P], F32, "norm_dump", 4)
+            nc.vector.scalar_tensor_tensor(out=dump[:], in0=grams[1][:, b, :], scalar=1.0, in1=ident[:], op0=ALU.mult, op1=ALU.mult, accum_out=n2_raw[:, b : b + 1])
+
+        def move_norms():
+            for b in range(4):
+                nc.sync.dma_start(out=n2_late[32 * b : 32 * (b + 1), :], in_=n2_raw[:, b : b + 1])
+
         def norms(h):
             n2[h] = bank((6, 3)[h], [P, 4], F32)
             for t in range(4):
@@ -372,9 +385,12 @@ def tile_doradirectiongradienttoloradown_w4_kernel(tc, x_bytes, x_scale, g, v, m
         mm1(1, [2], (1,))
         mm1(1, [3])
         ileave_g(1, 0, relay)
-        diagonals(1)
+        diagonal_late(0)
         quant_g(1, 0)
-        norms(1)
+        for b in range(1, 4):
+            diagonal_late(b)
+        move_norms()
+        turn_v(3)
         evac(0)
 
         for k in range(NT):
@@ -385,7 +401,7 @@ def tile_doradirectiongradienttoloradown_w4_kernel(tc, x_bytes, x_scale, g, v, m
                 relay_d(0, 2 * k - 11)
             if k < 5:
                 ileave_g(pair, q)
-                if k == 0:
+                if k == 2:
                     root(1)
             elif k < 7:
                 ileave_d(0, 2 * k - 10, on_s)
@@ -401,7 +417,7 @@ def tile_doradirectiongradienttoloradown_w4_kernel(tc, x_bytes, x_scale, g, v, m
             else:
                 direction(k - 1)
             fold(k)
-            if k == 1:
+            if k == 2:
                 factors(1)
             if k < 5:
                 quant_g(pair, q)
@@ -411,8 +427,6 @@ def tile_doradirectiongradienttoloradown_w4_kernel(tc, x_bytes, x_scale, g, v, m
                 quant_g(k // 2 + 1, 2 + k % 2)
             else:
                 quant_d(0, 2 * k - 11)
-            if k == 0:
-                turn_v(3)
             if k in (0, 2, 4):
                 mm1(k + 2, [1, 2, 3])
                 if k == 4:

@@ -24,7 +24,7 @@ HALF = 512
 QUART = 256
 NT = DO // P
 TRANSPOSED = (0, 2, 3, 7)
-SHARE = 512
+SHARE = 448
 
 def tile_doradirectiongradienttoloradown_w4_kernel(tc, x_bytes, x_scale, g, v, m, b_words, b_scales, out):
     nc = tc.nc
@@ -88,17 +88,19 @@ def tile_doradirectiongradienttoloradown_w4_kernel(tc, x_bytes, x_scale, g, v, m
 
         s4 = x_scale.rearrange("(q p j) o -> p q (j o)", p=P, j=4)
         nc.scalar.dma_start(out=xs[0][:], in_=s4[:, 0, :])
-        nc.scalar.dma_start(out=xs[1][:], in_=s4[:, 1:NQ, :])
-        load_x(0, slice(0, 2))
+        load_x(0, slice(0, 1))
+        load_x(0, slice(1, 2))
         load_x(0, slice(2, 4))
+        nc.sync.dma_start(out=xs[1][:], in_=s4[:, 1:NQ, :])
         load_x(1, slice(0, 2))
         load_x(1, slice(2, 4))
         load_v(0, 0)
-        load_x(2)
+        load_x(2, slice(0, 2))
         load_v(0, 1)
+        load_x(2, slice(2, 4))
         load_g(0, 0)
-        load_g(1, 0)
         load_x(3)
+        load_g(1, 0)
         load_v(1, 0)
         load_v(1, 1)
         load_g(2, 0)
@@ -287,10 +289,10 @@ def tile_doradirectiongradienttoloradown_w4_kernel(tc, x_bytes, x_scale, g, v, m
             di[h, c] = wt([P, DI], BF16, "gi", 4)
             copy(di[h, c][:].rearrange("p (c i t) -> p c t i", i=2, t=4), dv[h][:, c, :, :].rearrange("p t (c i) -> p c t i", i=2))
 
-        def ileave_pair(c, u, copy):
+        def ileave_pair(c, u, copy, cols=slice(0, QUART)):
             if u == 0:
                 di[1, c] = kt([P, DI], BF16, f"di{c}")
-            copy(di[1, c][:].rearrange("p (c u e) -> p u c e", u=2, e=2)[:, u], dv[1][:, c, 2 * u : 2 * u + 2, :].rearrange("p e c -> p c e"))
+            copy(di[1, c][:].rearrange("p (c u e) -> p u c e", u=2, e=2)[:, u, cols], dv[1][:, c, 2 * u : 2 * u + 2, cols].rearrange("p e c -> p c e"))
 
         def relay_d(h, c):
             di[h, c] = relay[:, 0:DI]
@@ -345,10 +347,10 @@ def tile_doradirectiongradienttoloradown_w4_kernel(tc, x_bytes, x_scale, g, v, m
         ileave_x(1)
         quant_x(0)
         gram(0)
-        stage_g(0, 7)
         turn_v(0)
-        stage_g(1, 5)
+        stage_g(0, 7)
         turn_v(1)
+        stage_g(1, 5)
         quant_x(1)
         diagonals(0)
         norms(0)
@@ -449,15 +451,19 @@ def tile_doradirectiongradienttoloradown_w4_kernel(tc, x_bytes, x_scale, g, v, m
         direction(7, slice(1, 2))
         ileave_pair(1, 1, on_s)
         ileave_pair(0, 1, on_v)
-        direction(7, slice(2, 4))
-        mm2(5, 0, 3)
-        ileave_pair(2, 1, on_s)
+        direction(7, slice(2, 3))
+        ileave_pair(2, 1, on_s, slice(0, P))
         finish(0)
-        ileave_pair(3, 1, on_v)
-        finish(1)
-        finish(3)
+        direction(7, slice(3, 4))
+        mm2(5, 0, 3)
         store_block(0)
         store_block(1)
+        finish(1)
+        ileave_pair(2, 1, on_v, slice(P, QUART))
+        ileave_pair(3, 1, on_v)
         finish(2)
-        for c in (1, 3, 2):
-            store_chunk(c)
+        finish(3)
+        store_block(2)
+        store_block(3)
+        store_chunk(2)
+        store_chunk(3)

@@ -88,10 +88,10 @@ def tile_doradirectiongradienttoloradown_w4_kernel(tc, x_bytes, x_scale, g, v, m
 
         s4 = x_scale.rearrange("(q p j) o -> p q (j o)", p=P, j=4)
         nc.scalar.dma_start(out=xs[0][:], in_=s4[:, 0, :])
+        nc.scalar.dma_start(out=xs[1][:], in_=s4[:, 1:NQ, :])
         load_x(0, slice(0, 1))
         load_x(0, slice(1, 2))
         load_x(0, slice(2, 4))
-        nc.sync.dma_start(out=xs[1][:], in_=s4[:, 1:NQ, :])
         load_x(1, slice(0, 2))
         load_x(1, slice(2, 4))
         load_v(0, 0)

from contextlib import ExitStack

import concourse.mybir as mybir
from concourse.masks import make_identity

T, DI, DO, R = 2048, 1024, 1024, 256
FLOPS = 2 * T * DI * DO + 2 * DI * DO * R

P = 128
F32 = mybir.dt.float32
BF16 = mybir.dt.bfloat16
I32 = mybir.dt.int32
U32 = mybir.dt.uint32
U8 = mybir.dt.uint8
FP8 = mybir.dt.float8_e4m3fn
E4M3X4 = mybir.dt.float8_e4m3fn_x4
E2M1X4 = mybir.dt.float4_e2m1fn_x4
ACT = mybir.ActivationFunctionType
ALU = mybir.AluOpType

NQ = T // 512
NG = DO // 512
HALF = 512
QUART = 256
NT = DO // P
TRANSPOSED = (0, 2, 3, 7)
SHARE = 448

def tile_doradirectiongradienttoloradown_w4_kernel(tc, x_bytes, x_scale, g, v, m, b_words, b_scales, out):
    nc = tc.nc
    with ExitStack() as ctx:
        keep = ctx.enter_context(tc.tile_pool(name="keep", bufs=1))
        work = ctx.enter_context(tc.tile_pool(name="work", bufs=2))
        psum = ctx.enter_context(tc.psum_pool(name="psum", bufs=1))
        ctx.enter_context(tc.manual_schedule())

        def kt(shape, dtype, name):
            t = keep.tile(shape, dtype, name=name, align_bytes=64)
            return t

        def wt(shape, dtype, name, bufs):
            t = work.tile(shape, dtype, name=name, tag=name, bufs=bufs, align_bytes=64)
            return t

        def bank(b, shape, dtype):
            t = psum.tile(shape, dtype, name=f"bank{b}", tag=f"bank{b}", bufs=1)
            return t

        xs = [kt([P, 4], F32, "xs_first"), kt([P, NQ - 1, 4], F32, "xs_rest")]
        xb = [kt([P, 4, DI], U8, f"xb{q}") for q in range(NQ)]
        g_early = [[kt([P, 4, HALF], BF16, f"g{q}_{h}") for q in range(2)] for h in range(NG)]
        g_late = [kt([P, 2, 4, HALF], BF16, f"g_late{h}") for h in range(NG)]
        vr = [[kt([P, 4, HALF], BF16, f"vr{h}_{a}") for a in range(2)] for h in range(NG)]
        xc = kt([P, NQ, DI], U32, "xc")
        xcs = kt([P, NQ, DI], U8, "xcs")
        gc = kt([P, 4, NQ, 2, P], U32, "gc")
        gcs = kt([P, 4, NQ, 2, P], U8, "gcs")
        dc = kt([P, NG, DI], U32, "dc")
        dcs = kt([P, NG, DI], U8, "dcs")
        ww = kt([P, NG, 2 * R], U8, "ww")
        ws = kt([P, NG, R], U8, "ws")
        mt = kt([P, NG, 4], BF16, "mt")
        r2 = kt([P, NT], F32, "r2")
        rn = kt([P, NT], F32, "rn")
        nbeta = kt([P, NT], F32, "nbeta")
        gam = kt([P, NT], F32, "gam")
        ident = kt([P, P], BF16, "ident")
        pick = kt([P, 4, 32], F32, "pick")
        ones = kt([P, 1], F32, "ones")
        warm = kt([P, 1], F32, "warm")

        g4 = g.rearrange("(q p j) o -> q p j o", p=P, j=4)
        x4 = x_bytes.rearrange("(q p j) i -> q p j i", p=P, j=4)
        v4 = v.rearrange("(s p n) o -> s p n o", p=P, n=4)
        out4 = out.rearrange("(s p n) r -> s p n r", p=P, n=4)

        def load_x(q, rows=slice(0, 4)):
            nc.sync.dma_start(out=xb[q][:, rows, :], in_=x4[q][:, rows, :])

        def g_pass(q, h):
            return g_early[h][q][:] if q < 2 else g_late[h][:, q - 2]

        def load_g(q, h):
            nc.sync.dma_start(out=g_pass(q, h), in_=g4[q][:, :, HALF * h : HALF * (h + 1)])

        def load_v(h, a):
            nc.sync.dma_start(out=vr[h][a][:], in_=v4[a][:, :, HALF * h : HALF * (h + 1)])

        s4 = x_scale.rearrange("(q p j) o -> p q (j o)", p=P, j=4)
        nc.scalar.dma_start(out=xs[0][:], in_=s4[:, 0, :])
        nc.scalar.dma_start(out=xs[1][:], in_=s4[:, 1:NQ, :])
        load_x(0, slice(0, 1))
        load_x(0, slice(1, 2))
        load_x(0, slice(2, 4))
        load_x(1, slice(0, 2))
        load_x(1, slice(2, 4))
        load_v(0, 0)
        load_x(2, slice(0, 2))
        load_v(0, 1)
        load_x(2, slice(2, 4))
        load_g(0, 0)
        load_x(3)
        load_g(1, 0)
        load_v(1, 0)
        load_v(1, 1)
        load_g(2, 0)
        load_g(3, 0)
        nc.gpsimd.memset(warm[:], 1.0)
        make_identity(nc, ident[:])
        nc.gpsimd.tensor_copy(out=pick[:], in_=ident[:].rearrange("j (m t) -> j t m", t=4))
        nc.gpsimd.memset(ones[:], 1.0)
        nc.gpsimd.memset(ws[:].rearrange("p g n -> p (g n)").bitcast(I32), 0)
        nc.sync.dma_start(out=mt[:], in_=m.rearrange("(h p t) -> p h t", p=P, t=4))
        for q in range(NQ):
            load_g(q, 1)
        nc.sync.dma_start(out=ww[:].rearrange("p g n -> p (g n)").bitcast(I32).rearrange("p (g n) -> p g n", g=NG),
                          in_=b_words.bitcast(I32).rearrange("g p n -> p g n"))
        ws32 = ws[:].rearrange("p g n -> p (g n)").bitcast(I32).rearrange("p (g n) -> p g n", g=NG)
        bs32 = b_scales.bitcast(I32)
        for quad in range(4):
            nc.sync.dma_start(out=ws32[32 * quad : 32 * quad + 4, :, :],
                              in_=bs32[:, 4 * quad : 4 * quad + 4, :].rearrange("g q n -> q g n"))

        nc.scalar.activation(warm[:], warm[:], ACT.Abs_reciprocal_sqrt)

        xp = {}
        xi = {}
        gi = {}

        def on_g(out, in_):
            nc.gpsimd.tensor_scalar(out=out, in0=in_, scalar1=1.0, scalar2=0.0, op0=ALU.mult, op1=ALU.add)

        on_v, on_s = nc.vector.tensor_copy, nc.scalar.copy

        def scale(q, j):
            return xs[0][:, j : j + 1] if q == 0 else xs[1][:, q - 1, j : j + 1]

        def planes(q, side=0, width=DI):
            xp[q, side] = wt([P, 4, width], BF16, "xp", 3)

        def widen_s(q, j, cols=slice(0, DI)):
            nc.scalar.activation(xp[q, 0][:, j, cols], xb[q][:, j, cols].bitcast(FP8), ACT.Copy, scale=scale(q, j))

        def widen_v(q, j, cols=slice(0, DI)):
            nc.vector.tensor_scalar(out=xp[q, 0][:, j, cols], in0=xb[q][:, j, cols].bitcast(FP8), scalar1=scale(q, j), scalar2=None, op0=ALU.mult)

        def widen_side(q, side):
            planes(q, side, HALF)
            for j in range(4):
                nc.scalar.activation(xp[q, side][:, j, :], xb[q][:, j, HALF * side : HALF * (side + 1)].bitcast(FP8), ACT.Copy, scale=scale(q, j))

        def open_xi(q):
            xi[q] = wt([P, 4 * DI], BF16, "xi", 2)

        def ileave_x(q, side=0, width=DI):
            nc.vector.tensor_copy(
                out=xi[q][:, 4 * HALF * side : 4 * (HALF * side + width)].rearrange("p (c i t) -> p c t i", i=2, t=4),
                in_=xp[q, side][:].rearrange("p t (c i) -> p c t i", i=2),
            )

        def quant_x(q, cols=slice(0, DI)):
            nc.vector.quantize_mx(out=xc[:, q, cols].bitcast(E4M3X4), scales=xcs[:, q, cols], in_=xi[q][:, 4 * cols.start : 4 * cols.stop])

        relay = kt([P, DI], BF16, "relay")

        def ileave_g(pair, q, to=None, copy=on_s):
            h, u = divmod(pair, 2)
            gi[pair, q] = wt([P, DI], BF16, "gi", 4) if to is None else to
            copy(gi[pair, q][:].rearrange("p (e m j) -> p m j e", e=2, j=4), g_pass(q, h).rearrange("p j (m u e) -> p u m j e", u=2, e=2)[:, u])

        staged = {}

        def stage_g(q, b):
            staged[q] = bank(b, [P, 2, P, 4], BF16)
            pairs = g_pass(q, 0).rearrange("p j (m u e) -> p u e m j", u=2, e=2)[:, 0]
            for e in range(2):
                for j in (0, 2):
                    nc.tensor.matmul(staged[q][:, e, :, j : j + 2], lhsT=ident[:], rhs=pairs[:, e, :, j : j + 2], start=True, stop=True)

        def unstage_g(q):
            gi[0, q] = wt([P, DI], BF16, "gi", 4)
            on_s(gi[0, q][:], staged[q][:].rearrange("p e m j -> p (e m j)"))

        def relay_g(k):
            h, t = divmod(k, 4)
            gi[k // 2, 2 + k % 2] = relay
            on_g(relay[:].rearrange("p (q m j) -> p q m j", q=2, j=4), g_late[h][:].rearrange("p q j (m t) -> p t q m j", t=4)[:, t])

        def quant_g(pair, slot):
            nc.vector.quantize_mx(out=gc[:, pair, slot].rearrange("p e m -> p (e m)").bitcast(E4M3X4),
                                  scales=gcs[:, pair, slot].rearrange("p e m -> p (e m)"), in_=gi[pair, slot][:])

        def g_codes(k, q):
            pair, e = divmod(k, 2)
            slot, part = (q, e) if pair == 0 or q < 2 else (2 + e, q - 2)
            return gc[:, pair, slot, part, :], gcs[:, pair, slot, part, :]

        def v_block(h, t, n):
            return vr[h][n // 4][:, n % 4, t:HALF:4]

        vt = {}
        grams = {}

        def turn_block(k, n):
            h, t = divmod(k, 4)
            if n == 0:
                vt[k] = bank(k % 4, [P, DI], BF16)
            nc.tensor.matmul(vt[k][:, P * n : P * (n + 1)], lhsT=v_block(h, t, n), rhs=ident[:], start=True, stop=True, is_transpose=k in TRANSPOSED)

        def turn_v(k):
            for n in range(8):
                turn_block(k, n)

        def gram(h):
            grams[h] = bank((6, 3)[h], [P, 4, P], F32)
            for n in range(8):
                for b in range(4):
                    block = vr[h][n // 4][:, n % 4, P * b : P * (b + 1)]
                    nc.tensor.matmul(grams[h][:, b, :], lhsT=block, rhs=block, start=(n == 0 and b == 0), stop=(n == 7 and b == 3))

        diag = {}
        n2 = {}

        def diagonals(h):
            diag[h] = kt([P, 4, P], F32, f"diag{h}")
            nc.vector.tensor_tensor(out=diag[h][:].rearrange("j t (b m) -> j t b m", b=4), in0=grams[h][:].rearrange("j b (m t) -> j t b m", t=4),
                                    in1=pick[:].unsqueeze(2).to_broadcast([P, 4, 4, 32]), op=ALU.mult)

        n2_raw = kt([P, 4], F32, "n2_raw")
        n2_late = kt([P, 4], F32, "n2_late")

        n2[1] = n2_late

        def diagonal_late(b):
            dump = wt([P, P], F32, "norm_dump", 4)
            nc.vector.scalar_tensor_tensor(out=dump[:], in0=grams[1][:, b, :], scalar=1.0, in1=ident[:], op0=ALU.mult, op1=ALU.mult, accum_out=n2_raw[:, b : b + 1])

        def move_norms():
            for b in range(4):
                nc.sync.dma_start(out=n2_late[32 * b : 32 * (b + 1), :], in_=n2_raw[:, b : b + 1])

        def norms(h):
            n2[h] = bank((6, 3)[h], [P, 4], F32)
            for t in range(4):
                nc.tensor.matmul(n2[h][:, t : t + 1], lhsT=diag[h][:, t, :], rhs=ones[:], start=True, stop=True)

        def root(h):
            nc.scalar.activation(rn[:, 4 * h : 4 * h + 4], n2[h][:], ACT.Abs_reciprocal_sqrt)

        def factors(h):
            four = slice(4 * h, 4 * h + 4)
            nc.vector.scalar_tensor_tensor(out=nbeta[:, four], in0=rn[:, four], scalar=-1.0, in1=mt[:, h, :], op0=ALU.mult, op1=ALU.mult)
            nc.scalar.activation(r2[:, four], rn[:, four], ACT.Square)

        banks = {}

        def mm1(k, passes, sides=(0, 1)):
            for q in passes:
                for s in sides:
                    if q == 0:
                        banks[k, s] = bank(4 + 2 * (k % 2) + s, [P, HALF], F32)
                    nc.tensor.matmul_mx(
                        banks[k, s][:],
                        lhsT=g_codes(k, q)[0].bitcast(E4M3X4), lhsT_scale=g_codes(k, q)[1],
                        rhs=xc[:, q, HALF * s : HALF * (s + 1)].bitcast(E4M3X4), rhs_scale=xcs[:, q, HALF * s : HALF * (s + 1)],
                        start=(q == 0), stop=(q == NQ - 1),
                    )

        gs = {}
        dv = [kt([P, 4, 4, QUART], BF16, f"dv{h}") for h in range(NG)]
        di = {}

        def evac(k, sides=(0, 1)):
            gs[k] = wt([P, DI], F32, "gs", 4)
            for s in sides:
                nc.scalar.activation(gs[k][:, HALF * s : HALF * (s + 1)].rearrange("p (n r) -> p n r", n=4), banks[k, s][:].rearrange("p (r n) -> p n r", n=4), ACT.Copy, scale=nbeta[:, k : k + 1])

        def fold(k):
            dump = wt([P, DI], F32, "xi", 2)
            nc.vector.scalar_tensor_tensor(out=dump[:], in0=gs[k][:], scalar=r2[:, k : k + 1], in1=vt[k][:], op0=ALU.mult, op1=ALU.mult, accum_out=gam[:, k : k + 1])

        def direction(k, chunks=slice(0, 4)):
            h, t = divmod(k, 4)
            nc.vector.scalar_tensor_tensor(
                out=dv[h][:, chunks, t, :], in0=vt[k][:].rearrange("p (c i) -> p c i", i=QUART)[:, chunks, :], scalar=gam[:, k : k + 1],
                in1=gs[k][:].rearrange("p (c i) -> p c i", i=QUART)[:, chunks, :], op0=ALU.mult, op1=ALU.subtract)

        def ileave_d(h, c, copy):
            di[h, c] = wt([P, DI], BF16, "gi", 4)
            copy(di[h, c][:].rearrange("p (c i t) -> p c t i", i=2, t=4), dv[h][:, c, :, :].rearrange("p t (c i) -> p c t i", i=2))

        def ileave_pair(c, u, copy, cols=slice(0, QUART)):
            if u == 0:
                di[1, c] = kt([P, DI], BF16, f"di{c}")
            copy(di[1, c][:].rearrange("p (c u e) -> p u c e", u=2, e=2)[:, u, cols], dv[1][:, c, 2 * u : 2 * u + 2, cols].rearrange("p e c -> p c e"))

        def relay_d(h, c):
            di[h, c] = relay[:, 0:DI]
            on_g(di[h, c].rearrange("p (c t) -> p c t", t=4), dv[h][:, c, :, :].rearrange("p t c -> p c t"))

        def quant_d(h, c):
            cols = slice(QUART * c, QUART * (c + 1))
            nc.vector.quantize_mx(out=dc[:, h, cols].bitcast(E4M3X4), scales=dcs[:, h, cols], in_=di[h, c][:])

        outs = {}

        def mm2(n, h, b=None):
            rows = slice(P * n, P * (n + 1))
            if h == 0:
                outs[n] = bank(b, [P, R], F32)
            nc.tensor.matmul_mx(outs[n][:], lhsT=dc[:, h, rows].bitcast(E4M3X4), lhsT_scale=dcs[:, h, rows],
                                rhs=ww[:, h, :].bitcast(E2M1X4), rhs_scale=ws[:, h, :], start=(h == 0), stop=(h == NG - 1))

        def finish(c):
            quant_d(1, c)
            mm2(2 * c, 1)
            mm2(2 * c + 1, 1)

        def store_block(n):
            res = kt([P, R], F32, f"res_block{n}")
            on_s(res[:], outs[n][:])
            nc.sync.dma_start(out=out4[n // 4][:, n % 4, :], in_=res[:])

        def store_chunk(c):
            res = kt([P, 2, R], F32, f"res_chunk{c}")
            on_s(res[:, 0, :], outs[2 * c][:])
            on_v(res[:, 1, :], outs[2 * c + 1][:])
            nc.sync.dma_start(out=out4[c // 2][:, 2 * (c % 2) : 2 * (c % 2) + 2, :], in_=res[:])

        planes(0)
        planes(1)
        widen_s(0, 0)
        widen_s(0, 3)
        widen_v(0, 1)
        widen_v(0, 2)
        widen_v(1, 0)
        widen_v(1, 1, slice(0, SHARE))
        widen_s(1, 1, slice(SHARE, DI))
        widen_s(1, 2)
        widen_s(1, 3)
        open_xi(0)
        ileave_x(0)
        planes(2)
        for j in range(4):
            widen_s(2, j)
        open_xi(1)
        ileave_x(1)
        quant_x(0)
        gram(0)
        turn_v(0)
        stage_g(0, 7)
        turn_v(1)
        stage_g(1, 5)
        quant_x(1)
        diagonals(0)
        norms(0)
        gram(1)
        turn_v(2)
        unstage_g(0)
        widen_side(3, 0)
        unstage_g(1)
        root(0)
        open_xi(2)
        ileave_x(2)
        widen_side(3, 1)
        quant_g(0, 0)
        quant_x(2)
        mm1(0, [0])
        mm1(1, [0])
        open_xi(3)
        ileave_x(3, 0, HALF)
        quant_g(0, 1)
        mm1(0, [1])
        mm1(1, [1])
        ileave_g(0, 2)
        ileave_x(3, 1, HALF)
        factors(0)
        ileave_g(0, 3)
        quant_g(0, 2)
        mm1(0, [2])
        quant_x(3, slice(0, HALF))
        quant_g(0, 3)
        quant_x(3, slice(HALF, DI))
        mm1(0, [3], (0,))
        mm1(1, [2], (0,))
        mm1(0, [3], (1,))
        mm1(1, [2], (1,))
        mm1(1, [3])
        ileave_g(1, 0, relay)
        diagonal_late(0)
        quant_g(1, 0)
        for b in range(1, 4):
            diagonal_late(b)
        move_norms()
        turn_v(3)
        evac(0)

        for k in range(NT):
            pair, q = divmod(k + 3, 2)
            if k < 6:
                relay_g(k + 2)
            else:
                relay_d(0, 2 * k - 11)
            if k < 5:
                ileave_g(pair, q)
                if k == 2:
                    root(1)
            elif k < 7:
                ileave_d(0, 2 * k - 10, on_s)
            if k == 7:
                ileave_pair(0, 0, on_s)
                evac(7)
                for c in range(1, 4):
                    ileave_pair(c, 0, on_s)
            elif k < 6:
                evac(k + 1)
            if k == 0:
                mm1(2, [0])
            else:
                direction(k - 1)
            fold(k)
            if k == 2:
                factors(1)
            if k < 5:
                quant_g(pair, q)
            elif k < 7:
                quant_d(0, 2 * k - 10)
            if k < 6:
                quant_g(k // 2 + 1, 2 + k % 2)
            else:
                quant_d(0, 2 * k - 11)
            if k in (0, 2, 4):
                mm1(k + 2, [1, 2, 3])
                if k == 4:
                    turn_v(6)
                mm1(k + 3, [0, 1])
            elif k in (1, 3):
                mm1(k + 2, [2, 3])
                if k == 3:
                    turn_v(5)
                mm1(k + 3, [0])
                if k == 1:
                    turn_v(4)
            elif k == 5:
                for s in range(2):
                    mm1(7, [2, 3], (s,))
                turn_v(7)
        for n, b in ((0, 2), (1, 0), (2, 1), (3, 4), (4, 7), (6, 5), (7, 6)):
            mm2(n, 0, b)
        direction(7, slice(0, 1))
        direction(7, slice(1, 2))
        ileave_pair(1, 1, on_s)
        ileave_pair(0, 1, on_v)
        direction(7, slice(2, 3))
        ileave_pair(2, 1, on_s, slice(0, P))
        finish(0)
        direction(7, slice(3, 4))
        mm2(5, 0, 3)
        store_block(0)
        store_block(1)
        finish(1)
        ileave_pair(2, 1, on_v, slice(P, QUART))
        ileave_pair(3, 1, on_v)
        finish(2)
        finish(3)
        store_block(2)
        store_block(3)
        store_chunk(2)
        store_chunk(3)
